import numpy as np
import ml_dtypes


def mxq(x, axis, fmt="e4m3"):
    dtype, down = {"e4m3": (ml_dtypes.float8_e4m3fn, 7), "e5m2": (ml_dtypes.float8_e5m2, 14)}[fmt]
    v = np.moveaxis(np.asarray(x, np.float32).astype(ml_dtypes.bfloat16).astype(np.float64), axis, -1)
    blocks = v.reshape(v.shape[:-1] + (-1, 32))
    amax = np.abs(blocks).max(-1, keepdims=True)
    byte = np.maximum(np.where(amax > 0, np.frexp(amax)[1] - 1 + 127, 0) - down, 1)
    scale = np.exp2(byte - 127.0)
    codes = (blocks / scale).astype(np.float32).astype(dtype).astype(np.float64)
    return np.moveaxis((codes * scale).reshape(v.shape), -1, axis)


WIDE = False


def mx_kscale(k):
    if not WIDE:
        return np.ones(k)
    levels = np.array([10, -10, 5, -5, 0])
    if k % 512:
        return np.exp2(np.random.permutation(np.resize(levels, k // 32))).repeat(32)
    a = np.empty((k // 512, 16))
    for p in range(k // 512):
        a[p, :8] = np.random.permutation(np.resize(levels, 8))
        for g in range(8):
            far = levels[np.abs(levels - a[p, g]) >= 10]
            a[p, g + 8] = far[np.random.randint(len(far))]
    return np.exp2(a.ravel()).repeat(32)


def f64(x):
    return np.asarray(x).astype(np.float64)


def striped(idx):
    return np.tile(idx.reshape(-1, 16).T, (8, 1)).astype(np.uint16)


def unstriped(offs):
    return offs[:16].T.reshape(-1).astype(np.int64)


E2M1 = np.array([0.0, 0.5, 1.0, 1.5, 2.0, 3.0, 4.0, 6.0, -0.0, -0.5, -1.0, -1.5, -2.0, -3.0, -4.0, -6.0])


def pack_weight(w, fmt):
    k, n = w.shape
    w = f64(np.asarray(w, np.float32).astype(ml_dtypes.bfloat16)).reshape(k // 32, 32, n)
    amax = np.abs(w).max(1)
    if fmt == "e4m3":
        byte = np.frexp(amax)[1] - 1 + 127 - 7
    else:
        mant, ex = np.frexp(amax / 6.0)
        byte = np.where(mant > 0.5, ex, ex - 1) + 127
    byte = np.clip(np.where(amax > 0, byte, 1), 1, 254)
    scaled = (w * np.exp2(127.0 - byte)[:, None, :]).reshape(k, n).astype(np.float32)
    by_word = np.ascontiguousarray(scaled.reshape(k // 512, 128, 4, n).transpose(0, 1, 3, 2))
    if fmt == "e4m3":
        words = by_word.astype(ml_dtypes.float8_e4m3fn).view(np.uint8)
    else:
        c = by_word.astype(ml_dtypes.float4_e2m1fn).view(np.uint8) & 0xF
        words = (c[..., 0::2] | (c[..., 1::2] << 4)).reshape(k // 512, 128, 2 * n)
    return np.ascontiguousarray(words), np.ascontiguousarray(byte.astype(np.uint8).reshape(k // 512, 16, n))


def unpack_weight(words, scales, fmt):
    g, _, n = scales.shape
    words = np.ascontiguousarray(words).reshape(g, 128, n, -1)
    if fmt == "e4m3":
        vals = words.view(ml_dtypes.float8_e4m3fn).astype(np.float64)
    else:
        nib = np.empty((g, 128, n, 4), np.uint8)
        nib[..., 0::2] = words & 0xF
        nib[..., 1::2] = words >> 4
        vals = E2M1[nib]
    vals = vals * np.repeat(np.exp2(scales.astype(np.float64) - 127.0), 8, axis=1)[..., None]
    return vals.transpose(0, 1, 3, 2).reshape(g * 512, n)


def gelu(v):
    return 0.5 * v * (1.0 + np.tanh(np.sqrt(2.0 / np.pi) * (v + 0.044715 * v**3)))


K, H, N, T, S, T2, P = 1536, 1024, 768, 4096, 1024, 2048, 512


def setup_inputs():
    n = np.random.standard_normal
    s = mx_kscale(K)[:, None]
    u = mx_kscale(H)[:, None]
    tab_words, tab_scales = pack_weight(n((K, T)) * s, "e4m3")
    wa_words, wa_scales = pack_weight(n((H, N)) / np.sqrt(H) / u, "e2m1")
    return {
        "tab_words": tab_words,
        "tab_scales": tab_scales,
        "offs": striped(np.random.permutation(T)[:S]),
        "w1": (n((K, H)) / np.sqrt(K) / s).astype(np.float32),
        "gain": (1.5 * np.exp(0.3 * n(H)) * u[:, 0]).astype(np.float32),
        "wgs": np.exp(0.3 * n((128, S))).astype(np.float32),
        "offs2": striped(np.random.permutation(T2)[:S]),
        "offs3": striped(np.random.permutation(T2)[:P]),
        "sess": (n((H, P)) * u).astype(np.float32),
        "wa_words": wa_words,
        "wa_scales": wa_scales,
        "wb": (n((H, N)) / np.sqrt(H) / u).astype(np.float32),
    }


def reference(tab_words, tab_scales, offs, w1, gain, wgs, offs2, offs3, sess, wa_words, wa_scales, wb):
    v = unpack_weight(tab_words, tab_scales, "e4m3")[:, unstriped(offs)]
    a = mxq(f64(w1), 0, "e4m3").T @ v
    gelu = 0.5 * a * (1.0 + np.tanh(0.7978845608028654 * (a + 0.044715 * a ** 3)))
    h = f64(gain)[:, None] * gelu
    page = np.zeros((H, T2))
    page[:, unstriped(offs2)] = np.tile(f64(wgs), (H // 128, 1)) * h
    x = page[:, unstriped(offs3)]
    z = x + f64(sess)
    zq = mxq(z, 0, "e4m3")
    wa = unpack_weight(wa_words, wa_scales, "e2m1")
    ya = wa.T @ zq
    yb = mxq(f64(wb), 0, "e4m3").T @ zq
    return np.maximum(ya, yb)

@@ -1,0 +1,301 @@
+from contextlib import ExitStack
+
+import concourse.mybir as mybir
+from concourse.masks import make_identity
+
+K, H, N, T, S, T2, M = 1536, 1024, 768, 4096, 1024, 2048, 512
+FLOPS = 2 * K * H * S + 2 * 2 * H * N * M
+
+F32 = mybir.dt.float32
+BF16 = mybir.dt.bfloat16
+I32 = mybir.dt.int32
+U32 = mybir.dt.uint32
+U16 = mybir.dt.uint16
+U8 = mybir.dt.uint8
+FP8X4 = mybir.dt.float8_e4m3fn_x4
+FP4X4 = mybir.dt.float4_e2m1fn_x4
+ACT = mybir.ActivationFunctionType
+ALU = mybir.AluOpType
+
+P = 128
+PACK = 4
+K_PASS = P * PACK
+BANK = 512
+K_PASSES = K // K_PASS
+R_PASSES = H // K_PASS
+R_TILES = H // P
+N_TILES = N // P
+TILES_PER_PASS = K_PASS // P
+M_HALF = M // 2
+LIST_ROWS = 16
+ALIGN = 64
+
+
+def interleave(nc, grouped, raw):
+    nc.scalar.copy(
+        out=grouped.rearrange("p (c j i) -> p c i j", j=4, i=PACK),
+        in_=raw.rearrange("p i (c j) -> p c i j", j=4),
+    )
+
+
+def tile_list_session_slot_verdict_kernel(
+    tc, tab_words, tab_scales, offs, w1, gain, wgs, offs2, offs3, sess, wa_words, wa_scales, wb, out
+):
+    nc = tc.nc
+    with ExitStack() as ctx:
+        keep = ctx.enter_context(tc.tile_pool(name="keep", bufs=1))
+        ring = ctx.enter_context(tc.tile_pool(name="ring", bufs=2))
+        psum = ctx.enter_context(tc.psum_pool(name="psum", bufs=1))
+
+        def bank(tag, shape):
+            return psum.tile(shape, F32, name=tag, tag=tag)
+
+        table_scales = keep.tile([P, T], U8, align_bytes=ALIGN)
+        nc.vector.memset(table_scales[:].bitcast(I32), 0)
+        page = keep.tile([P, T2], F32)
+        nc.vector.memset(page[:], 0.0)
+        wa_scale_sb = keep.tile([P, R_PASSES, N], U8, align_bytes=ALIGN)
+        nc.vector.memset(wa_scale_sb[:].rearrange("p a n -> p (a n)").bitcast(I32), 0)
+        gain_rows = keep.tile([P, P], F32)
+        nc.gpsimd.memset(gain_rows[:], 0.0)
+        ident = keep.tile([P, P], F32)
+        make_identity(nc, ident[:])
+        warm = keep.tile([P, 1], F32)
+        nc.scalar.activation(out=warm[:], in_=ident[:, 0:1], func=ACT.Gelu_apprx_tanh)
+
+        def load_table(a):
+            words = keep.tile([P, T], U32, name=f"table_words{a}")
+            nc.sync.dma_start(out=words[:].bitcast(I32), in_=tab_words[a].rearrange("p t i -> p (t i)").bitcast(I32))
+            return words
+
+        def load_w1(c, a):
+            raw = keep.tile([P, PACK, P], F32, name=f"w1_raw{c}_{a}", tag=f"w1_raw{a}", bufs=5)
+            rows = w1[a * K_PASS : (a + 1) * K_PASS, c * P : (c + 1) * P]
+            nc.sync.dma_start(out=raw[:], in_=rows.rearrange("(p i) c -> p i c", i=PACK))
+            return raw
+
+        def load_sess(c):
+            rows = keep.tile([P, M], F32, name=f"sess{c}")
+            nc.sync.dma_start(out=rows[:], in_=sess[c * P : (c + 1) * P, :])
+            return rows
+
+        list1 = keep.tile([P, S // LIST_ROWS], U16)
+        nc.sync.dma_start(list1[:], offs)
+        table_words = [load_table(0)]
+        for q in range(4):
+            nc.scalar.dma_start(
+                out=table_scales[32 * q : 32 * q + 4 * K_PASSES, :].bitcast(I32),
+                in_=tab_scales[:, 4 * q : 4 * q + 4, :].bitcast(I32),
+            )
+        nc.scalar.dma_start(out=gain_rows[0:R_TILES, :], in_=gain.rearrange("(c p) -> c p", p=P))
+        w1_raw = [[load_w1(0, a) for a in range(K_PASSES)]]
+        table_words.append(load_table(1))
+        table_words.append(load_table(2))
+        wgs_sb = keep.tile([P, S], F32)
+        nc.sync.dma_start(out=wgs_sb[:, 0:BANK], in_=wgs[:, 0:BANK])
+        list2 = keep.tile([P, S // LIST_ROWS], U16)
+        nc.sync.dma_start(list2[:], offs2)
+        w1_raw.append([load_w1(1, a) for a in range(K_PASSES)])
+        nc.sync.dma_start(out=wgs_sb[:, BANK:S], in_=wgs[:, BANK:S])
+        list3 = keep.tile([P, M // LIST_ROWS], U16)
+        nc.sync.dma_start(list3[:], offs3)
+        sess_sb = []
+        for c in range(2, R_TILES):
+            w1_raw.append([load_w1(c, a) for a in range(K_PASSES)])
+            sess_sb.append(load_sess(c - 2))
+        for c in range(R_TILES - 2, R_TILES):
+            sess_sb.append(load_sess(c))
+        wb_raw = []
+        for a in range(R_PASSES):
+            raw = keep.tile([P, PACK, N], F32, name=f"wb_raw{a}")
+            nc.sync.dma_start(out=raw[:], in_=wb[a * K_PASS : (a + 1) * K_PASS, :].rearrange("(p i) n -> p i n", i=PACK))
+            wb_raw.append(raw)
+        wa_codes = keep.tile([P, R_PASSES, 2 * N], U8, align_bytes=ALIGN)
+        nc.sync.dma_start(out=wa_codes[:].bitcast(I32), in_=wa_words.rearrange("a p n -> p a n").bitcast(I32))
+        for q in range(4):
+            nc.sync.dma_start(
+                out=wa_scale_sb[32 * q : 32 * q + 4, :, :].bitcast(I32),
+                in_=wa_scales[:, 4 * q : 4 * q + 4, :].rearrange("a r n -> r a n").bitcast(I32),
+            )
+
+        gain_ps = bank("words0", [P, P])
+        nc.tensor.transpose(gain_ps[:], gain_rows[:], ident[:])
+        gain_col = keep.tile([P, R_TILES], F32)
+        nc.scalar.copy(out=gain_col[:], in_=gain_ps[:, 0:R_TILES])
+
+        half_cols = BANK // LIST_ROWS
+        v_words = [keep.tile([P, S], U32, name=f"v_words{a}", align_bytes=ALIGN) for a in range(K_PASSES)]
+        v_scales = keep.tile([P, S], U8, align_bytes=ALIGN)
+        nc.vector.tensor_copy(v_words[0][:], table_words[0][:].indirect(list1[:]))
+        nc.vector.tensor_copy(v_scales[:], table_scales[:].indirect(list1[:]))
+        nc.vector.tensor_copy(v_words[1][:], table_words[1][:].indirect(list1[:]))
+
+        w1_codes = {}
+        w1_scales = {}
+
+        def quantize_w1(c, tag):
+            w1_codes[c] = keep.tile([P, K_PASSES * P], U32, name=f"w1_codes{c}", tag="w1_codes", bufs=3, align_bytes=ALIGN)
+            w1_scales[c] = keep.tile([P, K_PASSES * P], U8, name=f"w1_scales{c}", tag="w1_scales", bufs=3, align_bytes=ALIGN)
+            grouped = keep.tile([P, K_PASSES * K_PASS], BF16, name=f"w1_grouped{c}", tag=tag, align_bytes=ALIGN)
+            for a in range(K_PASSES):
+                interleave(nc, grouped[:, a * K_PASS : (a + 1) * K_PASS], w1_raw[c][a][:])
+            for lo, hi in ((0, 2 * P), (2 * P, 3 * P)):
+                nc.vector.quantize_mx(
+                    out=w1_codes[c][:, lo:hi].bitcast(FP8X4),
+                    scales=w1_scales[c][:, lo:hi],
+                    in_=grouped[:, PACK * lo : PACK * hi],
+                )
+
+        def features(c):
+            h = ring.tile([P, S], F32, name=f"h{c}", tag="h")
+            for half in range(2):
+                cols = slice(half * BANK, (half + 1) * BANK)
+                acc = bank(f"feat{half}", [P, BANK])
+                for a in range(K_PASSES):
+                    nc.tensor.matmul_mx(
+                        out=acc[:],
+                        lhsT=w1_codes[c][:, a * P : (a + 1) * P].bitcast(FP8X4),
+                        lhsT_scale=w1_scales[c][:, a * P : (a + 1) * P],
+                        rhs=v_words[a][:, cols].bitcast(FP8X4),
+                        rhs_scale=v_scales[4 * a : P, cols],
+                        start=(a == 0),
+                        stop=(a == K_PASSES - 1),
+                    )
+                nc.scalar.activation(out=h[:, cols], in_=acc[:], func=ACT.Gelu_apprx_tanh)
+            return h
+
+        def weights(c, tile, cols):
+            nc.scalar.activation(out=tile[:], in_=wgs_sb[:, cols], func=ACT.Copy, scale=gain_col[:, c : c + 1])
+
+        zt_pairs = [
+            [keep.tile([P, 2, 2, P, 2], BF16, name=f"zt_pairs{a}_{half}") for half in range(2)] for a in range(R_PASSES)
+        ]
+        z_codes = keep.tile([P, R_PASSES, M], U32, align_bytes=ALIGN)
+        z_scales = keep.tile([P, R_PASSES, M], U8, align_bytes=ALIGN)
+
+        def turn_and_round(c, x, half):
+            a, sub = divmod(c, TILES_PER_PASS)
+            zt = bank(f"sum{half}", [P, 2, P])
+            for step, src in enumerate((sess_sb[c], x)):
+                for t in range(2):
+                    m0 = half * M_HALF + t * P
+                    nc.tensor.matmul(
+                        zt[:, t, :],
+                        src[:, m0 : m0 + P],
+                        ident[:],
+                        start=(step == 0 and t == 0),
+                        stop=(step == 1 and t == 1),
+                        is_transpose=True,
+                    )
+            nc.scalar.copy(
+                out=zt_pairs[a][half][:, :, :, 32 * sub : 32 * sub + 32, :],
+                in_=zt[:].rearrange("p t (q u e) -> p t u q e", u=2, e=2),
+            )
+
+        def quantize_z(a, half, engine_copy):
+            words = zt_pairs[a][half][:].rearrange("p t u q e -> p (t u q e)").bitcast(F32)
+            turned = bank(f"words{half}", [P, 4, P])
+            for j in range(4):
+                nc.tensor.transpose(turned[:, j, :], words[:, j * P : (j + 1) * P], ident[:])
+            grouped = keep.tile([P, PACK * M_HALF], BF16, name=f"z_grouped{a}_{half}", tag=f"z_grouped{half}", align_bytes=ALIGN)
+            engine_copy(
+                out=grouped[:].bitcast(F32).rearrange("p (t m u) -> p t m u", t=2, u=2),
+                in_=turned[:].rearrange("p (t u) m -> p t m u", u=2),
+            )
+            cols = slice(half * M_HALF, (half + 1) * M_HALF)
+            nc.vector.quantize_mx(out=z_codes[:, a, cols].bitcast(FP8X4), scales=z_scales[:, a, cols], in_=grouped[:])
+
+        wb_codes = keep.tile([P, R_PASSES, N], U32, align_bytes=ALIGN)
+        wb_scales = keep.tile([P, R_PASSES, N], U8, align_bytes=ALIGN)
+
+        def quantize_wb(a):
+            for lo, hi in ((0, BANK), (BANK, N)):
+                grouped = keep.tile([P, PACK * (hi - lo)], BF16, name=f"wb_grouped{a}_{lo}", tag=f"wb_grouped{lo}", align_bytes=ALIGN)
+                interleave(nc, grouped[:], wb_raw[a][:, :, lo:hi])
+                nc.vector.quantize_mx(
+                    out=wb_codes[:, a, lo:hi].bitcast(FP8X4), scales=wb_scales[:, a, lo:hi], in_=grouped[:]
+                )
+
+        def score_pass(acc, rule_set, n, a):
+            if rule_set == 0:
+                codes = wa_codes[:, a, 2 * n * P : 2 * (n + 1) * P].bitcast(FP4X4)
+                scales = wa_scale_sb[:, a, n * P : (n + 1) * P]
+            else:
+                codes = wb_codes[:, a, n * P : (n + 1) * P].bitcast(FP8X4)
+                scales = wb_scales[:, a, n * P : (n + 1) * P]
+            nc.tensor.matmul_mx(
+                out=acc[:],
+                lhsT=codes,
+                lhsT_scale=scales,
+                rhs=z_codes[:, a, :].bitcast(FP8X4),
+                rhs_scale=z_scales[:, a, :],
+                start=(a == 0),
+                stop=(a == R_PASSES - 1),
+            )
+
+        quantize_w1(0, "head")
+        for half in range(2):
+            nc.vector.tensor_copy(
+                v_words[2][:, half * BANK : (half + 1) * BANK],
+                table_words[2][:].indirect(list1[:, half * half_cols : (half + 1) * half_cols]),
+            )
+        h = features(0)
+        first = ring.tile([P, BANK], F32, name="wg0a", tag="wg")
+        weights(0, first, slice(0, BANK))
+        nc.vector.tensor_tensor(page[:].indirect(list2[:, 0:half_cols]), h[:, 0:BANK], first[:], ALU.mult)
+        quantize_w1(1, "head")
+        second = keep.tile([P, BANK], F32, name="wg0b", tag="head", align_bytes=ALIGN)
+        weights(0, second, slice(BANK, S))
+        nc.vector.tensor_tensor(page[:].indirect(list2[:, half_cols : 2 * half_cols]), h[:, BANK:S], second[:], ALU.mult)
+
+        accs = {}
+        for c in range(R_TILES):
+            if c > 0:
+                nc.vector.tensor_tensor(page[:].indirect(list2[:]), h[:], wg[:], ALU.mult)
+            if c + 1 < R_TILES:
+                h = features(c + 1)
+                wg = ring.tile([P, S], F32, name=f"wg{c + 1}", tag="wg")
+                weights(c + 1, wg, slice(0, S))
+            if c + 2 < R_TILES:
+                quantize_w1(c + 2, "stage")
+            if c in (3, 5):
+                quantize_wb(0 if c == 3 else 1)
+            x = keep.tile([P, M], F32, name=f"x{c}", tag="stage", align_bytes=ALIGN)
+            if c + 1 < R_TILES:
+                nc.vector.tensor_copy(x[:], page[:].indirect(list3[:]))
+                for half in range(2):
+                    turn_and_round(c, x, half)
+            else:
+                for half in range(2):
+                    lo, hi = half * M_HALF, (half + 1) * M_HALF
+                    nc.vector.tensor_copy(x[:, lo:hi], page[:].indirect(list3[:, lo // LIST_ROWS : hi // LIST_ROWS]))
+                for half in range(2):
+                    turn_and_round(c, x, half)
+            if c == TILES_PER_PASS - 1:
+                for half in range(2):
+                    quantize_z(0, half, nc.scalar.copy)
+            if c == R_TILES - 2:
+                for n, tags in enumerate((("score0", "score1"), ("feat0", "feat1"))):
+                    for rule_set in range(2):
+                        accs[n, rule_set] = bank(tags[rule_set], [P, M])
+                        score_pass(accs[n, rule_set], rule_set, n, 0)
+
+        quantize_z(1, 0, nc.scalar.copy)
+        quantize_z(1, 1, nc.vector.tensor_copy)
+        for n, tags in ((2, ("sum0", "sum1")), (3, ("words0", "words1"))):
+            for rule_set in range(2):
+                accs[n, rule_set] = bank(tags[rule_set], [P, M])
+                score_pass(accs[n, rule_set], rule_set, n, 0)
+
+        late_tags = (("score0", "score1"), ("feat0", "feat1"))
+        for n in range(N_TILES):
+            for rule_set in range(2):
+                if n >= 4:
+                    accs[n, rule_set] = bank(late_tags[n - 4][rule_set], [P, M])
+                    score_pass(accs[n, rule_set], rule_set, n, 0)
+                score_pass(accs[n, rule_set], rule_set, n, 1)
+            ya = ring.tile([P, M], F32, name=f"ya{n}", tag="ya", bufs=3)
+            nc.scalar.copy(out=ya[:], in_=accs[n, 0][:])
+            best = keep.tile([P, M], F32, name=f"best{n}", tag="best", bufs=6)
+            nc.vector.tensor_tensor(best[:], accs[n, 1][:], ya[:], ALU.max)
+            nc.sync.dma_start(out=out[n * P : (n + 1) * P, :], in_=best[:])

@@ -51,13 +51,19 @@ def tile_list_session_slot_verdict_kernel(
             return psum.tile(shape, F32, name=tag, tag=tag)
 
         table_scales = keep.tile([P, T], U8, align_bytes=ALIGN)
-        nc.vector.memset(table_scales[:].bitcast(I32), 0)
+        nc.gpsimd.memset(table_scales[:].bitcast(I32), 0)
+        for q in range(4):
+            nc.gpsimd.dma_start(
+                out=table_scales[32 * q : 32 * q + 4 * K_PASSES, :].bitcast(I32),
+                in_=tab_scales[:, 4 * q : 4 * q + 4, :].bitcast(I32),
+            )
         page = keep.tile([P, T2], F32)
         nc.vector.memset(page[:], 0.0)
         wa_scale_sb = keep.tile([P, R_PASSES, N], U8, align_bytes=ALIGN)
         nc.vector.memset(wa_scale_sb[:].rearrange("p a n -> p (a n)").bitcast(I32), 0)
         gain_rows = keep.tile([P, P], F32)
         nc.gpsimd.memset(gain_rows[:], 0.0)
+        nc.gpsimd.dma_start(out=gain_rows[0:R_TILES, :], in_=gain.rearrange("(c p) -> c p", p=P))
         ident = keep.tile([P, P], F32)
         make_identity(nc, ident[:])
         warm = keep.tile([P, 1], F32)
@@ -69,28 +75,23 @@ def tile_list_session_slot_verdict_kernel(
             return words
 
         def load_w1(c, a):
-            raw = keep.tile([P, PACK, P], F32, name=f"w1_raw{c}_{a}", tag=f"w1_raw{a}", bufs=5)
+            if a == K_PASSES - 1:
+                raw = keep.tile([P, PACK, P], F32, name=f"w1_raw{c}_{a}", tag=f"w1_last{c}")
+            else:
+                raw = keep.tile([P, PACK, P], F32, name=f"w1_raw{c}_{a}", tag=f"w1_raw{a}", bufs=5)
             rows = w1[a * K_PASS : (a + 1) * K_PASS, c * P : (c + 1) * P]
             nc.sync.dma_start(out=raw[:], in_=rows.rearrange("(p i) c -> p i c", i=PACK))
             return raw
 
         def load_sess(c):
-            rows = keep.tile([P, M], F32, name=f"sess{c}")
+            rows = keep.tile([P, M], F32, name=f"sess{c}", tag=f"sess{c}")
             nc.sync.dma_start(out=rows[:], in_=sess[c * P : (c + 1) * P, :])
             return rows
 
         list1 = keep.tile([P, S // LIST_ROWS], U16)
         nc.sync.dma_start(list1[:], offs)
-        table_words = [load_table(0)]
-        for q in range(4):
-            nc.scalar.dma_start(
-                out=table_scales[32 * q : 32 * q + 4 * K_PASSES, :].bitcast(I32),
-                in_=tab_scales[:, 4 * q : 4 * q + 4, :].bitcast(I32),
-            )
-        nc.scalar.dma_start(out=gain_rows[0:R_TILES, :], in_=gain.rearrange("(c p) -> c p", p=P))
+        table_words = [load_table(a) for a in range(K_PASSES)]
         w1_raw = [[load_w1(0, a) for a in range(K_PASSES)]]
-        table_words.append(load_table(1))
-        table_words.append(load_table(2))
         wgs_sb = keep.tile([P, S], F32)
         nc.sync.dma_start(out=wgs_sb[:, 0:BANK], in_=wgs[:, 0:BANK])
         list2 = keep.tile([P, S // LIST_ROWS], U16)
@@ -123,28 +124,31 @@ def tile_list_session_slot_verdict_kernel(
         gain_col = keep.tile([P, R_TILES], F32)
         nc.scalar.copy(out=gain_col[:], in_=gain_ps[:, 0:R_TILES])
 
-        half_cols = BANK // LIST_ROWS
         v_words = [keep.tile([P, S], U32, name=f"v_words{a}", align_bytes=ALIGN) for a in range(K_PASSES)]
         v_scales = keep.tile([P, S], U8, align_bytes=ALIGN)
-        nc.vector.tensor_copy(v_words[0][:], table_words[0][:].indirect(list1[:]))
         nc.vector.tensor_copy(v_scales[:], table_scales[:].indirect(list1[:]))
-        nc.vector.tensor_copy(v_words[1][:], table_words[1][:].indirect(list1[:]))
+        for a in range(K_PASSES):
+            nc.vector.tensor_copy(v_words[a][:], table_words[a][:].indirect(list1[:]))
 
         w1_codes = {}
         w1_scales = {}
 
-        def quantize_w1(c, tag):
+        w1_grouped = {}
+
+        def group_w1(c):
+            w1_grouped[c] = keep.tile([P, K_PASSES * K_PASS], BF16, name=f"w1_grouped{c}", tag="w1_grouped", align_bytes=ALIGN)
+            for a in range(K_PASSES):
+                interleave(nc, w1_grouped[c][:, a * K_PASS : (a + 1) * K_PASS], w1_raw[c][a][:])
             w1_codes[c] = keep.tile([P, K_PASSES * P], U32, name=f"w1_codes{c}", tag="w1_codes", bufs=3, align_bytes=ALIGN)
             w1_scales[c] = keep.tile([P, K_PASSES * P], U8, name=f"w1_scales{c}", tag="w1_scales", bufs=3, align_bytes=ALIGN)
-            grouped = keep.tile([P, K_PASSES * K_PASS], BF16, name=f"w1_grouped{c}", tag=tag, align_bytes=ALIGN)
-            for a in range(K_PASSES):
-                interleave(nc, grouped[:, a * K_PASS : (a + 1) * K_PASS], w1_raw[c][a][:])
-            for lo, hi in ((0, 2 * P), (2 * P, 3 * P)):
-                nc.vector.quantize_mx(
-                    out=w1_codes[c][:, lo:hi].bitcast(FP8X4),
-                    scales=w1_scales[c][:, lo:hi],
-                    in_=grouped[:, PACK * lo : PACK * hi],
-                )
+
+        def quantize_w1(c, first_pass, end_pass):
+            lo, hi = first_pass * P, end_pass * P
+            nc.vector.quantize_mx(
+                out=w1_codes[c][:, lo:hi].bitcast(FP8X4),
+                scales=w1_scales[c][:, lo:hi],
+                in_=w1_grouped[c][:, PACK * lo : PACK * hi],
+            )
 
         def features(c):
             h = ring.tile([P, S], F32, name=f"h{c}", tag="h")
@@ -167,14 +171,15 @@ def tile_list_session_slot_verdict_kernel(
         def weights(c, tile, cols):
             nc.scalar.activation(out=tile[:], in_=wgs_sb[:, cols], func=ACT.Copy, scale=gain_col[:, c : c + 1])
 
-        zt_pairs = [
-            [keep.tile([P, 2, 2, P, 2], BF16, name=f"zt_pairs{a}_{half}") for half in range(2)] for a in range(R_PASSES)
-        ]
-        z_codes = keep.tile([P, R_PASSES, M], U32, align_bytes=ALIGN)
+        zt_pairs = {}
+        z_grouped = {}
+        z_codes = {}
         z_scales = keep.tile([P, R_PASSES, M], U8, align_bytes=ALIGN)
 
         def turn_and_round(c, x, half):
             a, sub = divmod(c, TILES_PER_PASS)
+            if sub == 0:
+                zt_pairs[a, half] = keep.tile([P, 2, 2, P, 2], BF16, name=f"zt_pairs{a}_{half}", tag=f"zt_pairs{half}")
             zt = bank(f"sum{half}", [P, 2, P])
             for step, src in enumerate((sess_sb[c], x)):
                 for t in range(2):
@@ -188,33 +193,34 @@ def tile_list_session_slot_verdict_kernel(
                         is_transpose=True,
                     )
             nc.scalar.copy(
-                out=zt_pairs[a][half][:, :, :, 32 * sub : 32 * sub + 32, :],
+                out=zt_pairs[a, half][:, :, :, 32 * sub : 32 * sub + 32, :],
                 in_=zt[:].rearrange("p t (q u e) -> p t u q e", u=2, e=2),
             )
 
-        def quantize_z(a, half, engine_copy):
-            words = zt_pairs[a][half][:].rearrange("p t u q e -> p (t u q e)").bitcast(F32)
+        def group_z(a, half):
+            words = zt_pairs[a, half][:].rearrange("p t u q e -> p (t u q e)").bitcast(F32)
             turned = bank(f"words{half}", [P, 4, P])
             for j in range(4):
                 nc.tensor.transpose(turned[:, j, :], words[:, j * P : (j + 1) * P], ident[:])
-            grouped = keep.tile([P, PACK * M_HALF], BF16, name=f"z_grouped{a}_{half}", tag=f"z_grouped{half}", align_bytes=ALIGN)
-            engine_copy(
-                out=grouped[:].bitcast(F32).rearrange("p (t m u) -> p t m u", t=2, u=2),
+            z_grouped[a, half] = keep.tile([P, PACK * M_HALF], BF16, name=f"z_grouped{a}_{half}", align_bytes=ALIGN)
+            nc.scalar.copy(
+                out=z_grouped[a, half][:].bitcast(F32).rearrange("p (t m u) -> p t m u", t=2, u=2),
                 in_=turned[:].rearrange("p (t u) m -> p t m u", u=2),
             )
-            cols = slice(half * M_HALF, (half + 1) * M_HALF)
-            nc.vector.quantize_mx(out=z_codes[:, a, cols].bitcast(FP8X4), scales=z_scales[:, a, cols], in_=grouped[:])
 
-        wb_codes = keep.tile([P, R_PASSES, N], U32, align_bytes=ALIGN)
+        def quantize_z(a, half):
+            cols = slice(half * M_HALF, (half + 1) * M_HALF)
+            nc.vector.quantize_mx(
+                out=z_codes[a][:, cols].bitcast(FP8X4), scales=z_scales[:, a, cols], in_=z_grouped[a, half][:]
+            )
+
+        wb_pieces = [(a, lo, hi) for a in range(R_PASSES) for lo, hi in ((0, BANK), (BANK, N))]
+        wb_grouped = {}
         wb_scales = keep.tile([P, R_PASSES, N], U8, align_bytes=ALIGN)
 
-        def quantize_wb(a):
-            for lo, hi in ((0, BANK), (BANK, N)):
-                grouped = keep.tile([P, PACK * (hi - lo)], BF16, name=f"wb_grouped{a}_{lo}", tag=f"wb_grouped{lo}", align_bytes=ALIGN)
-                interleave(nc, grouped[:], wb_raw[a][:, :, lo:hi])
-                nc.vector.quantize_mx(
-                    out=wb_codes[:, a, lo:hi].bitcast(FP8X4), scales=wb_scales[:, a, lo:hi], in_=grouped[:]
-                )
+        def group_wb(a, lo, hi):
+            wb_grouped[a, lo] = keep.tile([P, PACK * (hi - lo)], BF16, name=f"wb_grouped{a}_{lo}", align_bytes=ALIGN)
+            interleave(nc, wb_grouped[a, lo][:], wb_raw[a][:, :, lo:hi])
 
         def score_pass(acc, rule_set, n, a):
             if rule_set == 0:
@@ -227,75 +233,95 @@ def tile_list_session_slot_verdict_kernel(
                 out=acc[:],
                 lhsT=codes,
                 lhsT_scale=scales,
-                rhs=z_codes[:, a, :].bitcast(FP8X4),
+                rhs=z_codes[a][:].bitcast(FP8X4),
                 rhs_scale=z_scales[:, a, :],
                 start=(a == 0),
                 stop=(a == R_PASSES - 1),
             )
 
-        quantize_w1(0, "head")
-        for half in range(2):
-            nc.vector.tensor_copy(
-                v_words[2][:, half * BANK : (half + 1) * BANK],
-                table_words[2][:].indirect(list1[:, half * half_cols : (half + 1) * half_cols]),
-            )
-        h = features(0)
-        first = ring.tile([P, BANK], F32, name="wg0a", tag="wg")
-        weights(0, first, slice(0, BANK))
-        nc.vector.tensor_tensor(page[:].indirect(list2[:, 0:half_cols]), h[:, 0:BANK], first[:], ALU.mult)
-        quantize_w1(1, "head")
-        second = keep.tile([P, BANK], F32, name="wg0b", tag="head", align_bytes=ALIGN)
-        weights(0, second, slice(BANK, S))
-        nc.vector.tensor_tensor(page[:].indirect(list2[:, half_cols : 2 * half_cols]), h[:, BANK:S], second[:], ALU.mult)
+        def scatter(h, wg, lo, hi):
+            nc.vector.tensor_tensor(page[:].indirect(list2[:, lo // LIST_ROWS : hi // LIST_ROWS]), h[:, lo:hi], wg[:], ALU.mult)
 
-        accs = {}
-        for c in range(R_TILES):
+        def gather(x, lo, hi):
+            nc.vector.tensor_copy(x[:, lo:hi], page[:].indirect(list3[:, lo // LIST_ROWS : hi // LIST_ROWS]))
+
+        last = R_TILES - 1
+        group_w1(0)
+        for a in range(K_PASSES):
+            quantize_w1(0, a, a + 1)
+        h = features(0)
+        wg = ring.tile([P, BANK], F32, name="wg0a", tag="wg")
+        weights(0, wg, slice(0, BANK))
+        scatter(h, wg, 0, BANK)
+        group_w1(1)
+        quantize_w1(1, 0, 2)
+        quantize_w1(1, 2, 3)
+        wg = keep.tile([P, BANK], F32, name="wg0b", tag="w1_last1")
+        weights(0, wg, slice(BANK, S))
+        scatter(h, wg, BANK, S)
+
+        for c in range(last):
             if c > 0:
-                nc.vector.tensor_tensor(page[:].indirect(list2[:]), h[:], wg[:], ALU.mult)
-            if c + 1 < R_TILES:
-                h = features(c + 1)
+                scatter(h, wg, 0, S)
+            h = features(c + 1)
+            if c + 1 < last:
                 wg = ring.tile([P, S], F32, name=f"wg{c + 1}", tag="wg")
                 weights(c + 1, wg, slice(0, S))
-            if c + 2 < R_TILES:
-                quantize_w1(c + 2, "stage")
-            if c in (3, 5):
-                quantize_wb(0 if c == 3 else 1)
-            x = keep.tile([P, M], F32, name=f"x{c}", tag="stage", align_bytes=ALIGN)
-            if c + 1 < R_TILES:
-                nc.vector.tensor_copy(x[:], page[:].indirect(list3[:]))
-                for half in range(2):
-                    turn_and_round(c, x, half)
-            else:
-                for half in range(2):
-                    lo, hi = half * M_HALF, (half + 1) * M_HALF
-                    nc.vector.tensor_copy(x[:, lo:hi], page[:].indirect(list3[:, lo // LIST_ROWS : hi // LIST_ROWS]))
-                for half in range(2):
-                    turn_and_round(c, x, half)
+            if c + 2 <= last:
+                group_w1(c + 2)
+                quantize_w1(c + 2, 0, 2)
+            x = keep.tile([P, M], F32, name=f"x{c}", tag=f"w1_last{(c + 2) % R_TILES}")
+            gather(x, 0, M)
+            if c + 2 <= last:
+                quantize_w1(c + 2, 2, 3)
+            for half in range(2):
+                turn_and_round(c, x, half)
             if c == TILES_PER_PASS - 1:
                 for half in range(2):
-                    quantize_z(0, half, nc.scalar.copy)
-            if c == R_TILES - 2:
-                for n, tags in enumerate((("score0", "score1"), ("feat0", "feat1"))):
-                    for rule_set in range(2):
-                        accs[n, rule_set] = bank(tags[rule_set], [P, M])
-                        score_pass(accs[n, rule_set], rule_set, n, 0)
+                    group_z(0, half)
+            if c >= last - len(wb_pieces):
+                group_wb(*wb_pieces[c - (last - len(wb_pieces))])
 
-        quantize_z(1, 0, nc.scalar.copy)
-        quantize_z(1, 1, nc.vector.tensor_copy)
-        for n, tags in ((2, ("sum0", "sum1")), (3, ("words0", "words1"))):
-            for rule_set in range(2):
-                accs[n, rule_set] = bank(tags[rule_set], [P, M])
-                score_pass(accs[n, rule_set], rule_set, n, 0)
+        wg_a = keep.tile([P, BANK], F32, name="wg7a", tag="tail_a", align_bytes=ALIGN)
+        weights(last, wg_a, slice(0, BANK))
+        wg_b = keep.tile([P, BANK], F32, name="wg7b", tag="tail_b", align_bytes=ALIGN)
+        weights(last, wg_b, slice(BANK, S))
+        scatter(h, wg_a, 0, BANK)
+        z_codes[0] = keep.tile([P, M], U32, name="z_codes0", tag="tail_a", align_bytes=ALIGN)
+        for half in range(2):
+            quantize_z(0, half)
+        scatter(h, wg_b, BANK, S)
+        accs = {}
+        for n, tag in enumerate(("score0", "score1", "feat0", "feat1")):
+            accs[n, 0] = bank(tag, [P, M])
+            score_pass(accs[n, 0], 0, n, 0)
+        x = keep.tile([P, M], F32, name="x7", tag="w1_last1")
+        for half in range(2):
+            gather(x, half * M_HALF, (half + 1) * M_HALF)
+        wb_codes = keep.tile([P, R_PASSES, N], U32, tag="tail_b", align_bytes=ALIGN)
+        for a, lo, hi in wb_pieces:
+            nc.vector.quantize_mx(
+                out=wb_codes[:, a, lo:hi].bitcast(FP8X4), scales=wb_scales[:, a, lo:hi], in_=wb_grouped[a, lo][:]
+            )
+        for half in range(2):
+            turn_and_round(last, x, half)
+        z_codes[1] = keep.tile([P, M], U32, name="z_codes1", align_bytes=ALIGN)
+        for half in range(2):
+            group_z(1, half)
+            quantize_z(1, half)
+        for n, tag in enumerate(("sum0", "sum1", "words0", "words1")):
+            accs[n, 1] = bank(tag, [P, M])
+            score_pass(accs[n, 1], 1, n, 0)
 
-        late_tags = (("score0", "score1"), ("feat0", "feat1"))
+        reused = (("score0", "sum0"), ("score1", "sum1"))
         for n in range(N_TILES):
             for rule_set in range(2):
                 if n >= 4:
-                    accs[n, rule_set] = bank(late_tags[n - 4][rule_set], [P, M])
+                    accs[n, rule_set] = bank(reused[n - 4][rule_set], [P, M])
                     score_pass(accs[n, rule_set], rule_set, n, 0)
                 score_pass(accs[n, rule_set], rule_set, n, 1)
-            ya = ring.tile([P, M], F32, name=f"ya{n}", tag="ya", bufs=3)
+            ya = keep.tile([P, M], F32, name=f"ya{n}", tag=f"w1_last{n + 2}")
             nc.scalar.copy(out=ya[:], in_=accs[n, 0][:])
-            best = keep.tile([P, M], F32, name=f"best{n}", tag="best", bufs=6)
+            best = keep.tile([P, M], F32, name=f"best{n}", tag=f"sess{n}")
             nc.vector.tensor_tensor(best[:], accs[n, 1][:], ya[:], ALU.max)
             nc.sync.dma_start(out=out[n * P : (n + 1) * P, :], in_=best[:])

@@ -29,6 +29,8 @@ TILES_PER_PASS = K_PASS // P
 M_HALF = M // 2
 LIST_ROWS = 16
 ALIGN = 64
+WB_PIECE = 256
+LAST_CUT = 768
 
 
 def interleave(nc, grouped, raw):
@@ -44,30 +46,23 @@ def tile_list_session_slot_verdict_kernel(
     nc = tc.nc
     with ExitStack() as ctx:
         keep = ctx.enter_context(tc.tile_pool(name="keep", bufs=1))
-        ring = ctx.enter_context(tc.tile_pool(name="ring", bufs=2))
         psum = ctx.enter_context(tc.psum_pool(name="psum", bufs=1))
 
         def bank(tag, shape):
             return psum.tile(shape, F32, name=tag, tag=tag)
 
-        table_scales = keep.tile([P, T], U8, align_bytes=ALIGN)
-        nc.gpsimd.memset(table_scales[:].bitcast(I32), 0)
-        for q in range(4):
-            nc.gpsimd.dma_start(
-                out=table_scales[32 * q : 32 * q + 4 * K_PASSES, :].bitcast(I32),
-                in_=tab_scales[:, 4 * q : 4 * q + 4, :].bitcast(I32),
-            )
-        page = keep.tile([P, T2], F32)
-        nc.vector.memset(page[:], 0.0)
-        wa_scale_sb = keep.tile([P, R_PASSES, N], U8, align_bytes=ALIGN)
-        nc.vector.memset(wa_scale_sb[:].rearrange("p a n -> p (a n)").bitcast(I32), 0)
-        gain_rows = keep.tile([P, P], F32)
-        nc.gpsimd.memset(gain_rows[:], 0.0)
-        nc.gpsimd.dma_start(out=gain_rows[0:R_TILES, :], in_=gain.rearrange("(c p) -> c p", p=P))
         ident = keep.tile([P, P], F32)
         make_identity(nc, ident[:])
         warm = keep.tile([P, 1], F32)
         nc.scalar.activation(out=warm[:], in_=ident[:, 0:1], func=ACT.Gelu_apprx_tanh)
+        table_scales = keep.tile([P, T], U8, align_bytes=ALIGN)
+        nc.vector.memset(table_scales[:].bitcast(I32), 0)
+        gain_rows = keep.tile([P, P], F32)
+        nc.vector.memset(gain_rows[:], 0.0)
+        page = keep.tile([P, T2], F32)
+        nc.vector.memset(page[:], 0.0)
+        wa_scale_sb = keep.tile([P, R_PASSES, N], U8, align_bytes=ALIGN)
+        nc.vector.memset(wa_scale_sb[:].rearrange("p a n -> p (a n)").bitcast(I32), 0)
 
         def load_table(a):
             words = keep.tile([P, T], U32, name=f"table_words{a}")
@@ -75,10 +70,8 @@ def tile_list_session_slot_verdict_kernel(
             return words
 
         def load_w1(c, a):
-            if a == K_PASSES - 1:
-                raw = keep.tile([P, PACK, P], F32, name=f"w1_raw{c}_{a}", tag=f"w1_last{c}")
-            else:
-                raw = keep.tile([P, PACK, P], F32, name=f"w1_raw{c}_{a}", tag=f"w1_raw{a}", bufs=5)
+            tag = "wg_odd" if (c, a) == (2, 1) else f"w1_raw{c}_{a}"
+            raw = keep.tile([P, PACK, P], F32, name=f"w1_raw{c}_{a}", tag=tag, align_bytes=ALIGN)
             rows = w1[a * K_PASS : (a + 1) * K_PASS, c * P : (c + 1) * P]
             nc.sync.dma_start(out=raw[:], in_=rows.rearrange("(p i) c -> p i c", i=PACK))
             return raw
@@ -88,29 +81,40 @@ def tile_list_session_slot_verdict_kernel(
             nc.sync.dma_start(out=rows[:], in_=sess[c * P : (c + 1) * P, :])
             return rows
 
+        def load_wb(a):
+            raw = keep.tile([P, PACK, N], F32, name=f"wb_raw{a}")
+            nc.sync.dma_start(out=raw[:], in_=wb[a * K_PASS : (a + 1) * K_PASS, :].rearrange("(p i) n -> p i n", i=PACK))
+            return raw
+
         list1 = keep.tile([P, S // LIST_ROWS], U16)
         nc.sync.dma_start(list1[:], offs)
-        table_words = [load_table(a) for a in range(K_PASSES)]
-        w1_raw = [[load_w1(0, a) for a in range(K_PASSES)]]
-        wgs_sb = keep.tile([P, S], F32)
-        nc.sync.dma_start(out=wgs_sb[:, 0:BANK], in_=wgs[:, 0:BANK])
+        table_words = [load_table(0)]
         list2 = keep.tile([P, S // LIST_ROWS], U16)
         nc.sync.dma_start(list2[:], offs2)
-        w1_raw.append([load_w1(1, a) for a in range(K_PASSES)])
-        nc.sync.dma_start(out=wgs_sb[:, BANK:S], in_=wgs[:, BANK:S])
         list3 = keep.tile([P, M // LIST_ROWS], U16)
         nc.sync.dma_start(list3[:], offs3)
+        for q in range(4):
+            nc.sync.dma_start(
+                out=table_scales[32 * q : 32 * q + 4 * K_PASSES, :].bitcast(I32),
+                in_=tab_scales[:, 4 * q : 4 * q + 4, :].bitcast(I32),
+            )
+        table_words.append(load_table(1))
+        nc.sync.dma_start(out=gain_rows[0:R_TILES, :], in_=gain.rearrange("(c p) -> c p", p=P))
+        w1_raw = [[load_w1(0, a) for a in range(K_PASSES)]]
+        table_words.append(load_table(2))
+        wgs_sb = keep.tile([P, S], F32)
+        nc.sync.dma_start(out=wgs_sb[:, 0:BANK], in_=wgs[:, 0:BANK])
+        nc.sync.dma_start(out=wgs_sb[:, BANK:S], in_=wgs[:, BANK:S])
+        w1_raw.append([load_w1(1, a) for a in range(K_PASSES)])
         sess_sb = []
+        wb_raw = []
         for c in range(2, R_TILES):
             w1_raw.append([load_w1(c, a) for a in range(K_PASSES)])
             sess_sb.append(load_sess(c - 2))
+            if c in (3, 5):
+                wb_raw.append(load_wb(len(wb_raw)))
         for c in range(R_TILES - 2, R_TILES):
             sess_sb.append(load_sess(c))
-        wb_raw = []
-        for a in range(R_PASSES):
-            raw = keep.tile([P, PACK, N], F32, name=f"wb_raw{a}")
-            nc.sync.dma_start(out=raw[:], in_=wb[a * K_PASS : (a + 1) * K_PASS, :].rearrange("(p i) n -> p i n", i=PACK))
-            wb_raw.append(raw)
         wa_codes = keep.tile([P, R_PASSES, 2 * N], U8, align_bytes=ALIGN)
         nc.sync.dma_start(out=wa_codes[:].bitcast(I32), in_=wa_words.rearrange("a p n -> p a n").bitcast(I32))
         for q in range(4):
@@ -119,7 +123,7 @@ def tile_list_session_slot_verdict_kernel(
                 in_=wa_scales[:, 4 * q : 4 * q + 4, :].rearrange("a r n -> r a n").bitcast(I32),
             )
 
-        gain_ps = bank("words0", [P, P])
+        gain_ps = bank("score0", [P, P])
         nc.tensor.transpose(gain_ps[:], gain_rows[:], ident[:])
         gain_col = keep.tile([P, R_TILES], F32)
         nc.scalar.copy(out=gain_col[:], in_=gain_ps[:, 0:R_TILES])
@@ -127,7 +131,7 @@ def tile_list_session_slot_verdict_kernel(
         v_words = [keep.tile([P, S], U32, name=f"v_words{a}", align_bytes=ALIGN) for a in range(K_PASSES)]
         v_scales = keep.tile([P, S], U8, align_bytes=ALIGN)
         nc.vector.tensor_copy(v_scales[:], table_scales[:].indirect(list1[:]))
-        for a in range(K_PASSES):
+        for a in range(K_PASSES - 1):
             nc.vector.tensor_copy(v_words[a][:], table_words[a][:].indirect(list1[:]))
 
         w1_codes = {}
@@ -136,62 +140,80 @@ def tile_list_session_slot_verdict_kernel(
         w1_grouped = {}
 
         def group_w1(c):
-            w1_grouped[c] = keep.tile([P, K_PASSES * K_PASS], BF16, name=f"w1_grouped{c}", tag="w1_grouped", align_bytes=ALIGN)
+            shared = f"w1_scales{(c + 1) % 2}"
+            if c == 1:
+                whole = keep.tile([P, K_PASSES * K_PASS], BF16, name="w1_grouped1", tag=shared, align_bytes=ALIGN)
+                parts = [whole[:, a * K_PASS : (a + 1) * K_PASS] for a in range(K_PASSES)]
+                w1_grouped[c] = (whole[:, 0 : 2 * K_PASS], parts[2])
+            else:
+                front = keep.tile([P, 2 * K_PASS], BF16, name=f"w1_front{c}", tag="w1_front", align_bytes=ALIGN)
+                back = keep.tile([P, K_PASS], BF16, name=f"w1_back{c}", tag=shared if c != 2 else "w1_raw0_2", align_bytes=ALIGN)
+                parts = [front[:, 0:K_PASS], front[:, K_PASS : 2 * K_PASS], back[:]]
+                w1_grouped[c] = (front[:], back[:])
             for a in range(K_PASSES):
-                interleave(nc, w1_grouped[c][:, a * K_PASS : (a + 1) * K_PASS], w1_raw[c][a][:])
-            w1_codes[c] = keep.tile([P, K_PASSES * P], U32, name=f"w1_codes{c}", tag="w1_codes", bufs=3, align_bytes=ALIGN)
-            w1_scales[c] = keep.tile([P, K_PASSES * P], U8, name=f"w1_scales{c}", tag="w1_scales", bufs=3, align_bytes=ALIGN)
+                interleave(nc, parts[a], w1_raw[c][a][:])
+            w1_codes[c] = keep.tile([P, K_PASSES * P], U32, name=f"w1_codes{c}", tag="w1_codes", align_bytes=ALIGN)
+            w1_scales[c] = keep.tile([P, K_PASSES * P], U8, name=f"w1_scales{c}", tag=f"w1_scales{c % 2}", align_bytes=ALIGN)
 
-        def quantize_w1(c, first_pass, end_pass):
-            lo, hi = first_pass * P, end_pass * P
+        def quantize_w1(c, part):
+            lo, hi = ((0, 2 * P), (2 * P, 3 * P))[part]
             nc.vector.quantize_mx(
-                out=w1_codes[c][:, lo:hi].bitcast(FP8X4),
-                scales=w1_scales[c][:, lo:hi],
-                in_=w1_grouped[c][:, PACK * lo : PACK * hi],
+                out=w1_codes[c][:, lo:hi].bitcast(FP8X4), scales=w1_scales[c][:, lo:hi], in_=w1_grouped[c][part]
             )
 
+        def multiply_features(c, half):
+            cols = slice(half * BANK, (half + 1) * BANK)
+            acc = bank(f"feat{half}", [P, BANK])
+            for a in range(K_PASSES):
+                nc.tensor.matmul_mx(
+                    out=acc[:],
+                    lhsT=w1_codes[c][:, a * P : (a + 1) * P].bitcast(FP8X4),
+                    lhsT_scale=w1_scales[c][:, a * P : (a + 1) * P],
+                    rhs=v_words[a][:, cols].bitcast(FP8X4),
+                    rhs_scale=v_scales[4 * a : P, cols],
+                    start=(a == 0),
+                    stop=(a == K_PASSES - 1),
+                )
+            return acc
+
         def features(c):
-            h = ring.tile([P, S], F32, name=f"h{c}", tag="h")
+            h = keep.tile([P, S], F32, name=f"h{c}", tag=f"h{c % 2}", align_bytes=ALIGN)
             for half in range(2):
-                cols = slice(half * BANK, (half + 1) * BANK)
-                acc = bank(f"feat{half}", [P, BANK])
-                for a in range(K_PASSES):
-                    nc.tensor.matmul_mx(
-                        out=acc[:],
-                        lhsT=w1_codes[c][:, a * P : (a + 1) * P].bitcast(FP8X4),
-                        lhsT_scale=w1_scales[c][:, a * P : (a + 1) * P],
-                        rhs=v_words[a][:, cols].bitcast(FP8X4),
-                        rhs_scale=v_scales[4 * a : P, cols],
-                        start=(a == 0),
-                        stop=(a == K_PASSES - 1),
-                    )
-                nc.scalar.activation(out=h[:, cols], in_=acc[:], func=ACT.Gelu_apprx_tanh)
+                acc = multiply_features(c, half)
+                nc.scalar.activation(out=h[:, half * BANK : (half + 1) * BANK], in_=acc[:], func=ACT.Gelu_apprx_tanh)
             return h
 
-        def weights(c, tile, cols):
-            nc.scalar.activation(out=tile[:], in_=wgs_sb[:, cols], func=ACT.Copy, scale=gain_col[:, c : c + 1])
+        def weights(c, wg, cols):
+            nc.scalar.activation(out=wg, in_=wgs_sb[:, cols], func=ACT.Copy, scale=gain_col[:, c : c + 1])
 
         zt_pairs = {}
         z_grouped = {}
         z_codes = {}
         z_scales = keep.tile([P, R_PASSES, M], U8, align_bytes=ALIGN)
 
-        def turn_and_round(c, x, half):
+        def turn(zt, src, half, first):
+            for t in range(2):
+                m0 = half * M_HALF + t * P
+                nc.tensor.matmul(
+                    zt[:, t, :],
+                    src[:, m0 : m0 + P],
+                    ident[:],
+                    start=(first and t == 0),
+                    stop=(not first and t == 1),
+                    is_transpose=True,
+                )
+
+        def open_sums(c):
+            sums = [bank(f"sum{half}", [P, 2, P]) for half in range(2)]
+            for half in range(2):
+                turn(sums[half], sess_sb[c], half, True)
+            return sums
+
+        def close_and_round(c, zt, x, half):
             a, sub = divmod(c, TILES_PER_PASS)
             if sub == 0:
                 zt_pairs[a, half] = keep.tile([P, 2, 2, P, 2], BF16, name=f"zt_pairs{a}_{half}", tag=f"zt_pairs{half}")
-            zt = bank(f"sum{half}", [P, 2, P])
-            for step, src in enumerate((sess_sb[c], x)):
-                for t in range(2):
-                    m0 = half * M_HALF + t * P
-                    nc.tensor.matmul(
-                        zt[:, t, :],
-                        src[:, m0 : m0 + P],
-                        ident[:],
-                        start=(step == 0 and t == 0),
-                        stop=(step == 1 and t == 1),
-                        is_transpose=True,
-                    )
+            turn(zt, x, half, False)
             nc.scalar.copy(
                 out=zt_pairs[a, half][:, :, :, 32 * sub : 32 * sub + 32, :],
                 in_=zt[:].rearrange("p t (q u e) -> p t u q e", u=2, e=2),
@@ -199,7 +221,7 @@ def tile_list_session_slot_verdict_kernel(
 
         def group_z(a, half):
             words = zt_pairs[a, half][:].rearrange("p t u q e -> p (t u q e)").bitcast(F32)
-            turned = bank(f"words{half}", [P, 4, P])
+            turned = bank(f"sum{half}", [P, 4, P])
             for j in range(4):
                 nc.tensor.transpose(turned[:, j, :], words[:, j * P : (j + 1) * P], ident[:])
             z_grouped[a, half] = keep.tile([P, PACK * M_HALF], BF16, name=f"z_grouped{a}_{half}", align_bytes=ALIGN)
@@ -214,12 +236,12 @@ def tile_list_session_slot_verdict_kernel(
                 out=z_codes[a][:, cols].bitcast(FP8X4), scales=z_scales[:, a, cols], in_=z_grouped[a, half][:]
             )
 
-        wb_pieces = [(a, lo, hi) for a in range(R_PASSES) for lo, hi in ((0, BANK), (BANK, N))]
+        wb_pieces = [(a, lo, lo + WB_PIECE) for a in range(R_PASSES) for lo in range(0, N, WB_PIECE)]
         wb_grouped = {}
         wb_scales = keep.tile([P, R_PASSES, N], U8, align_bytes=ALIGN)
 
-        def group_wb(a, lo, hi):
-            wb_grouped[a, lo] = keep.tile([P, PACK * (hi - lo)], BF16, name=f"wb_grouped{a}_{lo}", align_bytes=ALIGN)
+        def group_wb(a, lo, hi, tag):
+            wb_grouped[a, lo] = keep.tile([P, PACK * (hi - lo)], BF16, name=f"wb_grouped{a}_{lo}", tag=tag, align_bytes=ALIGN)
             interleave(nc, wb_grouped[a, lo][:], wb_raw[a][:, :, lo:hi])
 
         def score_pass(acc, rule_set, n, a):
@@ -240,88 +262,97 @@ def tile_list_session_slot_verdict_kernel(
             )
 
         def scatter(h, wg, lo, hi):
-            nc.vector.tensor_tensor(page[:].indirect(list2[:, lo // LIST_ROWS : hi // LIST_ROWS]), h[:, lo:hi], wg[:], ALU.mult)
+            nc.vector.tensor_tensor(page[:].indirect(list2[:, lo // LIST_ROWS : hi // LIST_ROWS]), h, wg, ALU.mult)
 
         def gather(x, lo, hi):
             nc.vector.tensor_copy(x[:, lo:hi], page[:].indirect(list3[:, lo // LIST_ROWS : hi // LIST_ROWS]))
 
         last = R_TILES - 1
         group_w1(0)
-        for a in range(K_PASSES):
-            quantize_w1(0, a, a + 1)
-        h = features(0)
-        wg = ring.tile([P, BANK], F32, name="wg0a", tag="wg")
-        weights(0, wg, slice(0, BANK))
-        scatter(h, wg, 0, BANK)
+        for part in range(2):
+            quantize_w1(0, part)
+        for lo in (0, BANK):
+            nc.vector.tensor_copy(
+                v_words[K_PASSES - 1][:, lo : lo + BANK],
+                table_words[K_PASSES - 1][:].indirect(list1[:, lo // LIST_ROWS : (lo + BANK) // LIST_ROWS]),
+            )
+        accs = [multiply_features(0, half) for half in range(2)]
+        wg = keep.tile([P, S], F32, name="wg0", tag="wg_even", align_bytes=ALIGN)
+        h = keep.tile([P, BANK], F32, name="h0a", tag="h0", align_bytes=ALIGN)
+        nc.scalar.activation(out=h[:], in_=accs[0][:], func=ACT.Gelu_apprx_tanh)
+        for lo in (0, BANK):
+            weights(0, wg[:, lo : lo + BANK], slice(lo, lo + BANK))
+        scatter(h[:], wg[:, 0:BANK], 0, BANK)
         group_w1(1)
-        quantize_w1(1, 0, 2)
-        quantize_w1(1, 2, 3)
-        wg = keep.tile([P, BANK], F32, name="wg0b", tag="w1_last1")
-        weights(0, wg, slice(BANK, S))
-        scatter(h, wg, BANK, S)
+        for part in range(2):
+            quantize_w1(1, part)
+        h = keep.tile([P, BANK], F32, name="h0b", tag="w1_raw1_2", align_bytes=ALIGN)
+        nc.scalar.activation(out=h[:], in_=accs[1][:], func=ACT.Gelu_apprx_tanh)
+        scatter(h[:], wg[:, BANK:S], BANK, S)
 
         for c in range(last):
             if c > 0:
-                scatter(h, wg, 0, S)
+                scatter(h[:], wg[:], 0, S)
             h = features(c + 1)
-            if c + 1 < last:
-                wg = ring.tile([P, S], F32, name=f"wg{c + 1}", tag="wg")
-                weights(c + 1, wg, slice(0, S))
             if c + 2 <= last:
                 group_w1(c + 2)
-                quantize_w1(c + 2, 0, 2)
-            x = keep.tile([P, M], F32, name=f"x{c}", tag=f"w1_last{(c + 2) % R_TILES}")
+            if c + 1 < last:
+                wg = keep.tile([P, S], F32, name=f"wg{c + 1}", tag=("wg_odd", "wg_even")[c % 2], align_bytes=ALIGN)
+                weights(c + 1, wg[:], slice(0, S))
+            else:
+                wg_a = keep.tile([P, LAST_CUT], F32, name="wg7a", tag="wg_odd", align_bytes=ALIGN)
+                weights(last, wg_a[:], slice(0, LAST_CUT))
+                wg_b = keep.tile([P, S - LAST_CUT], F32, name="wg7b", tag="wg_even", align_bytes=ALIGN)
+                weights(last, wg_b[:], slice(LAST_CUT, S))
+            if c + 2 <= last:
+                quantize_w1(c + 2, 0)
+            tag = f"w1_raw{c + 2}_{K_PASSES - 1}" if c + 2 <= last else f"w1_scales{last % 2}"
+            x = keep.tile([P, M], F32, name=f"x{c}", tag=tag, align_bytes=ALIGN)
+            sums = open_sums(c)
             gather(x, 0, M)
             if c + 2 <= last:
-                quantize_w1(c + 2, 2, 3)
+                quantize_w1(c + 2, 1)
             for half in range(2):
-                turn_and_round(c, x, half)
+                close_and_round(c, sums[half], x, half)
+            if c > 0:
+                group_wb(*wb_pieces[c - 1], tag)
             if c == TILES_PER_PASS - 1:
                 for half in range(2):
                     group_z(0, half)
-            if c >= last - len(wb_pieces):
-                group_wb(*wb_pieces[c - (last - len(wb_pieces))])
 
-        wg_a = keep.tile([P, BANK], F32, name="wg7a", tag="tail_a", align_bytes=ALIGN)
-        weights(last, wg_a, slice(0, BANK))
-        wg_b = keep.tile([P, BANK], F32, name="wg7b", tag="tail_b", align_bytes=ALIGN)
-        weights(last, wg_b, slice(BANK, S))
-        scatter(h, wg_a, 0, BANK)
-        z_codes[0] = keep.tile([P, M], U32, name="z_codes0", tag="tail_a", align_bytes=ALIGN)
+        sums = open_sums(last)
+        scatter(h[:, 0:LAST_CUT], wg_a[:], 0, LAST_CUT)
+        z_codes[0] = keep.tile([P, M], U32, name="z_codes0", tag="wg_odd", align_bytes=ALIGN)
         for half in range(2):
             quantize_z(0, half)
-        scatter(h, wg_b, BANK, S)
+        scatter(h[:, LAST_CUT:S], wg_b[:], LAST_CUT, S)
         accs = {}
-        for n, tag in enumerate(("score0", "score1", "feat0", "feat1")):
+        first_banks = ("score0", "score1", "score2", "score3", "feat0", "feat1")
+        for n, tag in enumerate(first_banks):
             accs[n, 0] = bank(tag, [P, M])
             score_pass(accs[n, 0], 0, n, 0)
-        x = keep.tile([P, M], F32, name="x7", tag="w1_last1")
+        x = keep.tile([P, M], F32, name="x7", tag="w1_raw0_0", align_bytes=ALIGN)
         for half in range(2):
             gather(x, half * M_HALF, (half + 1) * M_HALF)
-        wb_codes = keep.tile([P, R_PASSES, N], U32, tag="tail_b", align_bytes=ALIGN)
+        wb_codes = keep.tile([P, R_PASSES, N], U32, tag="wg_even", align_bytes=ALIGN)
         for a, lo, hi in wb_pieces:
             nc.vector.quantize_mx(
                 out=wb_codes[:, a, lo:hi].bitcast(FP8X4), scales=wb_scales[:, a, lo:hi], in_=wb_grouped[a, lo][:]
             )
         for half in range(2):
-            turn_and_round(last, x, half)
+            close_and_round(last, sums[half], x, half)
         z_codes[1] = keep.tile([P, M], U32, name="z_codes1", align_bytes=ALIGN)
         for half in range(2):
             group_z(1, half)
             quantize_z(1, half)
-        for n, tag in enumerate(("sum0", "sum1", "words0", "words1")):
-            accs[n, 1] = bank(tag, [P, M])
-            score_pass(accs[n, 1], 1, n, 0)
-
-        reused = (("score0", "sum0"), ("score1", "sum1"))
+        second_banks = ("sum0", "sum1") + first_banks
         for n in range(N_TILES):
-            for rule_set in range(2):
-                if n >= 4:
-                    accs[n, rule_set] = bank(reused[n - 4][rule_set], [P, M])
-                    score_pass(accs[n, rule_set], rule_set, n, 0)
-                score_pass(accs[n, rule_set], rule_set, n, 1)
-            ya = keep.tile([P, M], F32, name=f"ya{n}", tag=f"w1_last{n + 2}")
+            score_pass(accs[n, 0], 0, n, 1)
+            ya = keep.tile([P, M], F32, name=f"ya{n}", tag=f"w1_raw{n + 2}_0", align_bytes=ALIGN)
             nc.scalar.copy(out=ya[:], in_=accs[n, 0][:])
+            yb = bank(second_banks[n], [P, M])
+            for a in range(R_PASSES):
+                score_pass(yb, 1, n, a)
             best = keep.tile([P, M], F32, name=f"best{n}", tag=f"sess{n}")
-            nc.vector.tensor_tensor(best[:], accs[n, 1][:], ya[:], ALU.max)
+            nc.vector.tensor_tensor(best[:], yb[:], ya[:], ALU.max)
             nc.sync.dma_start(out=out[n * P : (n + 1) * P, :], in_=best[:])

@@ -19,16 +19,19 @@ ALU = mybir.AluOpType
 
 P = 128
 PACK = 4
-K_PASS = P * PACK
+PASS = P * PACK
 BANK = 512
-K_PASSES = K // K_PASS
-R_PASSES = H // K_PASS
-R_TILES = H // P
-N_TILES = N // P
-TILES_PER_PASS = K_PASS // P
-M_HALF = M // 2
+QUADRANT = 32
+SCALE_ROWS = 4
 LIST_ROWS = 16
 ALIGN = 64
+K_PASSES = K // PASS
+R_PASSES = H // PASS
+R_TILES = H // P
+N_TILES = N // P
+TILES_PER_PASS = PASS // P
+LAST = R_TILES - 1
+M_HALF = M // 2
 WB_PIECE = 256
 LAST_CUT = 768
 
@@ -40,120 +43,125 @@ def interleave(nc, grouped, raw):
     )
 
 
+def entries(offsets, lo, hi):
+    return offsets[:, lo // LIST_ROWS : hi // LIST_ROWS]
+
+
 def tile_list_session_slot_verdict_kernel(
     tc, tab_words, tab_scales, offs, w1, gain, wgs, offs2, offs3, sess, wa_words, wa_scales, wb, out
 ):
     nc = tc.nc
     with ExitStack() as ctx:
-        keep = ctx.enter_context(tc.tile_pool(name="keep", bufs=1))
+        sbuf = ctx.enter_context(tc.tile_pool(name="sbuf", bufs=1))
         psum = ctx.enter_context(tc.psum_pool(name="psum", bufs=1))
 
         def bank(tag, shape):
             return psum.tile(shape, F32, name=tag, tag=tag)
 
-        ident = keep.tile([P, P], F32)
+        ident = sbuf.tile([P, P], F32)
         make_identity(nc, ident[:])
-        warm = keep.tile([P, 1], F32)
+        warm = sbuf.tile([P, 1], F32)
         nc.scalar.activation(out=warm[:], in_=ident[:, 0:1], func=ACT.Gelu_apprx_tanh)
-        table_scales = keep.tile([P, T], U8, align_bytes=ALIGN)
+        table_scales = sbuf.tile([P, T], U8, align_bytes=ALIGN)
         nc.vector.memset(table_scales[:].bitcast(I32), 0)
-        gain_rows = keep.tile([P, P], F32)
+        gain_rows = sbuf.tile([P, P], F32)
         nc.vector.memset(gain_rows[:], 0.0)
-        page = keep.tile([P, T2], F32)
+        page = sbuf.tile([P, T2], F32)
         nc.vector.memset(page[:], 0.0)
-        wa_scale_sb = keep.tile([P, R_PASSES, N], U8, align_bytes=ALIGN)
-        nc.vector.memset(wa_scale_sb[:].rearrange("p a n -> p (a n)").bitcast(I32), 0)
+        wa_scale_tile = sbuf.tile([P, R_PASSES, N], U8, align_bytes=ALIGN)
+        nc.vector.memset(wa_scale_tile[:].rearrange("p a n -> p (a n)").bitcast(I32), 0)
 
         def load_table(a):
-            words = keep.tile([P, T], U32, name=f"table_words{a}")
+            words = sbuf.tile([P, T], U32, name=f"table_words{a}")
             nc.sync.dma_start(out=words[:].bitcast(I32), in_=tab_words[a].rearrange("p t i -> p (t i)").bitcast(I32))
             return words
 
-        def load_w1(c, a):
-            tag = "wg_odd" if (c, a) == (2, 1) else f"w1_raw{c}_{a}"
-            raw = keep.tile([P, PACK, P], F32, name=f"w1_raw{c}_{a}", tag=tag, align_bytes=ALIGN)
-            rows = w1[a * K_PASS : (a + 1) * K_PASS, c * P : (c + 1) * P]
-            nc.sync.dma_start(out=raw[:], in_=rows.rearrange("(p i) c -> p i c", i=PACK))
-            return raw
+        def load_w1(c):
+            tiles = []
+            for a in range(K_PASSES):
+                tag = "wg_odd" if (c, a) == (2, 1) else f"w1_raw{c}_{a}"
+                raw = sbuf.tile([P, PACK, P], F32, name=f"w1_raw{c}_{a}", tag=tag, align_bytes=ALIGN)
+                rows = w1[a * PASS : (a + 1) * PASS, c * P : (c + 1) * P]
+                nc.sync.dma_start(out=raw[:], in_=rows.rearrange("(p i) c -> p i c", i=PACK))
+                tiles.append(raw)
+            return tiles
 
         def load_sess(c):
-            rows = keep.tile([P, M], F32, name=f"sess{c}", tag=f"sess{c}")
+            rows = sbuf.tile([P, M], F32, name=f"sess{c}", tag=f"sess{c}")
             nc.sync.dma_start(out=rows[:], in_=sess[c * P : (c + 1) * P, :])
             return rows
 
         def load_wb(a):
-            raw = keep.tile([P, PACK, N], F32, name=f"wb_raw{a}")
-            nc.sync.dma_start(out=raw[:], in_=wb[a * K_PASS : (a + 1) * K_PASS, :].rearrange("(p i) n -> p i n", i=PACK))
+            raw = sbuf.tile([P, PACK, N], F32, name=f"wb_raw{a}")
+            nc.sync.dma_start(out=raw[:], in_=wb[a * PASS : (a + 1) * PASS, :].rearrange("(p i) n -> p i n", i=PACK))
             return raw
 
-        list1 = keep.tile([P, S // LIST_ROWS], U16)
-        nc.sync.dma_start(list1[:], offs)
+        idx = sbuf.tile([P, S // LIST_ROWS], U16)
+        nc.sync.dma_start(idx[:], offs)
         table_words = [load_table(0)]
-        list2 = keep.tile([P, S // LIST_ROWS], U16)
-        nc.sync.dma_start(list2[:], offs2)
-        list3 = keep.tile([P, M // LIST_ROWS], U16)
-        nc.sync.dma_start(list3[:], offs3)
-        for q in range(4):
+        idx2 = sbuf.tile([P, S // LIST_ROWS], U16)
+        nc.sync.dma_start(idx2[:], offs2)
+        idx3 = sbuf.tile([P, M // LIST_ROWS], U16)
+        nc.sync.dma_start(idx3[:], offs3)
+        for q in range(P // QUADRANT):
             nc.sync.dma_start(
-                out=table_scales[32 * q : 32 * q + 4 * K_PASSES, :].bitcast(I32),
-                in_=tab_scales[:, 4 * q : 4 * q + 4, :].bitcast(I32),
+                out=table_scales[QUADRANT * q : QUADRANT * q + SCALE_ROWS * K_PASSES, :].bitcast(I32),
+                in_=tab_scales[:, SCALE_ROWS * q : SCALE_ROWS * (q + 1), :].bitcast(I32),
             )
         table_words.append(load_table(1))
         nc.sync.dma_start(out=gain_rows[0:R_TILES, :], in_=gain.rearrange("(c p) -> c p", p=P))
-        w1_raw = [[load_w1(0, a) for a in range(K_PASSES)]]
+        w1_raw = [load_w1(0)]
         table_words.append(load_table(2))
-        wgs_sb = keep.tile([P, S], F32)
-        nc.sync.dma_start(out=wgs_sb[:, 0:BANK], in_=wgs[:, 0:BANK])
-        nc.sync.dma_start(out=wgs_sb[:, BANK:S], in_=wgs[:, BANK:S])
-        w1_raw.append([load_w1(1, a) for a in range(K_PASSES)])
-        sess_sb = []
+        wgs_tile = sbuf.tile([P, S], F32)
+        for lo in range(0, S, BANK):
+            nc.sync.dma_start(out=wgs_tile[:, lo : lo + BANK], in_=wgs[:, lo : lo + BANK])
+        w1_raw.append(load_w1(1))
+        sess_tiles = []
         wb_raw = []
         for c in range(2, R_TILES):
-            w1_raw.append([load_w1(c, a) for a in range(K_PASSES)])
-            sess_sb.append(load_sess(c - 2))
+            w1_raw.append(load_w1(c))
+            sess_tiles.append(load_sess(c - 2))
             if c in (3, 5):
                 wb_raw.append(load_wb(len(wb_raw)))
         for c in range(R_TILES - 2, R_TILES):
-            sess_sb.append(load_sess(c))
-        wa_codes = keep.tile([P, R_PASSES, 2 * N], U8, align_bytes=ALIGN)
+            sess_tiles.append(load_sess(c))
+        wa_codes = sbuf.tile([P, R_PASSES, 2 * N], U8, align_bytes=ALIGN)
         nc.sync.dma_start(out=wa_codes[:].bitcast(I32), in_=wa_words.rearrange("a p n -> p a n").bitcast(I32))
-        for q in range(4):
+        for q in range(P // QUADRANT):
             nc.sync.dma_start(
-                out=wa_scale_sb[32 * q : 32 * q + 4, :, :].bitcast(I32),
-                in_=wa_scales[:, 4 * q : 4 * q + 4, :].rearrange("a r n -> r a n").bitcast(I32),
+                out=wa_scale_tile[QUADRANT * q : QUADRANT * q + SCALE_ROWS, :, :].bitcast(I32),
+                in_=wa_scales[:, SCALE_ROWS * q : SCALE_ROWS * (q + 1), :].rearrange("a r n -> r a n").bitcast(I32),
             )
 
-        gain_ps = bank("score0", [P, P])
-        nc.tensor.transpose(gain_ps[:], gain_rows[:], ident[:])
-        gain_col = keep.tile([P, R_TILES], F32)
-        nc.scalar.copy(out=gain_col[:], in_=gain_ps[:, 0:R_TILES])
+        gain_turned = bank("score0", [P, P])
+        nc.tensor.transpose(gain_turned[:], gain_rows[:], ident[:])
+        gain_col = sbuf.tile([P, R_TILES], F32)
+        nc.scalar.copy(out=gain_col[:], in_=gain_turned[:, 0:R_TILES])
 
-        v_words = [keep.tile([P, S], U32, name=f"v_words{a}", align_bytes=ALIGN) for a in range(K_PASSES)]
-        v_scales = keep.tile([P, S], U8, align_bytes=ALIGN)
-        nc.vector.tensor_copy(v_scales[:], table_scales[:].indirect(list1[:]))
+        v_words = [sbuf.tile([P, S], U32, name=f"v_words{a}", align_bytes=ALIGN) for a in range(K_PASSES)]
+        v_scales = sbuf.tile([P, S], U8, align_bytes=ALIGN)
+        nc.vector.tensor_copy(v_scales[:], table_scales[:].indirect(idx[:]))
         for a in range(K_PASSES - 1):
-            nc.vector.tensor_copy(v_words[a][:], table_words[a][:].indirect(list1[:]))
+            nc.vector.tensor_copy(v_words[a][:], table_words[a][:].indirect(idx[:]))
 
+        w1_grouped = {}
         w1_codes = {}
         w1_scales = {}
 
-        w1_grouped = {}
-
         def group_w1(c):
-            shared = f"w1_scales{(c + 1) % 2}"
+            previous_scales = f"w1_scales{(c - 1) % 2}"
             if c == 1:
-                whole = keep.tile([P, K_PASSES * K_PASS], BF16, name="w1_grouped1", tag=shared, align_bytes=ALIGN)
-                parts = [whole[:, a * K_PASS : (a + 1) * K_PASS] for a in range(K_PASSES)]
-                w1_grouped[c] = (whole[:, 0 : 2 * K_PASS], parts[2])
+                whole = sbuf.tile([P, K_PASSES * PASS], BF16, name="w1_grouped1", tag=previous_scales, align_bytes=ALIGN)
+                front, back = whole[:, 0 : 2 * PASS], whole[:, 2 * PASS : 3 * PASS]
             else:
-                front = keep.tile([P, 2 * K_PASS], BF16, name=f"w1_front{c}", tag="w1_front", align_bytes=ALIGN)
-                back = keep.tile([P, K_PASS], BF16, name=f"w1_back{c}", tag=shared if c != 2 else "w1_raw0_2", align_bytes=ALIGN)
-                parts = [front[:, 0:K_PASS], front[:, K_PASS : 2 * K_PASS], back[:]]
-                w1_grouped[c] = (front[:], back[:])
-            for a in range(K_PASSES):
-                interleave(nc, parts[a], w1_raw[c][a][:])
-            w1_codes[c] = keep.tile([P, K_PASSES * P], U32, name=f"w1_codes{c}", tag="w1_codes", align_bytes=ALIGN)
-            w1_scales[c] = keep.tile([P, K_PASSES * P], U8, name=f"w1_scales{c}", tag=f"w1_scales{c % 2}", align_bytes=ALIGN)
+                back_tag = "w1_raw0_2" if c == 2 else previous_scales
+                front = sbuf.tile([P, 2 * PASS], BF16, name=f"w1_front{c}", tag="w1_front", align_bytes=ALIGN)[:]
+                back = sbuf.tile([P, PASS], BF16, name=f"w1_back{c}", tag=back_tag, align_bytes=ALIGN)[:]
+            w1_grouped[c] = (front, back)
+            for a, grouped in enumerate((front[:, 0:PASS], front[:, PASS : 2 * PASS], back)):
+                interleave(nc, grouped, w1_raw[c][a][:])
+            w1_codes[c] = sbuf.tile([P, K_PASSES * P], U32, name=f"w1_codes{c}", tag="w1_codes", align_bytes=ALIGN)
+            w1_scales[c] = sbuf.tile([P, K_PASSES * P], U8, name=f"w1_scales{c}", tag=f"w1_scales{c % 2}", align_bytes=ALIGN)
 
         def quantize_w1(c, part):
             lo, hi = ((0, 2 * P), (2 * P, 3 * P))[part]
@@ -161,7 +169,7 @@ def tile_list_session_slot_verdict_kernel(
                 out=w1_codes[c][:, lo:hi].bitcast(FP8X4), scales=w1_scales[c][:, lo:hi], in_=w1_grouped[c][part]
             )
 
-        def multiply_features(c, half):
+        def multiply_w1(c, half):
             cols = slice(half * BANK, (half + 1) * BANK)
             acc = bank(f"feat{half}", [P, BANK])
             for a in range(K_PASSES):
@@ -170,52 +178,61 @@ def tile_list_session_slot_verdict_kernel(
                     lhsT=w1_codes[c][:, a * P : (a + 1) * P].bitcast(FP8X4),
                     lhsT_scale=w1_scales[c][:, a * P : (a + 1) * P],
                     rhs=v_words[a][:, cols].bitcast(FP8X4),
-                    rhs_scale=v_scales[4 * a : P, cols],
+                    rhs_scale=v_scales[SCALE_ROWS * a : P, cols],
                     start=(a == 0),
                     stop=(a == K_PASSES - 1),
                 )
             return acc
 
+        def gelu(dst, acc):
+            nc.scalar.activation(out=dst, in_=acc[:], func=ACT.Gelu_apprx_tanh)
+
         def features(c):
-            h = keep.tile([P, S], F32, name=f"h{c}", tag=f"h{c % 2}", align_bytes=ALIGN)
-            for half in range(2):
-                acc = multiply_features(c, half)
-                nc.scalar.activation(out=h[:, half * BANK : (half + 1) * BANK], in_=acc[:], func=ACT.Gelu_apprx_tanh)
+            h = sbuf.tile([P, S], F32, name=f"h{c}", tag=f"h{c % 2}", align_bytes=ALIGN)
+            for half in range(S // BANK):
+                gelu(h[:, half * BANK : (half + 1) * BANK], multiply_w1(c, half))
             return h
 
-        def weights(c, wg, cols):
-            nc.scalar.activation(out=wg, in_=wgs_sb[:, cols], func=ACT.Copy, scale=gain_col[:, c : c + 1])
+        def weigh(dst, c, lo, hi):
+            nc.scalar.activation(out=dst, in_=wgs_tile[:, lo:hi], func=ACT.Copy, scale=gain_col[:, c : c + 1])
+
+        def scatter(h, wg, lo, hi):
+            nc.vector.tensor_tensor(page[:].indirect(entries(idx2, lo, hi)), h, wg, ALU.mult)
+
+        def gather(x, lo, hi):
+            nc.vector.tensor_copy(x[:, lo:hi], page[:].indirect(entries(idx3, lo, hi)))
 
         zt_pairs = {}
         z_grouped = {}
         z_codes = {}
-        z_scales = keep.tile([P, R_PASSES, M], U8, align_bytes=ALIGN)
+        z_scales = sbuf.tile([P, R_PASSES, M], U8, align_bytes=ALIGN)
 
-        def turn(zt, src, half, first):
+        def turn(zt, rows, half, opens):
             for t in range(2):
                 m0 = half * M_HALF + t * P
                 nc.tensor.matmul(
                     zt[:, t, :],
-                    src[:, m0 : m0 + P],
+                    rows[:, m0 : m0 + P],
                     ident[:],
-                    start=(first and t == 0),
-                    stop=(not first and t == 1),
+                    start=(opens and t == 0),
+                    stop=(not opens and t == 1),
                     is_transpose=True,
                 )
 
         def open_sums(c):
             sums = [bank(f"sum{half}", [P, 2, P]) for half in range(2)]
             for half in range(2):
-                turn(sums[half], sess_sb[c], half, True)
+                turn(sums[half], sess_tiles[c], half, True)
             return sums
 
         def close_and_round(c, zt, x, half):
             a, sub = divmod(c, TILES_PER_PASS)
             if sub == 0:
-                zt_pairs[a, half] = keep.tile([P, 2, 2, P, 2], BF16, name=f"zt_pairs{a}_{half}", tag=f"zt_pairs{half}")
+                zt_pairs[a, half] = sbuf.tile([P, 2, 2, P, 2], BF16, name=f"zt_pairs{a}_{half}", tag=f"zt_pairs{half}")
             turn(zt, x, half, False)
+            quads = P // PACK
             nc.scalar.copy(
-                out=zt_pairs[a, half][:, :, :, 32 * sub : 32 * sub + 32, :],
+                out=zt_pairs[a, half][:, :, :, quads * sub : quads * (sub + 1), :],
                 in_=zt[:].rearrange("p t (q u e) -> p t u q e", u=2, e=2),
             )
 
@@ -224,7 +241,7 @@ def tile_list_session_slot_verdict_kernel(
             turned = bank(f"sum{half}", [P, 4, P])
             for j in range(4):
                 nc.tensor.transpose(turned[:, j, :], words[:, j * P : (j + 1) * P], ident[:])
-            z_grouped[a, half] = keep.tile([P, PACK * M_HALF], BF16, name=f"z_grouped{a}_{half}", align_bytes=ALIGN)
+            z_grouped[a, half] = sbuf.tile([P, PACK * M_HALF], BF16, name=f"z_grouped{a}_{half}", align_bytes=ALIGN)
             nc.scalar.copy(
                 out=z_grouped[a, half][:].bitcast(F32).rearrange("p (t m u) -> p t m u", t=2, u=2),
                 in_=turned[:].rearrange("p (t u) m -> p t m u", u=2),
@@ -238,19 +255,13 @@ def tile_list_session_slot_verdict_kernel(
 
         wb_pieces = [(a, lo, lo + WB_PIECE) for a in range(R_PASSES) for lo in range(0, N, WB_PIECE)]
         wb_grouped = {}
-        wb_scales = keep.tile([P, R_PASSES, N], U8, align_bytes=ALIGN)
+        wb_scales = sbuf.tile([P, R_PASSES, N], U8, align_bytes=ALIGN)
 
         def group_wb(a, lo, hi, tag):
-            wb_grouped[a, lo] = keep.tile([P, PACK * (hi - lo)], BF16, name=f"wb_grouped{a}_{lo}", tag=tag, align_bytes=ALIGN)
+            wb_grouped[a, lo] = sbuf.tile([P, PACK * (hi - lo)], BF16, name=f"wb_grouped{a}_{lo}", tag=tag, align_bytes=ALIGN)
             interleave(nc, wb_grouped[a, lo][:], wb_raw[a][:, :, lo:hi])
 
-        def score_pass(acc, rule_set, n, a):
-            if rule_set == 0:
-                codes = wa_codes[:, a, 2 * n * P : 2 * (n + 1) * P].bitcast(FP4X4)
-                scales = wa_scale_sb[:, a, n * P : (n + 1) * P]
-            else:
-                codes = wb_codes[:, a, n * P : (n + 1) * P].bitcast(FP8X4)
-                scales = wb_scales[:, a, n * P : (n + 1) * P]
+        def multiply_z(acc, codes, scales, a):
             nc.tensor.matmul_mx(
                 out=acc[:],
                 lhsT=codes,
@@ -261,98 +272,104 @@ def tile_list_session_slot_verdict_kernel(
                 stop=(a == R_PASSES - 1),
             )
 
-        def scatter(h, wg, lo, hi):
-            nc.vector.tensor_tensor(page[:].indirect(list2[:, lo // LIST_ROWS : hi // LIST_ROWS]), h, wg, ALU.mult)
+        def multiply_wa(acc, n, a):
+            codes = wa_codes[:, a, 2 * n * P : 2 * (n + 1) * P].bitcast(FP4X4)
+            multiply_z(acc, codes, wa_scale_tile[:, a, n * P : (n + 1) * P], a)
 
-        def gather(x, lo, hi):
-            nc.vector.tensor_copy(x[:, lo:hi], page[:].indirect(list3[:, lo // LIST_ROWS : hi // LIST_ROWS]))
+        def multiply_wb(acc, n, a):
+            codes = wb_codes[:, a, n * P : (n + 1) * P].bitcast(FP8X4)
+            multiply_z(acc, codes, wb_scales[:, a, n * P : (n + 1) * P], a)
 
-        last = R_TILES - 1
         group_w1(0)
         for part in range(2):
             quantize_w1(0, part)
-        for lo in (0, BANK):
+        for lo in range(0, S, BANK):
             nc.vector.tensor_copy(
                 v_words[K_PASSES - 1][:, lo : lo + BANK],
-                table_words[K_PASSES - 1][:].indirect(list1[:, lo // LIST_ROWS : (lo + BANK) // LIST_ROWS]),
+                table_words[K_PASSES - 1][:].indirect(entries(idx, lo, lo + BANK)),
             )
-        accs = [multiply_features(0, half) for half in range(2)]
-        wg = keep.tile([P, S], F32, name="wg0", tag="wg_even", align_bytes=ALIGN)
-        h = keep.tile([P, BANK], F32, name="h0a", tag="h0", align_bytes=ALIGN)
-        nc.scalar.activation(out=h[:], in_=accs[0][:], func=ACT.Gelu_apprx_tanh)
-        for lo in (0, BANK):
-            weights(0, wg[:, lo : lo + BANK], slice(lo, lo + BANK))
-        scatter(h[:], wg[:, 0:BANK], 0, BANK)
+        first_sums = [multiply_w1(0, half) for half in range(S // BANK)]
+        wg = sbuf.tile([P, S], F32, name="wg0", tag="wg_even", align_bytes=ALIGN)
+        h_front = sbuf.tile([P, BANK], F32, tag="h0", align_bytes=ALIGN)
+        gelu(h_front[:], first_sums[0])
+        for lo in range(0, S, BANK):
+            weigh(wg[:, lo : lo + BANK], 0, lo, lo + BANK)
+        scatter(h_front[:], wg[:, 0:BANK], 0, BANK)
         group_w1(1)
         for part in range(2):
             quantize_w1(1, part)
-        h = keep.tile([P, BANK], F32, name="h0b", tag="w1_raw1_2", align_bytes=ALIGN)
-        nc.scalar.activation(out=h[:], in_=accs[1][:], func=ACT.Gelu_apprx_tanh)
-        scatter(h[:], wg[:, BANK:S], BANK, S)
+        h_back = sbuf.tile([P, BANK], F32, tag="w1_raw1_2", align_bytes=ALIGN)
+        gelu(h_back[:], first_sums[1])
+        scatter(h_back[:], wg[:, BANK:S], BANK, S)
 
-        for c in range(last):
+        for c in range(LAST):
+            ahead = c + 2
             if c > 0:
                 scatter(h[:], wg[:], 0, S)
             h = features(c + 1)
-            if c + 2 <= last:
-                group_w1(c + 2)
-            if c + 1 < last:
-                wg = keep.tile([P, S], F32, name=f"wg{c + 1}", tag=("wg_odd", "wg_even")[c % 2], align_bytes=ALIGN)
-                weights(c + 1, wg[:], slice(0, S))
+            if ahead <= LAST:
+                group_w1(ahead)
+            if c + 1 < LAST:
+                wg = sbuf.tile([P, S], F32, name=f"wg{c + 1}", tag=("wg_odd", "wg_even")[c % 2], align_bytes=ALIGN)
+                weigh(wg[:], c + 1, 0, S)
             else:
-                wg_a = keep.tile([P, LAST_CUT], F32, name="wg7a", tag="wg_odd", align_bytes=ALIGN)
-                weights(last, wg_a[:], slice(0, LAST_CUT))
-                wg_b = keep.tile([P, S - LAST_CUT], F32, name="wg7b", tag="wg_even", align_bytes=ALIGN)
-                weights(last, wg_b[:], slice(LAST_CUT, S))
-            if c + 2 <= last:
-                quantize_w1(c + 2, 0)
-            tag = f"w1_raw{c + 2}_{K_PASSES - 1}" if c + 2 <= last else f"w1_scales{last % 2}"
-            x = keep.tile([P, M], F32, name=f"x{c}", tag=tag, align_bytes=ALIGN)
+                wg_front = sbuf.tile([P, LAST_CUT], F32, tag="wg_odd", align_bytes=ALIGN)
+                weigh(wg_front[:], LAST, 0, LAST_CUT)
+                wg_back = sbuf.tile([P, S - LAST_CUT], F32, tag="wg_even", align_bytes=ALIGN)
+                weigh(wg_back[:], LAST, LAST_CUT, S)
+            if ahead <= LAST:
+                quantize_w1(ahead, 0)
+            x_tag = f"w1_raw{ahead}_{K_PASSES - 1}" if ahead <= LAST else f"w1_scales{LAST % 2}"
+            x = sbuf.tile([P, M], F32, name=f"x{c}", tag=x_tag, align_bytes=ALIGN)
             sums = open_sums(c)
             gather(x, 0, M)
-            if c + 2 <= last:
-                quantize_w1(c + 2, 1)
+            if ahead <= LAST:
+                quantize_w1(ahead, 1)
             for half in range(2):
                 close_and_round(c, sums[half], x, half)
             if c > 0:
-                group_wb(*wb_pieces[c - 1], tag)
+                group_wb(*wb_pieces[c - 1], x_tag)
             if c == TILES_PER_PASS - 1:
                 for half in range(2):
                     group_z(0, half)
 
-        sums = open_sums(last)
-        scatter(h[:, 0:LAST_CUT], wg_a[:], 0, LAST_CUT)
-        z_codes[0] = keep.tile([P, M], U32, name="z_codes0", tag="wg_odd", align_bytes=ALIGN)
+        sums = open_sums(LAST)
+        scatter(h[:, 0:LAST_CUT], wg_front[:], 0, LAST_CUT)
+        z_codes[0] = sbuf.tile([P, M], U32, name="z_codes0", tag="wg_odd", align_bytes=ALIGN)
         for half in range(2):
             quantize_z(0, half)
-        scatter(h[:, LAST_CUT:S], wg_b[:], LAST_CUT, S)
-        accs = {}
-        first_banks = ("score0", "score1", "score2", "score3", "feat0", "feat1")
-        for n, tag in enumerate(first_banks):
-            accs[n, 0] = bank(tag, [P, M])
-            score_pass(accs[n, 0], 0, n, 0)
-        x = keep.tile([P, M], F32, name="x7", tag="w1_raw0_0", align_bytes=ALIGN)
+        scatter(h[:, LAST_CUT:S], wg_back[:], LAST_CUT, S)
+        wa_banks = ("score0", "score1", "score2", "score3", "feat0", "feat1")
+        wa_sums = []
+        for n in range(N_TILES):
+            wa_sums.append(bank(wa_banks[n], [P, M]))
+            multiply_wa(wa_sums[n], n, 0)
+        x = sbuf.tile([P, M], F32, name=f"x{LAST}", tag="w1_raw0_0", align_bytes=ALIGN)
         for half in range(2):
             gather(x, half * M_HALF, (half + 1) * M_HALF)
-        wb_codes = keep.tile([P, R_PASSES, N], U32, tag="wg_even", align_bytes=ALIGN)
+        wb_codes = sbuf.tile([P, R_PASSES, N], U32, tag="wg_even", align_bytes=ALIGN)
         for a, lo, hi in wb_pieces:
             nc.vector.quantize_mx(
                 out=wb_codes[:, a, lo:hi].bitcast(FP8X4), scales=wb_scales[:, a, lo:hi], in_=wb_grouped[a, lo][:]
             )
         for half in range(2):
-            close_and_round(last, sums[half], x, half)
-        z_codes[1] = keep.tile([P, M], U32, name="z_codes1", align_bytes=ALIGN)
+            close_and_round(LAST, sums[half], x, half)
+        z_codes[1] = sbuf.tile([P, M], U32, name="z_codes1", align_bytes=ALIGN)
         for half in range(2):
             group_z(1, half)
             quantize_z(1, half)
-        second_banks = ("sum0", "sum1") + first_banks
+
+        wb_banks = ("sum0", "sum1") + wa_banks
         for n in range(N_TILES):
-            score_pass(accs[n, 0], 0, n, 1)
-            ya = keep.tile([P, M], F32, name=f"ya{n}", tag=f"w1_raw{n + 2}_0", align_bytes=ALIGN)
-            nc.scalar.copy(out=ya[:], in_=accs[n, 0][:])
-            yb = bank(second_banks[n], [P, M])
+            multiply_wa(wa_sums[n], n, 1)
+            ya = sbuf.tile([P, M], F32, name=f"ya{n}", tag=f"w1_raw{n + 2}_0", align_bytes=ALIGN)
+            nc.scalar.copy(out=ya[:], in_=wa_sums[n][:])
+            wb_sum = bank(wb_banks[n], [P, M])
             for a in range(R_PASSES):
-                score_pass(yb, 1, n, a)
-            best = keep.tile([P, M], F32, name=f"best{n}", tag=f"sess{n}")
-            nc.vector.tensor_tensor(best[:], yb[:], ya[:], ALU.max)
-            nc.sync.dma_start(out=out[n * P : (n + 1) * P, :], in_=best[:])
+                multiply_wb(wb_sum, n, a)
+            best = sbuf.tile([P, M], F32, name=f"best{n}", tag=f"sess{n}")
+            width = M_HALF if n == N_TILES - 1 else M
+            for lo in range(0, M, width):
+                cols = slice(lo, lo + width)
+                nc.vector.tensor_tensor(best[:, cols], wb_sum[:, cols], ya[:, cols], ALU.max)
+                nc.sync.dma_start(out=out[n * P : (n + 1) * P, cols], in_=best[:, cols])

@@ -29,11 +29,13 @@ K_PASSES = K // PASS
 R_PASSES = H // PASS
 R_TILES = H // P
 N_TILES = N // P
-TILES_PER_PASS = PASS // P
+TURNED = PASS // P
 LAST = R_TILES - 1
 M_HALF = M // 2
 WB_PIECE = 256
+EARLY_WB = WB_PIECE // P
 LAST_CUT = 768
+WIDE_START = 5 * 4 * S
 
 
 def interleave(nc, grouped, raw):
@@ -53,120 +55,154 @@ def tile_list_session_slot_verdict_kernel(
     nc = tc.nc
     with ExitStack() as ctx:
         sbuf = ctx.enter_context(tc.tile_pool(name="sbuf", bufs=1))
+        placed = ctx.enter_context(tc.tile_pool(name="placed", bufs=1))
         psum = ctx.enter_context(tc.psum_pool(name="psum", bufs=1))
+
+        def tile(name, shape, dtype, tag=None):
+            return sbuf.tile(shape, dtype, name=name, tag=tag or name, align_bytes=ALIGN)
+
+        def place(name, shape, dtype, offset):
+            return placed.tile(shape, dtype, name=name, tag=name, align_bytes=ALIGN, offset=offset)
+
+        def plane_start(c):
+            return P + 4 * S * (c - TURNED)
 
         def bank(tag, shape):
             return psum.tile(shape, F32, name=tag, tag=tag)
 
-        ident = sbuf.tile([P, P], F32)
+        ident = tile("ident", [P, P], F32)
         make_identity(nc, ident[:])
-        warm = sbuf.tile([P, 1], F32)
-        nc.scalar.activation(out=warm[:], in_=ident[:, 0:1], func=ACT.Gelu_apprx_tanh)
-        table_scales = sbuf.tile([P, T], U8, align_bytes=ALIGN)
+        table_scales = tile("table_scales", [P, T], U8, tag="w1_scales0")
         nc.vector.memset(table_scales[:].bitcast(I32), 0)
-        gain_rows = sbuf.tile([P, P], F32)
+        for q in range(P // QUADRANT):
+            nc.gpsimd.dma_start(
+                out=table_scales[QUADRANT * q : QUADRANT * q + SCALE_ROWS * K_PASSES, :].bitcast(I32),
+                in_=tab_scales[:, SCALE_ROWS * q : SCALE_ROWS * (q + 1), :].bitcast(I32),
+            )
+        warm = tile("warm", [P, 1], F32)
+        nc.scalar.activation(out=warm[:], in_=ident[:, 0:1], func=ACT.Gelu_apprx_tanh)
+        gain_rows = tile("gain_rows", [P, P], F32)
         nc.vector.memset(gain_rows[:], 0.0)
-        page = sbuf.tile([P, T2], F32)
+        page = tile("page", [P, T2], F32)
         nc.vector.memset(page[:], 0.0)
-        wa_scale_tile = sbuf.tile([P, R_PASSES, N], U8, align_bytes=ALIGN)
+        wa_scale_tile = tile("wa_scale_tile", [P, R_PASSES, N], U8)
         nc.vector.memset(wa_scale_tile[:].rearrange("p a n -> p (a n)").bitcast(I32), 0)
 
         def load_table(a):
-            words = sbuf.tile([P, T], U32, name=f"table_words{a}")
+            words = tile(f"table_words{a}", [P, T], U32)
             nc.sync.dma_start(out=words[:].bitcast(I32), in_=tab_words[a].rearrange("p t i -> p (t i)").bitcast(I32))
             return words
 
         def load_w1(c):
             tiles = []
             for a in range(K_PASSES):
-                tag = "wg_odd" if (c, a) == (2, 1) else f"w1_raw{c}_{a}"
-                raw = sbuf.tile([P, PACK, P], F32, name=f"w1_raw{c}_{a}", tag=tag, align_bytes=ALIGN)
+                tag = "wg_odd" if (c, a) == (2, 1) else None
+                raw = tile(f"w1_raw{c}_{a}", [P, PACK, P], F32, tag=tag)
                 rows = w1[a * PASS : (a + 1) * PASS, c * P : (c + 1) * P]
                 nc.sync.dma_start(out=raw[:], in_=rows.rearrange("(p i) c -> p i c", i=PACK))
                 tiles.append(raw)
             return tiles
 
+        def load_wide(a):
+            if a < K_PASSES - 1:
+                wide = tile(f"w1_wide{a}", [P, PACK, PASS], F32)
+            else:
+                wide = place(f"w1_wide{a}", [P, PACK, PASS], F32, WIDE_START)
+            rows = w1[a * PASS : (a + 1) * PASS, PASS:H]
+            nc.sync.dma_start(out=wide[:], in_=rows.rearrange("(p i) c -> p i c", i=PACK))
+            return wide
+
         def load_sess(c):
-            rows = sbuf.tile([P, M], F32, name=f"sess{c}", tag=f"sess{c}")
-            nc.sync.dma_start(out=rows[:], in_=sess[c * P : (c + 1) * P, :])
+            rows = tile(f"sess{c}", [P, M], F32)
+            if c < TURNED:
+                nc.sync.dma_start(out=rows[:], in_=sess[c * P : (c + 1) * P, :])
+            else:
+                nc.sync.dma_start(out=rows[:], in_=sess[PASS:H, :].rearrange("(p t) m -> p t m", t=PACK)[:, c - TURNED, :])
             return rows
 
-        def load_wb(a):
-            raw = sbuf.tile([P, PACK, N], F32, name=f"wb_raw{a}")
-            nc.sync.dma_start(out=raw[:], in_=wb[a * PASS : (a + 1) * PASS, :].rearrange("(p i) n -> p i n", i=PACK))
-            return raw
-
+        table_words = [load_table(0)]
         idx = sbuf.tile([P, S // LIST_ROWS], U16)
         nc.sync.dma_start(idx[:], offs)
-        table_words = [load_table(0)]
-        idx2 = sbuf.tile([P, S // LIST_ROWS], U16)
-        nc.sync.dma_start(idx2[:], offs2)
-        idx3 = sbuf.tile([P, M // LIST_ROWS], U16)
-        nc.sync.dma_start(idx3[:], offs3)
-        for q in range(P // QUADRANT):
-            nc.sync.dma_start(
-                out=table_scales[QUADRANT * q : QUADRANT * q + SCALE_ROWS * K_PASSES, :].bitcast(I32),
-                in_=tab_scales[:, SCALE_ROWS * q : SCALE_ROWS * (q + 1), :].bitcast(I32),
-            )
         table_words.append(load_table(1))
-        nc.sync.dma_start(out=gain_rows[0:R_TILES, :], in_=gain.rearrange("(c p) -> c p", p=P))
+        nc.sync.dma_start(out=gain_rows[0:TURNED, :], in_=gain[0:PASS].rearrange("(c p) -> c p", p=P))
         w1_raw = [load_w1(0)]
         table_words.append(load_table(2))
-        wgs_tile = sbuf.tile([P, S], F32)
-        for lo in range(0, S, BANK):
-            nc.sync.dma_start(out=wgs_tile[:, lo : lo + BANK], in_=wgs[:, lo : lo + BANK])
+        wgs_tile = tile("wgs_tile", [P, S], F32)
+        nc.sync.dma_start(out=wgs_tile[:, 0:BANK], in_=wgs[:, 0:BANK])
+        idx2 = sbuf.tile([P, S // LIST_ROWS], U16)
+        nc.sync.dma_start(idx2[:], offs2)
+        nc.sync.dma_start(out=wgs_tile[:, BANK:S], in_=wgs[:, BANK:S])
         w1_raw.append(load_w1(1))
-        sess_tiles = []
-        wb_raw = []
-        for c in range(2, R_TILES):
-            w1_raw.append(load_w1(c))
-            sess_tiles.append(load_sess(c - 2))
-            if c in (3, 5):
-                wb_raw.append(load_wb(len(wb_raw)))
-        for c in range(R_TILES - 2, R_TILES):
+        idx3 = sbuf.tile([P, M // LIST_ROWS], U16)
+        nc.sync.dma_start(idx3[:], offs3)
+        w1_raw.append(load_w1(2))
+        sess_tiles = [load_sess(0)]
+        w1_raw.append(load_w1(3))
+        w1_wide = [load_wide(a) for a in range(K_PASSES)]
+        for c in range(1, TURNED):
             sess_tiles.append(load_sess(c))
-        wa_codes = sbuf.tile([P, R_PASSES, 2 * N], U8, align_bytes=ALIGN)
-        nc.sync.dma_start(out=wa_codes[:].bitcast(I32), in_=wa_words.rearrange("a p n -> p a n").bitcast(I32))
-        for q in range(P // QUADRANT):
-            nc.sync.dma_start(
-                out=wa_scale_tile[QUADRANT * q : QUADRANT * q + SCALE_ROWS, :, :].bitcast(I32),
-                in_=wa_scales[:, SCALE_ROWS * q : SCALE_ROWS * (q + 1), :].rearrange("a r n -> r a n").bitcast(I32),
-            )
 
         gain_turned = bank("score0", [P, P])
         nc.tensor.transpose(gain_turned[:], gain_rows[:], ident[:])
-        gain_col = sbuf.tile([P, R_TILES], F32)
-        nc.scalar.copy(out=gain_col[:], in_=gain_turned[:, 0:R_TILES])
+        gain_col = tile("gain_col", [P, TURNED], F32)
+        nc.scalar.copy(out=gain_col[:], in_=gain_turned[:, 0:TURNED])
 
-        v_words = [sbuf.tile([P, S], U32, name=f"v_words{a}", align_bytes=ALIGN) for a in range(K_PASSES)]
-        v_scales = sbuf.tile([P, S], U8, align_bytes=ALIGN)
+        v_scales = tile("v_scales", [P, S], U8)
         nc.vector.tensor_copy(v_scales[:], table_scales[:].indirect(idx[:]))
+        v_words = [tile(f"v_words{a}", [P, S], U32) for a in range(K_PASSES - 1)]
         for a in range(K_PASSES - 1):
             nc.vector.tensor_copy(v_words[a][:], table_words[a][:].indirect(idx[:]))
 
         w1_grouped = {}
         w1_codes = {}
         w1_scales = {}
+        w1_backs = tile("w1_backs", [P, PACK, PASS], BF16)
 
         def group_w1(c):
             previous_scales = f"w1_scales{(c - 1) % 2}"
             if c == 1:
-                whole = sbuf.tile([P, K_PASSES * PASS], BF16, name="w1_grouped1", tag=previous_scales, align_bytes=ALIGN)
+                whole = tile("w1_grouped1", [P, K_PASSES * PASS], BF16, tag=previous_scales)
                 front, back = whole[:, 0 : 2 * PASS], whole[:, 2 * PASS : 3 * PASS]
             else:
-                back_tag = "w1_raw0_2" if c == 2 else previous_scales
-                front = sbuf.tile([P, 2 * PASS], BF16, name=f"w1_front{c}", tag="w1_front", align_bytes=ALIGN)[:]
-                back = sbuf.tile([P, PASS], BF16, name=f"w1_back{c}", tag=back_tag, align_bytes=ALIGN)[:]
+                back_tag = {0: "v_last", 2: "w1_raw0_2", 3: previous_scales}[c]
+                front = tile(f"w1_front{c}", [P, 2 * PASS], BF16, tag="w1_front")[:]
+                back = tile(f"w1_back{c}", [P, PASS], BF16, tag=back_tag)[:]
             w1_grouped[c] = (front, back)
             for a, grouped in enumerate((front[:, 0:PASS], front[:, PASS : 2 * PASS], back)):
                 interleave(nc, grouped, w1_raw[c][a][:])
-            w1_codes[c] = sbuf.tile([P, K_PASSES * P], U32, name=f"w1_codes{c}", tag="w1_codes", align_bytes=ALIGN)
-            w1_scales[c] = sbuf.tile([P, K_PASSES * P], U8, name=f"w1_scales{c}", tag=f"w1_scales{c % 2}", align_bytes=ALIGN)
+
+        def deal(grouped, a, t0, count):
+            nc.scalar.copy(
+                out=grouped.rearrange("p t (q i) -> p q i t", i=PACK),
+                in_=w1_wide[a][:].rearrange("p i (q t) -> p q i t", t=PACK)[:, :, :, t0 : t0 + count],
+            )
+
+        def group_w1_dealt(c):
+            if c == TURNED:
+                fronts = tile(f"w1_fronts{c}", [P, 2, 2 * PASS], BF16)
+            else:
+                fronts = place(f"w1_fronts{c}", [P, 2, 2 * PASS], BF16, WIDE_START + 4 * S)
+            for a in range(2):
+                deal(fronts[:, :, a * PASS : (a + 1) * PASS], a, c - TURNED, 2)
+            if c == TURNED:
+                deal(w1_backs[:], K_PASSES - 1, 0, PACK)
+            for u in range(2):
+                w1_grouped[c + u] = (fronts[:, u, :], w1_backs[:, c - TURNED + u, :])
+
+        def make_w1_codes(c):
+            w1_codes[c] = tile(f"w1_codes{c}", [P, K_PASSES * P], U32, tag="w1_codes")
+            if c < TURNED:
+                scales = tile(f"w1_scales{c}", [P, K_PASSES * P], U8, tag=f"w1_scales{c % 2}")
+                w1_scales[c] = (scales[:, 0 : 2 * P], scales[:, 2 * P : 3 * P])
+            else:
+                front = tile(f"w1_scales{c}", [P, 2 * P], U8, tag=f"w1_scales{c % 2}")
+                back = place(f"w1_scales_back{c}", [P, P], U8, plane_start(c) - P)
+                w1_scales[c] = (front[:], back[:])
 
         def quantize_w1(c, part):
             lo, hi = ((0, 2 * P), (2 * P, 3 * P))[part]
             nc.vector.quantize_mx(
-                out=w1_codes[c][:, lo:hi].bitcast(FP8X4), scales=w1_scales[c][:, lo:hi], in_=w1_grouped[c][part]
+                out=w1_codes[c][:, lo:hi].bitcast(FP8X4), scales=w1_scales[c][part], in_=w1_grouped[c][part]
             )
 
         def multiply_w1(c, half):
@@ -176,7 +212,7 @@ def tile_list_session_slot_verdict_kernel(
                 nc.tensor.matmul_mx(
                     out=acc[:],
                     lhsT=w1_codes[c][:, a * P : (a + 1) * P].bitcast(FP8X4),
-                    lhsT_scale=w1_scales[c][:, a * P : (a + 1) * P],
+                    lhsT_scale=w1_scales[c][a // 2][:, a % 2 * P : (a % 2 + 1) * P],
                     rhs=v_words[a][:, cols].bitcast(FP8X4),
                     rhs_scale=v_scales[SCALE_ROWS * a : P, cols],
                     start=(a == 0),
@@ -188,24 +224,35 @@ def tile_list_session_slot_verdict_kernel(
             nc.scalar.activation(out=dst, in_=acc[:], func=ACT.Gelu_apprx_tanh)
 
         def features(c):
-            h = sbuf.tile([P, S], F32, name=f"h{c}", tag=f"h{c % 2}", align_bytes=ALIGN)
+            if c == TURNED - 1:
+                h = place(f"h{c}", [P, S], F32, WIDE_START)
+            else:
+                h = tile(f"h{c}", [P, S], F32, tag=f"h{c % 2}")
             for half in range(S // BANK):
                 gelu(h[:, half * BANK : (half + 1) * BANK], multiply_w1(c, half))
             return h
 
         def weigh(dst, c, lo, hi):
-            nc.scalar.activation(out=dst, in_=wgs_tile[:, lo:hi], func=ACT.Copy, scale=gain_col[:, c : c + 1])
+            if c < TURNED:
+                rows, gains = wgs_tile[:, lo:hi], gain_col[:, c : c + 1]
+            else:
+                rows, gains = wgs_dealt[c, lo][:], gain_dealt[:, c - TURNED : c - TURNED + 1]
+            nc.scalar.activation(out=dst, in_=rows, func=ACT.Copy, scale=gains)
 
         def scatter(h, wg, lo, hi):
             nc.vector.tensor_tensor(page[:].indirect(entries(idx2, lo, hi)), h, wg, ALU.mult)
 
-        def gather(x, lo, hi):
-            nc.vector.tensor_copy(x[:, lo:hi], page[:].indirect(entries(idx3, lo, hi)))
+        def gather(x, c, lo, hi):
+            picked = page[:].indirect(entries(idx3, lo, hi))
+            if c < TURNED:
+                nc.vector.tensor_copy(x[:, lo:hi], picked)
+            else:
+                nc.vector.tensor_tensor(x[:, lo:hi], picked, sess_tiles[c][:, lo:hi], ALU.add)
 
         zt_pairs = {}
-        z_grouped = {}
+        z_grouped = {(a, half): tile(f"z_grouped{a}_{half}", [P, PACK * M_HALF], BF16) for a in range(R_PASSES) for half in range(2)}
         z_codes = {}
-        z_scales = sbuf.tile([P, R_PASSES, M], U8, align_bytes=ALIGN)
+        z_scales = tile("z_scales", [P, R_PASSES, M], U8)
 
         def turn(zt, rows, half, opens):
             for t in range(2):
@@ -226,25 +273,29 @@ def tile_list_session_slot_verdict_kernel(
             return sums
 
         def close_and_round(c, zt, x, half):
-            a, sub = divmod(c, TILES_PER_PASS)
-            if sub == 0:
-                zt_pairs[a, half] = sbuf.tile([P, 2, 2, P, 2], BF16, name=f"zt_pairs{a}_{half}", tag=f"zt_pairs{half}")
+            if c == 0:
+                zt_pairs[half] = tile(f"zt_pairs{half}", [P, 2, 2, P, 2], BF16)
             turn(zt, x, half, False)
             quads = P // PACK
             nc.scalar.copy(
-                out=zt_pairs[a, half][:, :, :, quads * sub : quads * (sub + 1), :],
+                out=zt_pairs[half][:, :, :, quads * c : quads * (c + 1), :],
                 in_=zt[:].rearrange("p t (q u e) -> p t u q e", u=2, e=2),
             )
 
-        def group_z(a, half):
-            words = zt_pairs[a, half][:].rearrange("p t u q e -> p (t u q e)").bitcast(F32)
+        def group_z(half):
+            words = zt_pairs[half][:].rearrange("p t u q e -> p (t u q e)").bitcast(F32)
             turned = bank(f"sum{half}", [P, 4, P])
             for j in range(4):
                 nc.tensor.transpose(turned[:, j, :], words[:, j * P : (j + 1) * P], ident[:])
-            z_grouped[a, half] = sbuf.tile([P, PACK * M_HALF], BF16, name=f"z_grouped{a}_{half}", align_bytes=ALIGN)
             nc.scalar.copy(
-                out=z_grouped[a, half][:].bitcast(F32).rearrange("p (t m u) -> p t m u", t=2, u=2),
+                out=z_grouped[0, half][:].bitcast(F32).rearrange("p (t m u) -> p t m u", t=2, u=2),
                 in_=turned[:].rearrange("p (t u) m -> p t m u", u=2),
+            )
+
+        def place_z(c, z, half):
+            nc.scalar.copy(
+                out=z_grouped[1, half][:].rearrange("p (m t) -> p m t", t=PACK)[:, :, c - TURNED],
+                in_=z[:, half * M_HALF : (half + 1) * M_HALF],
             )
 
         def quantize_z(a, half):
@@ -253,13 +304,20 @@ def tile_list_session_slot_verdict_kernel(
                 out=z_codes[a][:, cols].bitcast(FP8X4), scales=z_scales[:, a, cols], in_=z_grouped[a, half][:]
             )
 
-        wb_pieces = [(a, lo, lo + WB_PIECE) for a in range(R_PASSES) for lo in range(0, N, WB_PIECE)]
         wb_grouped = {}
-        wb_scales = sbuf.tile([P, R_PASSES, N], U8, align_bytes=ALIGN)
+        wb_codes = {}
+        wb_scales = {}
 
-        def group_wb(a, lo, hi, tag):
-            wb_grouped[a, lo] = sbuf.tile([P, PACK * (hi - lo)], BF16, name=f"wb_grouped{a}_{lo}", tag=tag, align_bytes=ALIGN)
-            interleave(nc, wb_grouped[a, lo][:], wb_raw[a][:, :, lo:hi])
+        def group_wb(a, piece, offset):
+            wb_grouped[a, piece] = place(f"wb_grouped{a}_{piece}", [P, PACK * WB_PIECE], BF16, offset)
+            interleave(nc, wb_grouped[a, piece][:], wb_raw[a][:, :, piece * WB_PIECE : (piece + 1) * WB_PIECE])
+
+        def quantize_wb(a, piece):
+            nc.vector.quantize_mx(
+                out=wb_codes[a, piece].bitcast(FP8X4),
+                scales=wb_scales[a, piece],
+                in_=wb_grouped[a, piece][:],
+            )
 
         def multiply_z(acc, codes, scales, a):
             nc.tensor.matmul_mx(
@@ -277,28 +335,67 @@ def tile_list_session_slot_verdict_kernel(
             multiply_z(acc, codes, wa_scale_tile[:, a, n * P : (n + 1) * P], a)
 
         def multiply_wb(acc, n, a):
-            codes = wb_codes[:, a, n * P : (n + 1) * P].bitcast(FP8X4)
-            multiply_z(acc, codes, wb_scales[:, a, n * P : (n + 1) * P], a)
+            piece, sub = divmod(n, EARLY_WB)
+            codes = wb_codes[a, piece][:, sub * P : (sub + 1) * P].bitcast(FP8X4)
+            multiply_z(acc, codes, wb_scales[a, piece][:, sub * P : (sub + 1) * P], a)
 
         group_w1(0)
+        make_w1_codes(0)
         for part in range(2):
             quantize_w1(0, part)
+        v_words.append(tile("v_last", [P, S], U32))
         for lo in range(0, S, BANK):
             nc.vector.tensor_copy(
                 v_words[K_PASSES - 1][:, lo : lo + BANK],
                 table_words[K_PASSES - 1][:].indirect(entries(idx, lo, lo + BANK)),
             )
+
+        gain_dealt = tile("gain_dealt", [P, PACK], F32)
+        nc.sync.dma_start(out=gain_dealt[:], in_=gain[PASS:H].rearrange("(p t) -> p t", t=PACK))
+        wgs_dealt = {}
+
+        def load_dealt(c, lo, hi):
+            plane = place(f"wgs_dealt{c}_{lo}", [P, hi - lo], F32, plane_start(c) + 4 * lo)
+            rows = wgs.rearrange("(p t) j -> p t j", t=PACK)[:, c - TURNED, lo:hi]
+            for q in (0, 2, 1, 3):
+                nc.sync.dma_start(out=plane[QUADRANT * q : QUADRANT * (q + 1), :], in_=rows)
+            wgs_dealt[c, lo] = plane
+
+
+        def load_wb(a):
+            raw = tile(f"wb_raw{a}", [P, PACK, N], F32, tag=f"table_words{a}")
+            nc.sync.dma_start(out=raw[:], in_=wb[a * PASS : (a + 1) * PASS, :].rearrange("(p i) n -> p i n", i=PACK))
+            return raw
+
+        wb_raw = [load_wb(a) for a in range(R_PASSES)]
+        for c in range(TURNED, LAST - 1):
+            load_dealt(c, 0, S)
+            sess_tiles.append(load_sess(c))
+        wa_codes = tile("wa_codes", [P, R_PASSES, 2 * N], U8)
+        nc.sync.dma_start(out=wa_codes[:].bitcast(I32), in_=wa_words.rearrange("a p n -> p a n").bitcast(I32))
+        for q in range(P // QUADRANT):
+            nc.sync.dma_start(
+                out=wa_scale_tile[QUADRANT * q : QUADRANT * q + SCALE_ROWS, :, :].bitcast(I32),
+                in_=wa_scales[:, SCALE_ROWS * q : SCALE_ROWS * (q + 1), :].rearrange("a r n -> r a n").bitcast(I32),
+            )
+        load_dealt(LAST - 1, 0, S)
+        sess_tiles.append(load_sess(LAST - 1))
+        load_dealt(LAST, 0, LAST_CUT)
+        load_dealt(LAST, LAST_CUT, S)
+        sess_tiles.append(load_sess(LAST))
+
         first_sums = [multiply_w1(0, half) for half in range(S // BANK)]
-        wg = sbuf.tile([P, S], F32, name="wg0", tag="wg_even", align_bytes=ALIGN)
-        h_front = sbuf.tile([P, BANK], F32, tag="h0", align_bytes=ALIGN)
+        wg = tile("wg0", [P, S], F32, tag="wg_even")
+        h_front = tile("h_front", [P, BANK], F32, tag="h0")
         gelu(h_front[:], first_sums[0])
         for lo in range(0, S, BANK):
             weigh(wg[:, lo : lo + BANK], 0, lo, lo + BANK)
         scatter(h_front[:], wg[:, 0:BANK], 0, BANK)
         group_w1(1)
+        make_w1_codes(1)
         for part in range(2):
             quantize_w1(1, part)
-        h_back = sbuf.tile([P, BANK], F32, tag="w1_raw1_2", align_bytes=ALIGN)
+        h_back = tile("h_back", [P, BANK], F32, tag="w1_raw1_2")
         gelu(h_back[:], first_sums[1])
         scatter(h_back[:], wg[:, BANK:S], BANK, S)
 
@@ -306,70 +403,104 @@ def tile_list_session_slot_verdict_kernel(
             ahead = c + 2
             if c > 0:
                 scatter(h[:], wg[:], 0, S)
+            if ahead == TURNED:
+                group_w1_dealt(TURNED)
             h = features(c + 1)
-            if ahead <= LAST:
+            if ahead < TURNED:
                 group_w1(ahead)
             if c + 1 < LAST:
-                wg = sbuf.tile([P, S], F32, name=f"wg{c + 1}", tag=("wg_odd", "wg_even")[c % 2], align_bytes=ALIGN)
+                wg = tile(f"wg{c + 1}", [P, S], F32, tag=("wg_odd", "wg_even")[c % 2])
                 weigh(wg[:], c + 1, 0, S)
             else:
-                wg_front = sbuf.tile([P, LAST_CUT], F32, tag="wg_odd", align_bytes=ALIGN)
+                wg_front = tile("wg_front", [P, LAST_CUT], F32, tag="wg_odd")
                 weigh(wg_front[:], LAST, 0, LAST_CUT)
-                wg_back = sbuf.tile([P, S - LAST_CUT], F32, tag="wg_even", align_bytes=ALIGN)
-                weigh(wg_back[:], LAST, LAST_CUT, S)
             if ahead <= LAST:
+                make_w1_codes(ahead)
                 quantize_w1(ahead, 0)
-            x_tag = f"w1_raw{ahead}_{K_PASSES - 1}" if ahead <= LAST else f"w1_scales{LAST % 2}"
-            x = sbuf.tile([P, M], F32, name=f"x{c}", tag=x_tag, align_bytes=ALIGN)
-            sums = open_sums(c)
-            gather(x, 0, M)
+            else:
+                early = tile("wb_codes_early", [P, R_PASSES, WB_PIECE], U32, tag="w1_codes")
+                early_scales = [
+                    tile("wb_scales_early0", [P, WB_PIECE], U8),
+                    place("wb_scales_early1", [P, WB_PIECE], U8, plane_start(LAST) + 4 * M),
+                ]
+                for a in range(R_PASSES):
+                    wb_codes[a, 0] = early[:, a, :]
+                    wb_scales[a, 0] = early_scales[a][:]
+                quantize_wb(0, 0)
+            if ahead < TURNED:
+                x = tile(f"x{c}", [P, M], F32, tag=f"w1_raw{ahead}_{K_PASSES - 1}")
+            elif ahead == TURNED:
+                x = place(f"x{c}", [P, M], F32, WIDE_START + 4 * S)
+            else:
+                x = place(f"x{c}", [P, M], F32, plane_start(c + 1) - P)
+            if c < TURNED:
+                sums = open_sums(c)
+            gather(x, c, 0, M)
             if ahead <= LAST:
                 quantize_w1(ahead, 1)
+            else:
+                quantize_wb(1, 0)
             for half in range(2):
-                close_and_round(c, sums[half], x, half)
-            if c > 0:
-                group_wb(*wb_pieces[c - 1], x_tag)
-            if c == TILES_PER_PASS - 1:
+                if c < TURNED:
+                    close_and_round(c, sums[half], x, half)
+                else:
+                    place_z(c, x, half)
+            if ahead == TURNED:
+                group_w1_dealt(TURNED + 2)
+            if c == TURNED - 1:
                 for half in range(2):
-                    group_z(0, half)
+                    group_z(half)
+            if TURNED - 1 <= c < LAST - 1:
+                piece = c - TURNED + 1
+                group_wb(0, piece, plane_start(c + 1) - P + 4 * M)
+                group_wb(1, piece, plane_start(c + 1) - P)
 
-        sums = open_sums(LAST)
+        wg_back = tile("wg_back", [P, S - LAST_CUT], F32, tag=f"sess{LAST - 1}")
+        weigh(wg_back[:], LAST, LAST_CUT, S)
         scatter(h[:, 0:LAST_CUT], wg_front[:], 0, LAST_CUT)
-        z_codes[0] = sbuf.tile([P, M], U32, name="z_codes0", tag="wg_odd", align_bytes=ALIGN)
+        z_codes[0] = place("z_codes0", [P, M], U32, plane_start(LAST) - P)
         for half in range(2):
             quantize_z(0, half)
         scatter(h[:, LAST_CUT:S], wg_back[:], LAST_CUT, S)
         wa_banks = ("score0", "score1", "score2", "score3", "feat0", "feat1")
+        wb_banks = ("sum0", "sum1") + wa_banks
         wa_sums = []
+        wb_sums = []
         for n in range(N_TILES):
             wa_sums.append(bank(wa_banks[n], [P, M]))
             multiply_wa(wa_sums[n], n, 0)
-        x = sbuf.tile([P, M], F32, name=f"x{LAST}", tag="w1_raw0_0", align_bytes=ALIGN)
+        for n in range(EARLY_WB):
+            wb_sums.append(bank(wb_banks[n], [P, M]))
+            multiply_wb(wb_sums[n], n, 0)
+        late = place("wb_codes_late", [P, 2, R_PASSES, WB_PIECE], U32, plane_start(LAST) + 4 * LAST_CUT)
+        late_scales = tile("wb_scales_late", [P, 2, R_PASSES, WB_PIECE], U8)
+        for piece in (1, 2):
+            for a in range(R_PASSES):
+                wb_codes[a, piece] = late[:, piece - 1, a, :]
+                wb_scales[a, piece] = late_scales[:, piece - 1, a, :]
+        quantize_wb(0, 1)
+        x = tile(f"x{LAST}", [P, M], F32, tag="w1_raw0_0")
         for half in range(2):
-            gather(x, half * M_HALF, (half + 1) * M_HALF)
-        wb_codes = sbuf.tile([P, R_PASSES, N], U32, tag="wg_even", align_bytes=ALIGN)
-        for a, lo, hi in wb_pieces:
-            nc.vector.quantize_mx(
-                out=wb_codes[:, a, lo:hi].bitcast(FP8X4), scales=wb_scales[:, a, lo:hi], in_=wb_grouped[a, lo][:]
-            )
+            gather(x, LAST, half * M_HALF, (half + 1) * M_HALF)
+        z_codes[1] = tile("z_codes1", [P, M], U32)
+        quantize_wb(1, 1)
         for half in range(2):
-            close_and_round(LAST, sums[half], x, half)
-        z_codes[1] = sbuf.tile([P, M], U32, name="z_codes1", align_bytes=ALIGN)
-        for half in range(2):
-            group_z(1, half)
+            place_z(LAST, x, half)
             quantize_z(1, half)
+            quantize_wb(half, 2)
 
-        wb_banks = ("sum0", "sum1") + wa_banks
+        spare = [f"w1_raw{c}_{a}" for c in (1, 2, 3) for a in (0, 2)]
         for n in range(N_TILES):
             multiply_wa(wa_sums[n], n, 1)
-            ya = sbuf.tile([P, M], F32, name=f"ya{n}", tag=f"w1_raw{n + 2}_0", align_bytes=ALIGN)
+            ya = tile(f"ya{n}", [P, M], F32, tag=spare[n])
             nc.scalar.copy(out=ya[:], in_=wa_sums[n][:])
-            wb_sum = bank(wb_banks[n], [P, M])
-            for a in range(R_PASSES):
-                multiply_wb(wb_sum, n, a)
-            best = sbuf.tile([P, M], F32, name=f"best{n}", tag=f"sess{n}")
+            if n >= EARLY_WB:
+                wb_sums.append(bank(wb_banks[n], [P, M]))
+                multiply_wb(wb_sums[n], n, 0)
+            multiply_wb(wb_sums[n], n, 1)
+            best = tile(f"best{n}", [P, M], F32, tag=f"sess{n}")
             width = M_HALF if n == N_TILES - 1 else M
             for lo in range(0, M, width):
                 cols = slice(lo, lo + width)
-                nc.vector.tensor_tensor(best[:, cols], wb_sum[:, cols], ya[:, cols], ALU.max)
+                nc.vector.tensor_tensor(best[:, cols], wb_sums[n][:, cols], ya[:, cols], ALU.max)
                 nc.sync.dma_start(out=out[n * P : (n + 1) * P, cols], in_=best[:, cols])

@@ -138,9 +138,10 @@ def tile_list_session_slot_verdict_kernel(
         w1_raw.append(load_w1(2))
         sess_tiles = [load_sess(0)]
         w1_raw.append(load_w1(3))
-        w1_wide = [load_wide(a) for a in range(K_PASSES)]
-        for c in range(1, TURNED):
-            sess_tiles.append(load_sess(c))
+        sess_tiles.append(load_sess(1))
+        w1_wide = [load_wide(a) for a in range(K_PASSES - 1)]
+        sess_tiles.append(load_sess(2))
+        w1_wide.append(load_wide(K_PASSES - 1))
 
         gain_turned = bank("score0", [P, P])
         nc.tensor.transpose(gain_turned[:], gain_rows[:], ident[:])
@@ -156,7 +157,7 @@ def tile_list_session_slot_verdict_kernel(
         w1_grouped = {}
         w1_codes = {}
         w1_scales = {}
-        w1_backs = tile("w1_backs", [P, PACK, PASS], BF16)
+        w1_backs = []
 
         def group_w1(c):
             previous_scales = f"w1_scales{(c - 1) % 2}"
@@ -179,15 +180,16 @@ def tile_list_session_slot_verdict_kernel(
 
         def group_w1_dealt(c):
             if c == TURNED:
-                fronts = tile(f"w1_fronts{c}", [P, 2, 2 * PASS], BF16)
+                fronts = tile(f"w1_fronts{c}", [P, 2, 2 * PASS], BF16, tag="w1_front")
+                w1_backs.append(tile("w1_backs", [P, PACK, PASS], BF16, tag=f"w1_raw{TURNED - 1}_{K_PASSES - 1}"))
             else:
                 fronts = place(f"w1_fronts{c}", [P, 2, 2 * PASS], BF16, WIDE_START + 4 * S)
             for a in range(2):
                 deal(fronts[:, :, a * PASS : (a + 1) * PASS], a, c - TURNED, 2)
             if c == TURNED:
-                deal(w1_backs[:], K_PASSES - 1, 0, PACK)
+                deal(w1_backs[0][:], K_PASSES - 1, 0, PACK)
             for u in range(2):
-                w1_grouped[c + u] = (fronts[:, u, :], w1_backs[:, c - TURNED + u, :])
+                w1_grouped[c + u] = (fronts[:, u, :], w1_backs[0][:, c - TURNED + u, :])
 
         def make_w1_codes(c):
             w1_codes[c] = tile(f"w1_codes{c}", [P, K_PASSES * P], U32, tag="w1_codes")
@@ -243,39 +245,20 @@ def tile_list_session_slot_verdict_kernel(
             nc.vector.tensor_tensor(page[:].indirect(entries(idx2, lo, hi)), h, wg, ALU.mult)
 
         def gather(x, c, lo, hi):
-            picked = page[:].indirect(entries(idx3, lo, hi))
-            if c < TURNED:
-                nc.vector.tensor_copy(x[:, lo:hi], picked)
-            else:
-                nc.vector.tensor_tensor(x[:, lo:hi], picked, sess_tiles[c][:, lo:hi], ALU.add)
+            nc.vector.tensor_tensor(x[:, lo:hi], page[:].indirect(entries(idx3, lo, hi)), sess_tiles[c][:, lo:hi], ALU.add)
 
         zt_pairs = {}
         z_grouped = {(a, half): tile(f"z_grouped{a}_{half}", [P, PACK * M_HALF], BF16) for a in range(R_PASSES) for half in range(2)}
         z_codes = {}
         z_scales = tile("z_scales", [P, R_PASSES, M], U8)
 
-        def turn(zt, rows, half, opens):
-            for t in range(2):
-                m0 = half * M_HALF + t * P
-                nc.tensor.matmul(
-                    zt[:, t, :],
-                    rows[:, m0 : m0 + P],
-                    ident[:],
-                    start=(opens and t == 0),
-                    stop=(not opens and t == 1),
-                    is_transpose=True,
-                )
-
-        def open_sums(c):
-            sums = [bank(f"sum{half}", [P, 2, P]) for half in range(2)]
-            for half in range(2):
-                turn(sums[half], sess_tiles[c], half, True)
-            return sums
-
-        def close_and_round(c, zt, x, half):
+        def turn_and_round(c, x, half):
             if c == 0:
                 zt_pairs[half] = tile(f"zt_pairs{half}", [P, 2, 2, P, 2], BF16)
-            turn(zt, x, half, False)
+            zt = bank(f"sum{half}", [P, 2, P])
+            for t in range(2):
+                m0 = half * M_HALF + t * P
+                nc.tensor.transpose(zt[:, t, :], x[:, m0 : m0 + P], ident[:])
             quads = P // PACK
             nc.scalar.copy(
                 out=zt_pairs[half][:, :, :, quads * c : quads * (c + 1), :],
@@ -367,10 +350,13 @@ def tile_list_session_slot_verdict_kernel(
             nc.sync.dma_start(out=raw[:], in_=wb[a * PASS : (a + 1) * PASS, :].rearrange("(p i) n -> p i n", i=PACK))
             return raw
 
-        wb_raw = [load_wb(a) for a in range(R_PASSES)]
-        for c in range(TURNED, LAST - 1):
-            load_dealt(c, 0, S)
-            sess_tiles.append(load_sess(c))
+        wb_raw = []
+        for a in range(R_PASSES):
+            sess_tiles.append(load_sess(TURNED - 1 + a))
+            load_dealt(TURNED + a, 0, S)
+            wb_raw.append(load_wb(a))
+        sess_tiles.append(load_sess(LAST - 2))
+        load_dealt(LAST - 1, 0, S)
         wa_codes = tile("wa_codes", [P, R_PASSES, 2 * N], U8)
         nc.sync.dma_start(out=wa_codes[:].bitcast(I32), in_=wa_words.rearrange("a p n -> p a n").bitcast(I32))
         for q in range(P // QUADRANT):
@@ -378,11 +364,10 @@ def tile_list_session_slot_verdict_kernel(
                 out=wa_scale_tile[QUADRANT * q : QUADRANT * q + SCALE_ROWS, :, :].bitcast(I32),
                 in_=wa_scales[:, SCALE_ROWS * q : SCALE_ROWS * (q + 1), :].rearrange("a r n -> r a n").bitcast(I32),
             )
-        load_dealt(LAST - 1, 0, S)
-        sess_tiles.append(load_sess(LAST - 1))
+        for c in range(LAST - 1, R_TILES):
+            sess_tiles.append(load_sess(c))
         load_dealt(LAST, 0, LAST_CUT)
         load_dealt(LAST, LAST_CUT, S)
-        sess_tiles.append(load_sess(LAST))
 
         first_sums = [multiply_w1(0, half) for half in range(S // BANK)]
         wg = tile("wg0", [P, S], F32, tag="wg_even")
@@ -433,8 +418,6 @@ def tile_list_session_slot_verdict_kernel(
                 x = place(f"x{c}", [P, M], F32, WIDE_START + 4 * S)
             else:
                 x = place(f"x{c}", [P, M], F32, plane_start(c + 1) - P)
-            if c < TURNED:
-                sums = open_sums(c)
             gather(x, c, 0, M)
             if ahead <= LAST:
                 quantize_w1(ahead, 1)
@@ -442,7 +425,7 @@ def tile_list_session_slot_verdict_kernel(
                 quantize_wb(1, 0)
             for half in range(2):
                 if c < TURNED:
-                    close_and_round(c, sums[half], x, half)
+                    turn_and_round(c, x, half)
                 else:
                     place_z(c, x, half)
             if ahead == TURNED:

@@ -174,8 +174,8 @@ def tile_list_session_slot_verdict_kernel(
 
         def deal(grouped, a, t0, count):
             nc.scalar.copy(
-                out=grouped.rearrange("p t (q i) -> p q i t", i=PACK),
-                in_=w1_wide[a][:].rearrange("p i (q t) -> p q i t", t=PACK)[:, :, :, t0 : t0 + count],
+                out=grouped.rearrange("p t (q e i) -> p q i e t", e=2, i=PACK),
+                in_=w1_wide[a][:].rearrange("p i (q e t) -> p q i e t", e=2, t=PACK)[:, :, :, :, t0 : t0 + count],
             )
 
         def group_w1_dealt(c):

@@ -35,7 +35,8 @@ M_HALF = M // 2
 WB_PIECE = 256
 EARLY_WB = WB_PIECE // P
 LAST_CUT = 768
-WIDE_START = 5 * 4 * S
+PLANES_START = 2304
+LATE_START = PLANES_START + 6 * 4 * S
 
 
 def interleave(nc, grouped, raw):
@@ -64,8 +65,17 @@ def tile_list_session_slot_verdict_kernel(
         def place(name, shape, dtype, offset):
             return placed.tile(shape, dtype, name=name, tag=name, align_bytes=ALIGN, offset=offset)
 
-        def plane_start(c):
-            return P + 4 * S * (c - TURNED)
+        def plane(c):
+            return PLANES_START + 4 * S * (c - TURNED + 2)
+
+        z_dealt = tile("z_dealt", [P, PACK * M], F32)
+
+        def z_rows(c):
+            return z_dealt[:, (c - TURNED) * M : (c - TURNED + 1) * M]
+
+        def gain_of(c):
+            column = (c - TURNED - 1) % PACK * M
+            return z_dealt[:, column : column + 1]
 
         def bank(tag, shape):
             return psum.tile(shape, F32, name=tag, tag=tag)
@@ -97,23 +107,26 @@ def tile_list_session_slot_verdict_kernel(
             tiles = []
             for a in range(K_PASSES):
                 tag = "wg_odd" if (c, a) == (2, 1) else None
-                raw = tile(f"w1_raw{c}_{a}", [P, PACK, P], F32, tag=tag)
+                if (c, a) == (TURNED - 1, K_PASSES - 1):
+                    raw = place(f"w1_raw{c}_{a}", [P, PACK, P], F32, P)
+                else:
+                    raw = tile(f"w1_raw{c}_{a}", [P, PACK, P], F32, tag=tag)
                 rows = w1[a * PASS : (a + 1) * PASS, c * P : (c + 1) * P]
                 nc.sync.dma_start(out=raw[:], in_=rows.rearrange("(p i) c -> p i c", i=PACK))
                 tiles.append(raw)
             return tiles
 
         def load_wide(a):
-            if a < K_PASSES - 1:
-                wide = tile(f"w1_wide{a}", [P, PACK, PASS], F32)
-            else:
-                wide = place(f"w1_wide{a}", [P, PACK, PASS], F32, WIDE_START)
+            wide = tile(f"w1_wide{a}", [P, PACK, PASS], F32)
             rows = w1[a * PASS : (a + 1) * PASS, PASS:H]
             nc.sync.dma_start(out=wide[:], in_=rows.rearrange("(p i) c -> p i c", i=PACK))
             return wide
 
         def load_sess(c):
-            rows = tile(f"sess{c}", [P, M], F32)
+            if c == LAST - 1:
+                rows = place(f"sess{c}", [P, M], F32, LATE_START + 5 * 1024)
+            else:
+                rows = tile(f"sess{c}", [P, M], F32)
             if c < TURNED:
                 nc.sync.dma_start(out=rows[:], in_=sess[c * P : (c + 1) * P, :])
             else:
@@ -137,6 +150,8 @@ def tile_list_session_slot_verdict_kernel(
         nc.sync.dma_start(idx3[:], offs3)
         w1_raw.append(load_w1(2))
         sess_tiles = [load_sess(0)]
+        gain_dealt = tile("gain_dealt", [P, PACK], F32)
+        nc.sync.dma_start(out=gain_dealt[:], in_=gain[PASS:H].rearrange("(p t) -> p t", t=PACK))
         w1_raw.append(load_w1(3))
         sess_tiles.append(load_sess(1))
         w1_wide = [load_wide(a) for a in range(K_PASSES - 1)]
@@ -157,7 +172,6 @@ def tile_list_session_slot_verdict_kernel(
         w1_grouped = {}
         w1_codes = {}
         w1_scales = {}
-        w1_backs = []
 
         def group_w1(c):
             previous_scales = f"w1_scales{(c - 1) % 2}"
@@ -165,47 +179,45 @@ def tile_list_session_slot_verdict_kernel(
                 whole = tile("w1_grouped1", [P, K_PASSES * PASS], BF16, tag=previous_scales)
                 front, back = whole[:, 0 : 2 * PASS], whole[:, 2 * PASS : 3 * PASS]
             else:
-                back_tag = {0: "v_last", 2: "w1_raw0_2", 3: previous_scales}[c]
+                back_tag = {0: "v_last", 2: "w1_raw0_2", 3: "w1_raw0_1"}[c]
                 front = tile(f"w1_front{c}", [P, 2 * PASS], BF16, tag="w1_front")[:]
                 back = tile(f"w1_back{c}", [P, PASS], BF16, tag=back_tag)[:]
             w1_grouped[c] = (front, back)
             for a, grouped in enumerate((front[:, 0:PASS], front[:, PASS : 2 * PASS], back)):
                 interleave(nc, grouped, w1_raw[c][a][:])
 
-        def deal(grouped, a, t0, count):
+        def deal(c, a, grouped):
+            t0, count = c - TURNED, grouped.shape[1]
             nc.scalar.copy(
                 out=grouped.rearrange("p t (q e i) -> p q i e t", e=2, i=PACK),
                 in_=w1_wide[a][:].rearrange("p i (q e t) -> p q i e t", e=2, t=PACK)[:, :, :, :, t0 : t0 + count],
             )
-
-        def group_w1_dealt(c):
-            if c == TURNED:
-                fronts = tile(f"w1_fronts{c}", [P, 2, 2 * PASS], BF16, tag="w1_front")
-                w1_backs.append(tile("w1_backs", [P, PACK, PASS], BF16, tag=f"w1_raw{TURNED - 1}_{K_PASSES - 1}"))
-            else:
-                fronts = place(f"w1_fronts{c}", [P, 2, 2 * PASS], BF16, WIDE_START + 4 * S)
-            for a in range(2):
-                deal(fronts[:, :, a * PASS : (a + 1) * PASS], a, c - TURNED, 2)
-            if c == TURNED:
-                deal(w1_backs[0][:], K_PASSES - 1, 0, PACK)
-            for u in range(2):
-                w1_grouped[c + u] = (fronts[:, u, :], w1_backs[0][:, c - TURNED + u, :])
+            for u in range(count):
+                w1_grouped[c + u, a] = grouped[:, u, :]
 
         def make_w1_codes(c):
-            w1_codes[c] = tile(f"w1_codes{c}", [P, K_PASSES * P], U32, tag="w1_codes")
-            if c < TURNED:
+            w1_codes[c] = tile(f"w1_codes{c}", [P, K_PASSES * P], U32, tag="w1_codes_odd" if c in (5, 7) else "w1_codes")
+            if c < 2:
                 scales = tile(f"w1_scales{c}", [P, K_PASSES * P], U8, tag=f"w1_scales{c % 2}")
                 w1_scales[c] = (scales[:, 0 : 2 * P], scales[:, 2 * P : 3 * P])
+            elif c == 2:
+                front = tile(f"w1_scales{c}", [P, 2 * P], U8, tag="w1_scales0")
+                w1_scales[c] = (front[:], place(f"w1_scales_back{c}", [P, P], U8, 0)[:])
             else:
-                front = tile(f"w1_scales{c}", [P, 2 * P], U8, tag=f"w1_scales{c % 2}")
-                back = place(f"w1_scales_back{c}", [P, P], U8, plane_start(c) - P)
-                w1_scales[c] = (front[:], back[:])
+                scales = place(f"w1_scales{c}", [P, K_PASSES * P], U8, plane(c) - K_PASSES * P)
+                w1_scales[c] = (scales[:, 0 : 2 * P], scales[:, 2 * P : 3 * P])
 
         def quantize_w1(c, part):
-            lo, hi = ((0, 2 * P), (2 * P, 3 * P))[part]
-            nc.vector.quantize_mx(
-                out=w1_codes[c][:, lo:hi].bitcast(FP8X4), scales=w1_scales[c][part], in_=w1_grouped[c][part]
-            )
+            if c < TURNED:
+                pieces = [((0, 2 * P), (2 * P, 3 * P))[part] + (w1_scales[c][part], w1_grouped[c][part])]
+            else:
+                passes = (((2, 0), (1,)) if c == TURNED else ((0, 1), (2,)))[part]
+                pieces = [
+                    (a * P, (a + 1) * P, w1_scales[c][a // 2][:, a % 2 * P : (a % 2 + 1) * P], w1_grouped[c, a])
+                    for a in passes
+                ]
+            for lo, hi, scales, grouped in pieces:
+                nc.vector.quantize_mx(out=w1_codes[c][:, lo:hi].bitcast(FP8X4), scales=scales, in_=grouped)
 
         def multiply_w1(c, half):
             cols = slice(half * BANK, (half + 1) * BANK)
@@ -226,10 +238,7 @@ def tile_list_session_slot_verdict_kernel(
             nc.scalar.activation(out=dst, in_=acc[:], func=ACT.Gelu_apprx_tanh)
 
         def features(c):
-            if c == TURNED - 1:
-                h = place(f"h{c}", [P, S], F32, WIDE_START)
-            else:
-                h = tile(f"h{c}", [P, S], F32, tag=f"h{c % 2}")
+            h = tile(f"h{c}", [P, S], F32, tag=f"h{c % 2}")
             for half in range(S // BANK):
                 gelu(h[:, half * BANK : (half + 1) * BANK], multiply_w1(c, half))
             return h
@@ -238,7 +247,7 @@ def tile_list_session_slot_verdict_kernel(
             if c < TURNED:
                 rows, gains = wgs_tile[:, lo:hi], gain_col[:, c : c + 1]
             else:
-                rows, gains = wgs_dealt[c, lo][:], gain_dealt[:, c - TURNED : c - TURNED + 1]
+                rows, gains = wgs_dealt[c][:, lo:hi], gain_of(c)
             nc.scalar.activation(out=dst, in_=rows, func=ACT.Copy, scale=gains)
 
         def scatter(h, wg, lo, hi):
@@ -248,7 +257,7 @@ def tile_list_session_slot_verdict_kernel(
             nc.vector.tensor_tensor(x[:, lo:hi], page[:].indirect(entries(idx3, lo, hi)), sess_tiles[c][:, lo:hi], ALU.add)
 
         zt_pairs = {}
-        z_grouped = {(a, half): tile(f"z_grouped{a}_{half}", [P, PACK * M_HALF], BF16) for a in range(R_PASSES) for half in range(2)}
+        z_grouped = {(1, half): tile(f"z_grouped1_{half}", [P, PACK * M_HALF], BF16)[:] for half in range(2)}
         z_codes = {}
         z_scales = tile("z_scales", [P, R_PASSES, M], U8)
 
@@ -271,35 +280,36 @@ def tile_list_session_slot_verdict_kernel(
             for j in range(4):
                 nc.tensor.transpose(turned[:, j, :], words[:, j * P : (j + 1) * P], ident[:])
             nc.scalar.copy(
-                out=z_grouped[0, half][:].bitcast(F32).rearrange("p (t m u) -> p t m u", t=2, u=2),
+                out=z_grouped[0, half].bitcast(F32).rearrange("p (t m u) -> p t m u", t=2, u=2),
                 in_=turned[:].rearrange("p (t u) m -> p t m u", u=2),
             )
 
-        def place_z(c, z, half):
-            nc.scalar.copy(
-                out=z_grouped[1, half][:].rearrange("p (m t) -> p m t", t=PACK)[:, :, c - TURNED],
-                in_=z[:, half * M_HALF : (half + 1) * M_HALF],
+        def join_z(engine_copy, half):
+            rows = z_dealt[:].rearrange("p (t m) -> p t m", t=PACK)
+            engine_copy(
+                out=z_grouped[1, half].rearrange("p (c j i) -> p c i j", j=4, i=PACK),
+                in_=rows[:, :, half * M_HALF : (half + 1) * M_HALF].rearrange("p i (c j) -> p c i j", j=4),
             )
 
         def quantize_z(a, half):
             cols = slice(half * M_HALF, (half + 1) * M_HALF)
             nc.vector.quantize_mx(
-                out=z_codes[a][:, cols].bitcast(FP8X4), scales=z_scales[:, a, cols], in_=z_grouped[a, half][:]
+                out=z_codes[a][:, cols].bitcast(FP8X4), scales=z_scales[:, a, cols], in_=z_grouped[a, half]
             )
 
         wb_grouped = {}
         wb_codes = {}
         wb_scales = {}
 
-        def group_wb(a, piece, offset):
-            wb_grouped[a, piece] = place(f"wb_grouped{a}_{piece}", [P, PACK * WB_PIECE], BF16, offset)
-            interleave(nc, wb_grouped[a, piece][:], wb_raw[a][:, :, piece * WB_PIECE : (piece + 1) * WB_PIECE])
+        def group_wb(grouped, a, piece):
+            wb_grouped[a, piece] = grouped
+            interleave(nc, grouped, wb_raw[a][:, :, piece * WB_PIECE : (piece + 1) * WB_PIECE])
 
         def quantize_wb(a, piece):
             nc.vector.quantize_mx(
                 out=wb_codes[a, piece].bitcast(FP8X4),
                 scales=wb_scales[a, piece],
-                in_=wb_grouped[a, piece][:],
+                in_=wb_grouped[a, piece],
             )
 
         def multiply_z(acc, codes, scales, a):
@@ -307,7 +317,7 @@ def tile_list_session_slot_verdict_kernel(
                 out=acc[:],
                 lhsT=codes,
                 lhsT_scale=scales,
-                rhs=z_codes[a][:].bitcast(FP8X4),
+                rhs=z_codes[a].bitcast(FP8X4),
                 rhs_scale=z_scales[:, a, :],
                 start=(a == 0),
                 stop=(a == R_PASSES - 1),
@@ -333,17 +343,16 @@ def tile_list_session_slot_verdict_kernel(
                 table_words[K_PASSES - 1][:].indirect(entries(idx, lo, lo + BANK)),
             )
 
-        gain_dealt = tile("gain_dealt", [P, PACK], F32)
-        nc.sync.dma_start(out=gain_dealt[:], in_=gain[PASS:H].rearrange("(p t) -> p t", t=PACK))
+
+        for c in range(TURNED, R_TILES):
+            nc.scalar.copy(out=gain_of(c), in_=gain_dealt[:, c - TURNED : c - TURNED + 1])
         wgs_dealt = {}
 
-        def load_dealt(c, lo, hi):
-            plane = place(f"wgs_dealt{c}_{lo}", [P, hi - lo], F32, plane_start(c) + 4 * lo)
-            rows = wgs.rearrange("(p t) j -> p t j", t=PACK)[:, c - TURNED, lo:hi]
+        def load_dealt(c):
+            wgs_dealt[c] = place(f"wgs_dealt{c}", [P, S], F32, plane(c))
+            rows = wgs.rearrange("(p t) j -> p t j", t=PACK)[:, c - TURNED, :]
             for q in (0, 2, 1, 3):
-                nc.sync.dma_start(out=plane[QUADRANT * q : QUADRANT * (q + 1), :], in_=rows)
-            wgs_dealt[c, lo] = plane
-
+                nc.sync.dma_start(out=wgs_dealt[c][QUADRANT * q : QUADRANT * (q + 1), :], in_=rows)
 
         def load_wb(a):
             raw = tile(f"wb_raw{a}", [P, PACK, N], F32, tag=f"table_words{a}")
@@ -353,10 +362,10 @@ def tile_list_session_slot_verdict_kernel(
         wb_raw = []
         for a in range(R_PASSES):
             sess_tiles.append(load_sess(TURNED - 1 + a))
-            load_dealt(TURNED + a, 0, S)
+            load_dealt(TURNED + a)
             wb_raw.append(load_wb(a))
         sess_tiles.append(load_sess(LAST - 2))
-        load_dealt(LAST - 1, 0, S)
+        load_dealt(LAST - 1)
         wa_codes = tile("wa_codes", [P, R_PASSES, 2 * N], U8)
         nc.sync.dma_start(out=wa_codes[:].bitcast(I32), in_=wa_words.rearrange("a p n -> p a n").bitcast(I32))
         for q in range(P // QUADRANT):
@@ -366,8 +375,7 @@ def tile_list_session_slot_verdict_kernel(
             )
         for c in range(LAST - 1, R_TILES):
             sess_tiles.append(load_sess(c))
-        load_dealt(LAST, 0, LAST_CUT)
-        load_dealt(LAST, LAST_CUT, S)
+        load_dealt(LAST)
 
         first_sums = [multiply_w1(0, half) for half in range(S // BANK)]
         wg = tile("wg0", [P, S], F32, tag="wg_even")
@@ -388,63 +396,77 @@ def tile_list_session_slot_verdict_kernel(
             ahead = c + 2
             if c > 0:
                 scatter(h[:], wg[:], 0, S)
-            if ahead == TURNED:
-                group_w1_dealt(TURNED)
             h = features(c + 1)
             if ahead < TURNED:
                 group_w1(ahead)
-            if c + 1 < LAST:
+            if c + 1 < TURNED:
                 wg = tile(f"wg{c + 1}", [P, S], F32, tag=("wg_odd", "wg_even")[c % 2])
                 weigh(wg[:], c + 1, 0, S)
             else:
-                wg_front = tile("wg_front", [P, LAST_CUT], F32, tag="wg_odd")
-                weigh(wg_front[:], LAST, 0, LAST_CUT)
+                wg = wg_ahead
+            if c == 1:
+                deal(TURNED, 0, tile("w1_dealt4_0", [P, 2, PASS], BF16)[:])
+            if c == 2:
+                deal(TURNED, 1, tile("w1_dealt4_1", [P, 2, PASS], BF16, tag="w1_front")[:])
+                deal(TURNED, 2, place("w1_dealt4_2", [P, 1, PASS], BF16, 0)[:])
+            if TURNED <= ahead <= LAST:
+                wg_ahead = place(f"wg{ahead}", [P, S], F32, plane(ahead - 2))
+                weigh(wg_ahead[:], ahead, 0, S)
             if ahead <= LAST:
                 make_w1_codes(ahead)
                 quantize_w1(ahead, 0)
             else:
                 early = tile("wb_codes_early", [P, R_PASSES, WB_PIECE], U32, tag="w1_codes")
-                early_scales = [
-                    tile("wb_scales_early0", [P, WB_PIECE], U8),
-                    place("wb_scales_early1", [P, WB_PIECE], U8, plane_start(LAST) + 4 * M),
-                ]
+                early_scales = place("wb_scales_early", [P, R_PASSES, WB_PIECE], U8, plane(LAST))
                 for a in range(R_PASSES):
                     wb_codes[a, 0] = early[:, a, :]
-                    wb_scales[a, 0] = early_scales[a][:]
+                    wb_scales[a, 0] = early_scales[:, a, :]
                 quantize_wb(0, 0)
-            if ahead < TURNED:
-                x = tile(f"x{c}", [P, M], F32, tag=f"w1_raw{ahead}_{K_PASSES - 1}")
-            elif ahead == TURNED:
-                x = place(f"x{c}", [P, M], F32, WIDE_START + 4 * S)
+            if c == 0:
+                x = tile("x0", [P, M], F32, tag="w1_raw2_2")
+            elif c == 1:
+                x = place("x1", [P, M], F32, 0)
+            elif c == 2:
+                x = place("x2", [P, M], F32, 0)
+            elif c == 3:
+                x = place("x3", [P, M], F32, plane(TURNED))
             else:
-                x = place(f"x{c}", [P, M], F32, plane_start(c + 1) - P)
+                x = z_rows(c)
             gather(x, c, 0, M)
             if ahead <= LAST:
                 quantize_w1(ahead, 1)
             else:
                 quantize_wb(1, 0)
-            for half in range(2):
-                if c < TURNED:
-                    turn_and_round(c, x, half)
-                else:
-                    place_z(c, x, half)
-            if ahead == TURNED:
-                group_w1_dealt(TURNED + 2)
-            if c == TURNED - 1:
+            if c < TURNED:
                 for half in range(2):
+                    turn_and_round(c, x, half)
+            if c == 2:
+                deal(TURNED + 1, 2, tile("w1_dealt5_2", [P, 1, PASS], BF16, tag="sess2")[:])
+                deal(TURNED + 2, 0, place("w1_dealt6_0", [P, 2, PASS], BF16, 0)[:])
+            if c == 3:
+                dealt = tile("w1_dealt6_12", [P, 2, 2, PASS], BF16, tag="sess3")
+                for a in (1, 2):
+                    deal(TURNED + 2, a, dealt[:, a - 1, :, :])
+            if c == 4:
+                staged = tile("staged4", [P, 3, PACK * WB_PIECE], BF16, tag="sess4")
+                for half in range(2):
+                    z_grouped[0, half] = staged[:, half, :]
                     group_z(half)
-            if TURNED - 1 <= c < LAST - 1:
-                piece = c - TURNED + 1
-                group_wb(0, piece, plane_start(c + 1) - P + 4 * M)
-                group_wb(1, piece, plane_start(c + 1) - P)
+                group_wb(staged[:, 2, :], 0, 0)
+            if c == 5:
+                staged = tile("staged5", [P, 3, PACK * WB_PIECE], BF16, tag="sess5")
+                for u, (a, piece) in enumerate(((1, 0), (0, 1), (1, 1))):
+                    group_wb(staged[:, u, :], a, piece)
 
-        wg_back = tile("wg_back", [P, S - LAST_CUT], F32, tag=f"sess{LAST - 1}")
-        weigh(wg_back[:], LAST, LAST_CUT, S)
-        scatter(h[:, 0:LAST_CUT], wg_front[:], 0, LAST_CUT)
-        z_codes[0] = place("z_codes0", [P, M], U32, plane_start(LAST) - P)
+        staged = place("staged6", [P, 2, PACK * WB_PIECE], BF16, LATE_START + 6 * 1024)
+        for a in range(R_PASSES):
+            group_wb(staged[:, a, :], a, 2)
+        scatter(h[:, 0:LAST_CUT], wg[:, 0:LAST_CUT], 0, LAST_CUT)
+        codes = place("late_codes", [P, M + 4 * WB_PIECE], U32, LATE_START)
+        z_codes[0] = codes[:, 0:M]
         for half in range(2):
             quantize_z(0, half)
-        scatter(h[:, LAST_CUT:S], wg_back[:], LAST_CUT, S)
+        scatter(h[:, LAST_CUT:S], wg[:, LAST_CUT:S], LAST_CUT, S)
         wa_banks = ("score0", "score1", "score2", "score3", "feat0", "feat1")
         wb_banks = ("sum0", "sum1") + wa_banks
         wa_sums = []
@@ -455,24 +477,27 @@ def tile_list_session_slot_verdict_kernel(
         for n in range(EARLY_WB):
             wb_sums.append(bank(wb_banks[n], [P, M]))
             multiply_wb(wb_sums[n], n, 0)
-        late = place("wb_codes_late", [P, 2, R_PASSES, WB_PIECE], U32, plane_start(LAST) + 4 * LAST_CUT)
+        late = codes[:, M : M + 4 * WB_PIECE].rearrange("p (s a n) -> p s a n", s=2, a=R_PASSES)
         late_scales = tile("wb_scales_late", [P, 2, R_PASSES, WB_PIECE], U8)
         for piece in (1, 2):
             for a in range(R_PASSES):
                 wb_codes[a, piece] = late[:, piece - 1, a, :]
                 wb_scales[a, piece] = late_scales[:, piece - 1, a, :]
         quantize_wb(0, 1)
-        x = tile(f"x{LAST}", [P, M], F32, tag="w1_raw0_0")
+        x = z_rows(LAST)
         for half in range(2):
             gather(x, LAST, half * M_HALF, (half + 1) * M_HALF)
-        z_codes[1] = tile("z_codes1", [P, M], U32)
+        z_codes[1] = tile("z_codes1", [P, M], U32)[:]
         quantize_wb(1, 1)
+        join_z(nc.scalar.copy, 0)
+        join_z(nc.vector.tensor_copy, 1)
+        quantize_wb(0, 2)
         for half in range(2):
-            place_z(LAST, x, half)
             quantize_z(1, half)
-            quantize_wb(half, 2)
+        wb_codes[1, 2] = tile("wb_codes_last", [P, WB_PIECE], U32, tag="z_grouped1_1")[:]
+        quantize_wb(1, 2)
 
-        spare = [f"w1_raw{c}_{a}" for c in (1, 2, 3) for a in (0, 2)]
+        spare = ("w1_raw0_0", "w1_raw1_0", "w1_raw1_1", "w1_raw2_0", "w1_raw3_0", "w1_raw3_1")
         for n in range(N_TILES):
             multiply_wa(wa_sums[n], n, 1)
             ya = tile(f"ya{n}", [P, M], F32, tag=spare[n])
@@ -481,7 +506,7 @@ def tile_list_session_slot_verdict_kernel(
                 wb_sums.append(bank(wb_banks[n], [P, M]))
                 multiply_wb(wb_sums[n], n, 0)
             multiply_wb(wb_sums[n], n, 1)
-            best = tile(f"best{n}", [P, M], F32, tag=f"sess{n}")
+            best = tile(f"best{n}", [P, M], F32, tag=("sess0", "sess1", "w1_raw1_2", "w1_raw2_2", "wg_even", "h1")[n])
             width = M_HALF if n == N_TILES - 1 else M
             for lo in range(0, M, width):
                 cols = slice(lo, lo + width)

@@ -33,7 +33,7 @@ TURNED = PASS // P
 LAST = R_TILES - 1
 M_HALF = M // 2
 WB_PIECE = 256
-EARLY_WB = WB_PIECE // P
+EARLY = 4
 LAST_CUT = 768
 PLANES_START = 2304
 LATE_START = PLANES_START + 6 * 4 * S
@@ -284,11 +284,11 @@ def tile_list_session_slot_verdict_kernel(
                 in_=turned[:].rearrange("p (t u) m -> p t m u", u=2),
             )
 
-        def join_z(engine_copy, half):
-            rows = z_dealt[:].rearrange("p (t m) -> p t m", t=PACK)
-            engine_copy(
-                out=z_grouped[1, half].rearrange("p (c j i) -> p c i j", j=4, i=PACK),
-                in_=rows[:, :, half * M_HALF : (half + 1) * M_HALF].rearrange("p i (c j) -> p c i j", j=4),
+        def join_z(half, lo, hi):
+            rows = z_dealt[:].rearrange("p (t m) -> p m t", t=PACK)
+            nc.scalar.copy(
+                out=z_grouped[1, half].rearrange("p (m t) -> p m t", t=PACK)[:, :, lo:hi],
+                in_=rows[:, half * M_HALF : (half + 1) * M_HALF, lo:hi],
             )
 
         def quantize_z(a, half):
@@ -312,25 +312,25 @@ def tile_list_session_slot_verdict_kernel(
                 in_=wb_grouped[a, piece],
             )
 
-        def multiply_z(acc, codes, scales, a):
+        def multiply_z(acc, codes, scales, a, lo, hi):
             nc.tensor.matmul_mx(
-                out=acc[:],
+                out=acc[:, lo:hi],
                 lhsT=codes,
                 lhsT_scale=scales,
-                rhs=z_codes[a].bitcast(FP8X4),
-                rhs_scale=z_scales[:, a, :],
+                rhs=z_codes[a][:, lo:hi].bitcast(FP8X4),
+                rhs_scale=z_scales[:, a, lo:hi],
                 start=(a == 0),
-                stop=(a == R_PASSES - 1),
+                stop=(a == R_PASSES - 1 and hi == M),
             )
 
         def multiply_wa(acc, n, a):
             codes = wa_codes[:, a, 2 * n * P : 2 * (n + 1) * P].bitcast(FP4X4)
-            multiply_z(acc, codes, wa_scale_tile[:, a, n * P : (n + 1) * P], a)
+            multiply_z(acc, codes, wa_scale_tile[:, a, n * P : (n + 1) * P], a, 0, M)
 
-        def multiply_wb(acc, n, a):
-            piece, sub = divmod(n, EARLY_WB)
+        def multiply_wb(acc, n, a, lo, hi):
+            piece, sub = divmod(n, WB_PIECE // P)
             codes = wb_codes[a, piece][:, sub * P : (sub + 1) * P].bitcast(FP8X4)
-            multiply_z(acc, codes, wb_scales[a, piece][:, sub * P : (sub + 1) * P], a)
+            multiply_z(acc, codes, wb_scales[a, piece][:, sub * P : (sub + 1) * P], a, lo, hi)
 
         group_w1(0)
         make_w1_codes(0)
@@ -418,9 +418,9 @@ def tile_list_session_slot_verdict_kernel(
             else:
                 early = tile("wb_codes_early", [P, R_PASSES, WB_PIECE], U32, tag="w1_codes")
                 early_scales = place("wb_scales_early", [P, R_PASSES, WB_PIECE], U8, plane(LAST))
-                for a in range(R_PASSES):
-                    wb_codes[a, 0] = early[:, a, :]
-                    wb_scales[a, 0] = early_scales[:, a, :]
+                for piece in range(2):
+                    wb_codes[0, piece] = early[:, piece, :]
+                    wb_scales[0, piece] = early_scales[:, piece, :]
                 quantize_wb(0, 0)
             if c == 0:
                 x = tile("x0", [P, M], F32, tag="w1_raw2_2")
@@ -436,7 +436,7 @@ def tile_list_session_slot_verdict_kernel(
             if ahead <= LAST:
                 quantize_w1(ahead, 1)
             else:
-                quantize_wb(1, 0)
+                quantize_wb(0, 1)
             if c < TURNED:
                 for half in range(2):
                     turn_and_round(c, x, half)
@@ -455,57 +455,63 @@ def tile_list_session_slot_verdict_kernel(
                 group_wb(staged[:, 2, :], 0, 0)
             if c == 5:
                 staged = tile("staged5", [P, 3, PACK * WB_PIECE], BF16, tag="sess5")
-                for u, (a, piece) in enumerate(((1, 0), (0, 1), (1, 1))):
+                for u, (a, piece) in enumerate(((0, 1), (1, 0), (1, 1))):
                     group_wb(staged[:, u, :], a, piece)
 
         staged = place("staged6", [P, 2, PACK * WB_PIECE], BF16, LATE_START + 6 * 1024)
         for a in range(R_PASSES):
             group_wb(staged[:, a, :], a, 2)
+        for half in range(2):
+            join_z(half, 0, PACK - 1)
         scatter(h[:, 0:LAST_CUT], wg[:, 0:LAST_CUT], 0, LAST_CUT)
-        codes = place("late_codes", [P, M + 4 * WB_PIECE], U32, LATE_START)
+        codes = place("late_codes", [P, M + 3 * WB_PIECE], U32, LATE_START + 1024)
         z_codes[0] = codes[:, 0:M]
         for half in range(2):
             quantize_z(0, half)
         scatter(h[:, LAST_CUT:S], wg[:, LAST_CUT:S], LAST_CUT, S)
-        wa_banks = ("score0", "score1", "score2", "score3", "feat0", "feat1")
-        wb_banks = ("sum0", "sum1") + wa_banks
+        banks = ("score0", "score1", "score2", "score3", "sum0", "sum1", "feat0", "feat1")
         wa_sums = []
         wb_sums = []
-        for n in range(N_TILES):
-            wa_sums.append(bank(wa_banks[n], [P, M]))
+        for n in range(EARLY):
+            wa_sums.append(bank(banks[2 * n], [P, M]))
             multiply_wa(wa_sums[n], n, 0)
-        for n in range(EARLY_WB):
-            wb_sums.append(bank(wb_banks[n], [P, M]))
-            multiply_wb(wb_sums[n], n, 0)
-        late = codes[:, M : M + 4 * WB_PIECE].rearrange("p (s a n) -> p s a n", s=2, a=R_PASSES)
-        late_scales = tile("wb_scales_late", [P, 2, R_PASSES, WB_PIECE], U8)
-        for piece in (1, 2):
-            for a in range(R_PASSES):
-                wb_codes[a, piece] = late[:, piece - 1, a, :]
-                wb_scales[a, piece] = late_scales[:, piece - 1, a, :]
-        quantize_wb(0, 1)
+            wb_sums.append(bank(banks[2 * n + 1], [P, M]))
+            multiply_wb(wb_sums[n], n, 0, 0, M)
+        late_scales = tile("wb_scales_late", [P, 4, WB_PIECE], U8)
+        for u, key in enumerate(((1, 0), (1, 1), (0, 2), (1, 2))):
+            wb_scales[key] = late_scales[:, u, :]
+            if u < 3:
+                wb_codes[key] = codes[:, M + u * WB_PIECE : M + (u + 1) * WB_PIECE]
+        quantize_wb(1, 0)
         x = z_rows(LAST)
         for half in range(2):
             gather(x, LAST, half * M_HALF, (half + 1) * M_HALF)
         z_codes[1] = tile("z_codes1", [P, M], U32)[:]
         quantize_wb(1, 1)
-        join_z(nc.scalar.copy, 0)
-        join_z(nc.vector.tensor_copy, 1)
-        quantize_wb(0, 2)
         for half in range(2):
-            quantize_z(1, half)
+            join_z(half, PACK - 1, PACK)
+        quantize_z(1, 0)
+        for n in range(EARLY):
+            multiply_wb(wb_sums[n], n, 1, 0, M_HALF)
+        quantize_wb(0, 2)
+        quantize_z(1, 1)
         wb_codes[1, 2] = tile("wb_codes_last", [P, WB_PIECE], U32, tag="z_grouped1_1")[:]
         quantize_wb(1, 2)
 
         spare = ("w1_raw0_0", "w1_raw1_0", "w1_raw1_1", "w1_raw2_0", "w1_raw3_0", "w1_raw3_1")
         for n in range(N_TILES):
+            if n >= EARLY:
+                wa_sums.append(bank(banks[4 * (n - EARLY)], [P, M]))
+                multiply_wa(wa_sums[n], n, 0)
             multiply_wa(wa_sums[n], n, 1)
             ya = tile(f"ya{n}", [P, M], F32, tag=spare[n])
             nc.scalar.copy(out=ya[:], in_=wa_sums[n][:])
-            if n >= EARLY_WB:
-                wb_sums.append(bank(wb_banks[n], [P, M]))
-                multiply_wb(wb_sums[n], n, 0)
-            multiply_wb(wb_sums[n], n, 1)
+            if n >= EARLY:
+                wb_sums.append(bank(banks[4 * (n - EARLY) + 2], [P, M]))
+                for a in range(R_PASSES):
+                    multiply_wb(wb_sums[n], n, a, 0, M)
+            else:
+                multiply_wb(wb_sums[n], n, 1, M_HALF, M)
             best = tile(f"best{n}", [P, M], F32, tag=("sess0", "sess1", "w1_raw1_2", "w1_raw2_2", "wg_even", "h1")[n])
             width = M_HALF if n == N_TILES - 1 else M
             for lo in range(0, M, width):

@@ -142,16 +142,14 @@ def tile_list_session_slot_verdict_kernel(
         table_words.append(load_table(2))
         wgs_tile = tile("wgs_tile", [P, S], F32)
         nc.sync.dma_start(out=wgs_tile[:, 0:BANK], in_=wgs[:, 0:BANK])
+        nc.sync.dma_start(out=wgs_tile[:, BANK:S], in_=wgs[:, BANK:S])
         idx2 = sbuf.tile([P, S // LIST_ROWS], U16)
         nc.sync.dma_start(idx2[:], offs2)
-        nc.sync.dma_start(out=wgs_tile[:, BANK:S], in_=wgs[:, BANK:S])
         w1_raw.append(load_w1(1))
         idx3 = sbuf.tile([P, M // LIST_ROWS], U16)
         nc.sync.dma_start(idx3[:], offs3)
         w1_raw.append(load_w1(2))
         sess_tiles = [load_sess(0)]
-        gain_dealt = tile("gain_dealt", [P, PACK], F32)
-        nc.sync.dma_start(out=gain_dealt[:], in_=gain[PASS:H].rearrange("(p t) -> p t", t=PACK))
         w1_raw.append(load_w1(3))
         sess_tiles.append(load_sess(1))
         w1_wide = [load_wide(a) for a in range(K_PASSES - 1)]
@@ -180,7 +178,7 @@ def tile_list_session_slot_verdict_kernel(
                 front, back = whole[:, 0 : 2 * PASS], whole[:, 2 * PASS : 3 * PASS]
             else:
                 back_tag = {0: "v_last", 2: "w1_raw0_2", 3: "w1_raw0_1"}[c]
-                front = tile(f"w1_front{c}", [P, 2 * PASS], BF16, tag="w1_front")[:]
+                front = tile(f"w1_front{c}", [P, 2 * PASS], BF16, tag="w1_raw1_1" if c > 0 else None)[:]
                 back = tile(f"w1_back{c}", [P, PASS], BF16, tag=back_tag)[:]
             w1_grouped[c] = (front, back)
             for a, grouped in enumerate((front[:, 0:PASS], front[:, PASS : 2 * PASS], back)):
@@ -196,7 +194,7 @@ def tile_list_session_slot_verdict_kernel(
                 w1_grouped[c + u, a] = grouped[:, u, :]
 
         def make_w1_codes(c):
-            w1_codes[c] = tile(f"w1_codes{c}", [P, K_PASSES * P], U32, tag="w1_codes_odd" if c in (5, 7) else "w1_codes")
+            w1_codes[c] = tile(f"w1_codes{c}", [P, K_PASSES * P], U32, tag="w1_codes_odd" if c in (1, 5, 7) else "w1_codes")
             if c < 2:
                 scales = tile(f"w1_scales{c}", [P, K_PASSES * P], U8, tag=f"w1_scales{c % 2}")
                 w1_scales[c] = (scales[:, 0 : 2 * P], scales[:, 2 * P : 3 * P])
@@ -344,11 +342,12 @@ def tile_list_session_slot_verdict_kernel(
             )
 
 
-        for c in range(TURNED, R_TILES):
-            nc.scalar.copy(out=gain_of(c), in_=gain_dealt[:, c - TURNED : c - TURNED + 1])
         wgs_dealt = {}
 
         def load_dealt(c):
+            gains = gain[PASS:H].rearrange("(p t) -> p t", t=PACK)[:, c - TURNED : c - TURNED + 1]
+            with nc.allow_non_contiguous_dma(reason="one gain for each partition"):
+                nc.sync.dma_start(out=gain_of(c), in_=gains)
             wgs_dealt[c] = place(f"wgs_dealt{c}", [P, S], F32, plane(c))
             rows = wgs.rearrange("(p t) j -> p t j", t=PACK)[:, c - TURNED, :]
             for q in (0, 2, 1, 3):
@@ -407,7 +406,7 @@ def tile_list_session_slot_verdict_kernel(
             if c == 1:
                 deal(TURNED, 0, tile("w1_dealt4_0", [P, 2, PASS], BF16)[:])
             if c == 2:
-                deal(TURNED, 1, tile("w1_dealt4_1", [P, 2, PASS], BF16, tag="w1_front")[:])
+                deal(TURNED, 1, tile("w1_dealt4_1", [P, 2, PASS], BF16, tag="w1_raw1_1")[:])
                 deal(TURNED, 2, place("w1_dealt4_2", [P, 1, PASS], BF16, 0)[:])
             if TURNED <= ahead <= LAST:
                 wg_ahead = place(f"wg{ahead}", [P, S], F32, plane(ahead - 2))

@@ -37,6 +37,7 @@ EARLY = 4
 LAST_CUT = 768
 PLANES_START = 2304
 LATE_START = PLANES_START + 6 * 4 * S
+WORDS_START = LATE_START + 10 * 1024
 
 
 def interleave(nc, grouped, raw):
@@ -93,13 +94,14 @@ def tile_list_session_slot_verdict_kernel(
         nc.scalar.activation(out=warm[:], in_=ident[:, 0:1], func=ACT.Gelu_apprx_tanh)
         gain_rows = tile("gain_rows", [P, P], F32)
         nc.vector.memset(gain_rows[:], 0.0)
-        page = tile("page", [P, T2], F32)
-        nc.vector.memset(page[:], 0.0)
         wa_scale_tile = tile("wa_scale_tile", [P, R_PASSES, N], U8)
         nc.vector.memset(wa_scale_tile[:].rearrange("p a n -> p (a n)").bitcast(I32), 0)
 
         def load_table(a):
-            words = tile(f"table_words{a}", [P, T], U32)
+            if a == 1:
+                words = place(f"table_words{a}", [P, T], U32, WORDS_START)
+            else:
+                words = tile(f"table_words{a}", [P, T], U32)
             nc.sync.dma_start(out=words[:].bitcast(I32), in_=tab_words[a].rearrange("p t i -> p (t i)").bitcast(I32))
             return words
 
@@ -161,11 +163,13 @@ def tile_list_session_slot_verdict_kernel(
         gain_col = tile("gain_col", [P, TURNED], F32)
         nc.scalar.copy(out=gain_col[:], in_=gain_turned[:, 0:TURNED])
 
-        v_scales = tile("v_scales", [P, S], U8)
-        nc.vector.tensor_copy(v_scales[:], table_scales[:].indirect(idx[:]))
         v_words = [tile(f"v_words{a}", [P, S], U32) for a in range(K_PASSES - 1)]
         for a in range(K_PASSES - 1):
             nc.vector.tensor_copy(v_words[a][:], table_words[a][:].indirect(idx[:]))
+        page = tile("page", [P, T2], F32, tag="table_words0")
+        nc.vector.memset(page[:], 0.0)
+        v_scales = place("v_scales", [P, S], U8, WORDS_START + 4 * PACK * N)
+        nc.vector.tensor_copy(v_scales[:], table_scales[:].indirect(idx[:]))
 
         w1_grouped = {}
         w1_codes = {}
@@ -354,7 +358,10 @@ def tile_list_session_slot_verdict_kernel(
                 nc.sync.dma_start(out=wgs_dealt[c][QUADRANT * q : QUADRANT * (q + 1), :], in_=rows)
 
         def load_wb(a):
-            raw = tile(f"wb_raw{a}", [P, PACK, N], F32, tag=f"table_words{a}")
+            if a == 0:
+                raw = place(f"wb_raw{a}", [P, PACK, N], F32, WORDS_START)
+            else:
+                raw = tile(f"wb_raw{a}", [P, PACK, N], F32, tag=f"table_words{K_PASSES - 1}")
             nc.sync.dma_start(out=raw[:], in_=wb[a * PASS : (a + 1) * PASS, :].rearrange("(p i) n -> p i n", i=PACK))
             return raw
 

@@ -35,8 +35,11 @@ M_HALF = M // 2
 WB_PIECE = 256
 EARLY = 4
 LAST_CUT = 768
-PLANES_START = 2304
-LATE_START = PLANES_START + 6 * 4 * S
+PLANES = {4: 14592, 5: 22784, 6: 39168, 7: 47360}
+WEIGHTS = {4: 2304, 5: 6400, 6: 18688, 7: 26880}
+SCALES = {3: 6016, 4: 10112, 5: 18624, 6: 26816, 7: 42880}
+LATE_START = 51456
+M_QUARTER = M // 4
 WORDS_START = LATE_START + 10 * 1024
 
 
@@ -67,7 +70,10 @@ def tile_list_session_slot_verdict_kernel(
             return placed.tile(shape, dtype, name=name, tag=name, align_bytes=ALIGN, offset=offset)
 
         def plane(c):
-            return PLANES_START + 4 * S * (c - TURNED + 2)
+            return PLANES[c]
+
+        def behind_weighing(name, shape, c):
+            return place(name, shape, BF16, plane(c) + ALIGN - 2 * shape[1] * shape[2])
 
         z_dealt = tile("z_dealt", [P, PACK * M], F32)
 
@@ -206,7 +212,7 @@ def tile_list_session_slot_verdict_kernel(
                 front = tile(f"w1_scales{c}", [P, 2 * P], U8, tag="w1_scales0")
                 w1_scales[c] = (front[:], place(f"w1_scales_back{c}", [P, P], U8, 0)[:])
             else:
-                scales = place(f"w1_scales{c}", [P, K_PASSES * P], U8, plane(c) - K_PASSES * P)
+                scales = place(f"w1_scales{c}", [P, K_PASSES * P], U8, SCALES[c])
                 w1_scales[c] = (scales[:, 0 : 2 * P], scales[:, 2 * P : 3 * P])
 
         def quantize_w1(c, part):
@@ -286,11 +292,11 @@ def tile_list_session_slot_verdict_kernel(
                 in_=turned[:].rearrange("p (t u) m -> p t m u", u=2),
             )
 
-        def join_z(half, lo, hi):
-            rows = z_dealt[:].rearrange("p (t m) -> p m t", t=PACK)
+        def join_z(m0, m1, lo, hi):
+            half, first = divmod(m0, M_HALF)
             nc.scalar.copy(
-                out=z_grouped[1, half].rearrange("p (m t) -> p m t", t=PACK)[:, :, lo:hi],
-                in_=rows[:, half * M_HALF : (half + 1) * M_HALF, lo:hi],
+                out=z_grouped[1, half].rearrange("p (m t) -> p m t", t=PACK)[:, first : first + m1 - m0, lo:hi],
+                in_=z_dealt[:].rearrange("p (t m) -> p m t", t=PACK)[:, m0:m1, lo:hi],
             )
 
         def quantize_z(a, half):
@@ -416,14 +422,14 @@ def tile_list_session_slot_verdict_kernel(
                 deal(TURNED, 1, tile("w1_dealt4_1", [P, 2, PASS], BF16, tag="w1_raw1_1")[:])
                 deal(TURNED, 2, place("w1_dealt4_2", [P, 1, PASS], BF16, 0)[:])
             if TURNED <= ahead <= LAST:
-                wg_ahead = place(f"wg{ahead}", [P, S], F32, plane(ahead - 2))
+                wg_ahead = place(f"wg{ahead}", [P, S], F32, WEIGHTS[ahead])
                 weigh(wg_ahead[:], ahead, 0, S)
             if ahead <= LAST:
                 make_w1_codes(ahead)
                 quantize_w1(ahead, 0)
             else:
                 early = tile("wb_codes_early", [P, R_PASSES, WB_PIECE], U32, tag="w1_codes")
-                early_scales = place("wb_scales_early", [P, R_PASSES, WB_PIECE], U8, plane(LAST))
+                early_scales = place("wb_scales_early", [P, R_PASSES, WB_PIECE], U8, plane(LAST) + 1024)
                 for piece in range(2):
                     wb_codes[0, piece] = early[:, piece, :]
                     wb_scales[0, piece] = early_scales[:, piece, :]
@@ -435,7 +441,7 @@ def tile_list_session_slot_verdict_kernel(
             elif c == 2:
                 x = place("x2", [P, M], F32, 0)
             elif c == 3:
-                x = place("x3", [P, M], F32, plane(TURNED))
+                x = place("x3", [P, M], F32, plane(TURNED) + 1024)
             else:
                 x = z_rows(c)
             gather(x, c, 0, M)
@@ -448,27 +454,28 @@ def tile_list_session_slot_verdict_kernel(
                     turn_and_round(c, x, half)
             if c == 2:
                 deal(TURNED + 1, 2, tile("w1_dealt5_2", [P, 1, PASS], BF16, tag="sess2")[:])
-                deal(TURNED + 2, 0, place("w1_dealt6_0", [P, 2, PASS], BF16, 0)[:])
+                fronts = behind_weighing("w1_dealt6_01", [P, 4, PASS], 4)
+                for a in range(2):
+                    deal(TURNED + 2, a, fronts[:, 2 * a : 2 * a + 2, :])
             if c == 3:
-                dealt = tile("w1_dealt6_12", [P, 2, 2, PASS], BF16, tag="sess3")
-                for a in (1, 2):
-                    deal(TURNED + 2, a, dealt[:, a - 1, :, :])
+                deal(TURNED + 2, 2, tile("w1_dealt6_2", [P, 2, PASS], BF16, tag="sess3")[:])
             if c == 4:
-                staged = tile("staged4", [P, 3, PACK * WB_PIECE], BF16, tag="sess4")
+                staged = behind_weighing("staged4", [P, 4, PACK * WB_PIECE], 6)
+                for piece in range(2):
+                    group_wb(staged[:, piece, :], 0, piece)
                 for half in range(2):
-                    z_grouped[0, half] = staged[:, half, :]
+                    z_grouped[0, half] = staged[:, 2 + half, :]
                     group_z(half)
-                group_wb(staged[:, 2, :], 0, 0)
             if c == 5:
-                staged = tile("staged5", [P, 3, PACK * WB_PIECE], BF16, tag="sess5")
-                for u, (a, piece) in enumerate(((0, 1), (1, 0), (1, 1))):
-                    group_wb(staged[:, u, :], a, piece)
+                staged = behind_weighing("staged5", [P, 2, PACK * WB_PIECE], 7)
+                for piece in range(2):
+                    group_wb(staged[:, piece, :], 1, piece)
 
         staged = place("staged6", [P, 2, PACK * WB_PIECE], BF16, LATE_START + 6 * 1024)
         for a in range(R_PASSES):
             group_wb(staged[:, a, :], a, 2)
         for half in range(2):
-            join_z(half, 0, PACK - 1)
+            join_z(half * M_HALF, (half + 1) * M_HALF, 0, PACK - 1)
         scatter(h[:, 0:LAST_CUT], wg[:, 0:LAST_CUT], 0, LAST_CUT)
         codes = place("late_codes", [P, M + 3 * WB_PIECE], U32, LATE_START + 1024)
         z_codes[0] = codes[:, 0:M]
@@ -490,12 +497,12 @@ def tile_list_session_slot_verdict_kernel(
                 wb_codes[key] = codes[:, M + u * WB_PIECE : M + (u + 1) * WB_PIECE]
         quantize_wb(1, 0)
         x = z_rows(LAST)
-        for half in range(2):
-            gather(x, LAST, half * M_HALF, (half + 1) * M_HALF)
+        for lo in range(0, M, M_QUARTER):
+            gather(x, LAST, lo, lo + M_QUARTER)
         z_codes[1] = tile("z_codes1", [P, M], U32)[:]
         quantize_wb(1, 1)
-        for half in range(2):
-            join_z(half, PACK - 1, PACK)
+        for lo in range(0, M, M_QUARTER):
+            join_z(lo, lo + M_QUARTER, PACK - 1, PACK)
         quantize_z(1, 0)
         for n in range(EARLY):
             multiply_wb(wb_sums[n], n, 1, 0, M_HALF)
@@ -511,7 +518,9 @@ def tile_list_session_slot_verdict_kernel(
                 multiply_wa(wa_sums[n], n, 0)
             multiply_wa(wa_sums[n], n, 1)
             ya = tile(f"ya{n}", [P, M], F32, tag=spare[n])
-            nc.scalar.copy(out=ya[:], in_=wa_sums[n][:])
+            width = M_HALF if n in (0, N_TILES - 1) else M
+            for lo in range(0, M, width):
+                nc.scalar.copy(out=ya[:, lo : lo + width], in_=wa_sums[n][:, lo : lo + width])
             if n >= EARLY:
                 wb_sums.append(bank(banks[4 * (n - EARLY) + 2], [P, M]))
                 for a in range(R_PASSES):
@@ -519,7 +528,6 @@ def tile_list_session_slot_verdict_kernel(
             else:
                 multiply_wb(wb_sums[n], n, 1, M_HALF, M)
             best = tile(f"best{n}", [P, M], F32, tag=("sess0", "sess1", "w1_raw1_2", "w1_raw2_2", "wg_even", "h1")[n])
-            width = M_HALF if n == N_TILES - 1 else M
             for lo in range(0, M, width):
                 cols = slice(lo, lo + width)
                 nc.vector.tensor_tensor(best[:, cols], wb_sums[n][:, cols], ya[:, cols], ALU.max)

@@ -29,18 +29,30 @@ K_PASSES = K // PASS
 R_PASSES = H // PASS
 R_TILES = H // P
 N_TILES = N // P
-TURNED = PASS // P
+NATURAL = PASS // P
 LAST = R_TILES - 1
 M_HALF = M // 2
-WB_PIECE = 256
-EARLY = 4
-LAST_CUT = 768
-PLANES = {4: 14592, 5: 22784, 6: 39168, 7: 47360}
-WEIGHTS = {4: 2304, 5: 6400, 6: 18688, 7: 26880}
-SCALES = {3: 6016, 4: 10112, 5: 18624, 6: 26816, 7: 42880}
-LATE_START = 51456
 M_QUARTER = M // 4
-WORDS_START = LATE_START + 10 * 1024
+WB_PIECE = 256
+FIRST_CUT = 256
+LAST_CUT = 640
+
+KIB = 1024
+SIZES = (
+    ("table0", 16 * KIB), ("table1", 16 * KIB), ("table2", 16 * KIB), ("v01", 8 * KIB), ("v2", 4 * KIB),
+    ("grouped2", 3 * KIB - ALIGN), ("table_scales", 4 * KIB), ("scales2", 384), ("wg0", 4 * KIB),
+    ("h", 8 * KIB), ("raw0", 8 * KIB), ("raw1", 6 * KIB), ("raw2", 6 * KIB), ("raw3", 6 * KIB),
+    ("wide", 24 * KIB), ("wgs", 4 * KIB), ("plane4", 6 * KIB + ALIGN), ("plane5", 4 * KIB),
+    ("plane6", 4 * KIB + 512), ("plane7", 6 * KIB + 512), ("sess", 16 * KIB),
+    ("wa", 3 * KIB), ("wa_scales", 1536), ("codes0", 1536), ("codes1", 3 * KIB), ("scales1", 384),
+    ("before_codes2", 4 * KIB - ALIGN), ("codes2", 1536), ("after_codes2", 4 * KIB - ALIGN), ("codes3", 1536),
+    ("codes4", 4 * KIB), ("scales4", 384), ("codes5", 1536),
+    ("before_codes6", 2 * KIB - ALIGN), ("codes6", 1536), ("after_codes6", 2 * KIB - ALIGN),
+    ("codes7", 1536),
+    ("z_dealt", 8 * KIB), ("z_scales", KIB), ("z_codes_front", KIB), ("wb_scales", KIB),
+    ("ident", 512), ("gain_rows", 512), ("gain_col", ALIGN), ("warm", ALIGN),
+)
+AT = {name: sum(size for other, size in SIZES[:i]) for i, (name, width) in enumerate(SIZES)}
 
 
 def interleave(nc, grouped, raw):
@@ -59,186 +71,170 @@ def tile_list_session_slot_verdict_kernel(
 ):
     nc = tc.nc
     with ExitStack() as ctx:
-        sbuf = ctx.enter_context(tc.tile_pool(name="sbuf", bufs=1))
+        lists = ctx.enter_context(tc.tile_pool(name="lists", bufs=1))
         placed = ctx.enter_context(tc.tile_pool(name="placed", bufs=1))
         psum = ctx.enter_context(tc.psum_pool(name="psum", bufs=1))
-
-        def tile(name, shape, dtype, tag=None):
-            return sbuf.tile(shape, dtype, name=name, tag=tag or name, align_bytes=ALIGN)
 
         def place(name, shape, dtype, offset):
             return placed.tile(shape, dtype, name=name, tag=name, align_bytes=ALIGN, offset=offset)
 
-        def plane(c):
-            return PLANES[c]
+        def bank(b, width=BANK):
+            return psum.tile([P, width], F32, name=f"bank{b}", tag=f"bank{b}")
 
-        def behind_weighing(name, shape, c):
-            return place(name, shape, BF16, plane(c) + ALIGN - 2 * shape[1] * shape[2])
-
-        z_dealt = tile("z_dealt", [P, PACK * M], F32)
-
-        def z_rows(c):
-            return z_dealt[:, (c - TURNED) * M : (c - TURNED + 1) * M]
-
-        def gain_of(c):
-            column = (c - TURNED - 1) % PACK * M
-            return z_dealt[:, column : column + 1]
-
-        def bank(tag, shape):
-            return psum.tile(shape, F32, name=tag, tag=tag)
-
-        ident = tile("ident", [P, P], F32)
-        make_identity(nc, ident[:])
-        table_scales = tile("table_scales", [P, T], U8, tag="w1_scales0")
+        table_scales = place("table_scales", [P, T], U8, AT["table_scales"])
         nc.vector.memset(table_scales[:].bitcast(I32), 0)
         for q in range(P // QUADRANT):
             nc.gpsimd.dma_start(
                 out=table_scales[QUADRANT * q : QUADRANT * q + SCALE_ROWS * K_PASSES, :].bitcast(I32),
                 in_=tab_scales[:, SCALE_ROWS * q : SCALE_ROWS * (q + 1), :].bitcast(I32),
             )
-        warm = tile("warm", [P, 1], F32)
-        nc.scalar.activation(out=warm[:], in_=ident[:, 0:1], func=ACT.Gelu_apprx_tanh)
-        gain_rows = tile("gain_rows", [P, P], F32)
+        gain_rows = place("gain_rows", [P, P], F32, AT["gain_rows"])
         nc.vector.memset(gain_rows[:], 0.0)
-        wa_scale_tile = tile("wa_scale_tile", [P, R_PASSES, N], U8)
+        ident = place("ident", [P, P], F32, AT["ident"])
+        make_identity(nc, ident[:])
+        warm = place("warm", [P, 1], F32, AT["warm"])
+        nc.scalar.activation(out=warm[:], in_=ident[:, 0:1], func=ACT.Gelu_apprx_tanh)
+        wa_scale_tile = place("wa_scale_tile", [P, R_PASSES, N], U8, AT["wa_scales"])
         nc.vector.memset(wa_scale_tile[:].rearrange("p a n -> p (a n)").bitcast(I32), 0)
 
         def load_table(a):
-            if a == 1:
-                words = place(f"table_words{a}", [P, T], U32, WORDS_START)
-            else:
-                words = tile(f"table_words{a}", [P, T], U32)
+            words = place(f"table_words{a}", [P, T], U32, AT[f"table{a}"])
             nc.sync.dma_start(out=words[:].bitcast(I32), in_=tab_words[a].rearrange("p t i -> p (t i)").bitcast(I32))
             return words
 
         def load_w1(c):
             tiles = []
             for a in range(K_PASSES):
-                tag = "wg_odd" if (c, a) == (2, 1) else None
-                if (c, a) == (TURNED - 1, K_PASSES - 1):
-                    raw = place(f"w1_raw{c}_{a}", [P, PACK, P], F32, P)
-                else:
-                    raw = tile(f"w1_raw{c}_{a}", [P, PACK, P], F32, tag=tag)
+                raw = place(f"w1_raw{c}_{a}", [P, PACK, P], F32, AT[f"raw{c}"] + a * 2 * KIB)
                 rows = w1[a * PASS : (a + 1) * PASS, c * P : (c + 1) * P]
                 nc.sync.dma_start(out=raw[:], in_=rows.rearrange("(p i) c -> p i c", i=PACK))
                 tiles.append(raw)
             return tiles
 
         def load_wide(a):
-            wide = tile(f"w1_wide{a}", [P, PACK, PASS], F32)
+            wide = place(f"w1_wide{a}", [P, PACK, PASS], F32, AT["wide"] + a * 8 * KIB)
             rows = w1[a * PASS : (a + 1) * PASS, PASS:H]
             nc.sync.dma_start(out=wide[:], in_=rows.rearrange("(p i) c -> p i c", i=PACK))
             return wide
 
+        sess_tiles = {}
+
         def load_sess(c):
-            if c == LAST - 1:
-                rows = place(f"sess{c}", [P, M], F32, LATE_START + 5 * 1024)
+            sess_tiles[c] = place(f"sess{c}", [P, M], F32, AT["sess"] + c * 2 * KIB)
+            if c < NATURAL:
+                rows = sess[c * P : (c + 1) * P, :]
             else:
-                rows = tile(f"sess{c}", [P, M], F32)
-            if c < TURNED:
-                nc.sync.dma_start(out=rows[:], in_=sess[c * P : (c + 1) * P, :])
-            else:
-                nc.sync.dma_start(out=rows[:], in_=sess[PASS:H, :].rearrange("(p t) m -> p t m", t=PACK)[:, c - TURNED, :])
-            return rows
+                rows = sess[PASS:H, :].rearrange("(p t) m -> p t m", t=PACK)[:, c - NATURAL, :]
+            nc.sync.dma_start(out=sess_tiles[c][:], in_=rows)
 
         table_words = [load_table(0)]
-        idx = sbuf.tile([P, S // LIST_ROWS], U16)
+        idx = lists.tile([P, S // LIST_ROWS], U16)
         nc.sync.dma_start(idx[:], offs)
         table_words.append(load_table(1))
-        nc.sync.dma_start(out=gain_rows[0:TURNED, :], in_=gain[0:PASS].rearrange("(c p) -> c p", p=P))
+        nc.sync.dma_start(out=gain_rows[0:NATURAL, :], in_=gain[0:PASS].rearrange("(c p) -> c p", p=P))
         w1_raw = [load_w1(0)]
         table_words.append(load_table(2))
-        wgs_tile = tile("wgs_tile", [P, S], F32)
-        nc.sync.dma_start(out=wgs_tile[:, 0:BANK], in_=wgs[:, 0:BANK])
-        nc.sync.dma_start(out=wgs_tile[:, BANK:S], in_=wgs[:, BANK:S])
-        idx2 = sbuf.tile([P, S // LIST_ROWS], U16)
+        wgs_tile = place("wgs_tile", [P, S], F32, AT["wgs"])
+        for lo in range(0, S, BANK):
+            nc.sync.dma_start(out=wgs_tile[:, lo : lo + BANK], in_=wgs[:, lo : lo + BANK])
+        idx2 = lists.tile([P, S // LIST_ROWS], U16)
         nc.sync.dma_start(idx2[:], offs2)
         w1_raw.append(load_w1(1))
-        idx3 = sbuf.tile([P, M // LIST_ROWS], U16)
+        idx3 = lists.tile([P, M // LIST_ROWS], U16)
         nc.sync.dma_start(idx3[:], offs3)
         w1_raw.append(load_w1(2))
-        sess_tiles = [load_sess(0)]
+        load_sess(0)
         w1_raw.append(load_w1(3))
-        sess_tiles.append(load_sess(1))
-        w1_wide = [load_wide(a) for a in range(K_PASSES - 1)]
-        sess_tiles.append(load_sess(2))
-        w1_wide.append(load_wide(K_PASSES - 1))
+        load_sess(1)
+        w1_wide = {a: load_wide(a) for a in (1, 2)}
+        load_sess(2)
+        w1_wide[0] = load_wide(0)
+        load_sess(3)
 
-        gain_turned = bank("score0", [P, P])
+        gain_turned = bank(2, P)
         nc.tensor.transpose(gain_turned[:], gain_rows[:], ident[:])
-        gain_col = tile("gain_col", [P, TURNED], F32)
-        nc.scalar.copy(out=gain_col[:], in_=gain_turned[:, 0:TURNED])
+        gain_col = place("gain_col", [P, NATURAL], F32, AT["gain_col"])
+        nc.scalar.copy(out=gain_col[:], in_=gain_turned[:, 0:NATURAL])
 
-        v_words = [tile(f"v_words{a}", [P, S], U32) for a in range(K_PASSES - 1)]
-        for a in range(K_PASSES - 1):
-            nc.vector.tensor_copy(v_words[a][:], table_words[a][:].indirect(idx[:]))
-        page = tile("page", [P, T2], F32, tag="table_words0")
-        nc.vector.memset(page[:], 0.0)
-        v_scales = place("v_scales", [P, S], U8, WORDS_START + 4 * PACK * N)
+        v_words = [place(f"v_words{a}", [P, S], U32, AT["v01"] + a * 4 * KIB) for a in range(2)]
+        nc.vector.tensor_copy(v_words[0][:], table_words[0][:].indirect(idx[:]))
+        pages = [place(f"page{u}", [P, T2], F32, AT["table0"] + u * 8 * KIB) for u in range(2)]
+        for page in pages:
+            nc.vector.memset(page[:].bitcast(I32), 0)
+        z_dealt = place("z_dealt", [P, PACK * M], F32, AT["z_dealt"])
+        nc.vector.tensor_copy(v_words[1][:], table_words[1][:].indirect(idx[:]))
+        v_scales = place("v_scales", [P, S], U8, AT["table1"] + 12 * KIB)
         nc.vector.tensor_copy(v_scales[:], table_scales[:].indirect(idx[:]))
 
-        w1_grouped = {}
-        w1_codes = {}
-        w1_scales = {}
+        def z_rows(c):
+            return z_dealt[:, (c - NATURAL) * M : (c - NATURAL + 1) * M]
+
+        def gain_of(c):
+            column = (c - NATURAL - 1) % PACK * M
+            return z_dealt[:, column : column + 1]
+
+        fronts, backs, w1_codes, w1_scales = {}, {}, {}, {}
+        SCALES_AT = (AT["table_scales"], AT["scales1"], AT["scales2"], AT["raw1"], AT["scales4"],
+                     AT["plane4"], AT["plane5"], AT["plane6"])
+        WEIGHTS_AT = (AT["wg0"], AT["raw2"], AT["raw3"], AT["wide"] + 2 * KIB, AT["raw1"],
+                      AT["wide"] + 16 * KIB, AT["plane4"], AT["raw0"])
+        X_AT = (AT["raw2"] + 4 * KIB, AT["raw3"] + 4 * KIB, AT["wide"], AT["plane4"] + 4 * KIB)
+        PLANE_AT = {4: AT["plane4"] + ALIGN, 5: AT["plane5"], 6: AT["plane6"], 7: AT["plane7"]}
 
         def group_w1(c):
-            previous_scales = f"w1_scales{(c - 1) % 2}"
-            if c == 1:
-                whole = tile("w1_grouped1", [P, K_PASSES * PASS], BF16, tag=previous_scales)
-                front, back = whole[:, 0 : 2 * PASS], whole[:, 2 * PASS : 3 * PASS]
+            if c == 0:
+                fronts[c] = place("w1_front0", [P, 2 * PASS], BF16, AT["raw0"] + 6 * KIB)[:]
+                backs[c] = place("w1_back0", [P, PASS], BF16, AT["v2"])[:]
             else:
-                back_tag = {0: "v_last", 2: "w1_raw0_2", 3: "w1_raw0_1"}[c]
-                front = tile(f"w1_front{c}", [P, 2 * PASS], BF16, tag="w1_raw1_1" if c > 0 else None)[:]
-                back = tile(f"w1_back{c}", [P, PASS], BF16, tag=back_tag)[:]
-            w1_grouped[c] = (front, back)
-            for a, grouped in enumerate((front[:, 0:PASS], front[:, PASS : 2 * PASS], back)):
+                offset = (AT["table_scales"], AT["grouped2"], AT["codes1"])[c - 1]
+                whole = place(f"w1_grouped{c}", [P, K_PASSES * PASS], BF16, offset)
+                fronts[c], backs[c] = whole[:, 0 : 2 * PASS], whole[:, 2 * PASS : 3 * PASS]
+            for a, grouped in enumerate((fronts[c][:, 0:PASS], fronts[c][:, PASS : 2 * PASS], backs[c])):
                 interleave(nc, grouped, w1_raw[c][a][:])
 
-        def deal(c, a, grouped):
-            t0, count = c - TURNED, grouped.shape[1]
+        def deal(a, t0, grouped):
+            count = grouped.shape[1]
             nc.scalar.copy(
                 out=grouped.rearrange("p t (q e i) -> p q i e t", e=2, i=PACK),
                 in_=w1_wide[a][:].rearrange("p i (q e t) -> p q i e t", e=2, t=PACK)[:, :, :, :, t0 : t0 + count],
             )
-            for u in range(count):
-                w1_grouped[c + u, a] = grouped[:, u, :]
 
-        def make_w1_codes(c):
-            w1_codes[c] = tile(f"w1_codes{c}", [P, K_PASSES * P], U32, tag="w1_codes_odd" if c in (1, 5, 7) else "w1_codes")
-            if c < 2:
-                scales = tile(f"w1_scales{c}", [P, K_PASSES * P], U8, tag=f"w1_scales{c % 2}")
-                w1_scales[c] = (scales[:, 0 : 2 * P], scales[:, 2 * P : 3 * P])
-            elif c == 2:
-                front = tile(f"w1_scales{c}", [P, 2 * P], U8, tag="w1_scales0")
-                w1_scales[c] = (front[:], place(f"w1_scales_back{c}", [P, P], U8, 0)[:])
-            else:
-                scales = place(f"w1_scales{c}", [P, K_PASSES * P], U8, SCALES[c])
-                w1_scales[c] = (scales[:, 0 : 2 * P], scales[:, 2 * P : 3 * P])
+        def deal_fronts(c, offset):
+            pair = place(f"w1_fronts{c}", [P, 2, 2 * PASS], BF16, offset)
+            for a in (1, 2):
+                deal(a, c - NATURAL, pair[:, :, (a - 1) * PASS : a * PASS])
+            for u in range(2):
+                fronts[c + u] = pair[:, u, :]
+
+        def deal_backs(offset):
+            four = place("w1_backs", [P, PACK, PASS], BF16, offset)
+            deal(0, 0, four[:])
+            for t in range(PACK):
+                backs[NATURAL + t] = four[:, t, :]
+
+        def passes_of(c):
+            return (0, 1, 2) if c < NATURAL else (1, 2, 0)
 
         def quantize_w1(c, part):
-            if c < TURNED:
-                pieces = [((0, 2 * P), (2 * P, 3 * P))[part] + (w1_scales[c][part], w1_grouped[c][part])]
-            else:
-                passes = (((2, 0), (1,)) if c == TURNED else ((0, 1), (2,)))[part]
-                pieces = [
-                    (a * P, (a + 1) * P, w1_scales[c][a // 2][:, a % 2 * P : (a % 2 + 1) * P], w1_grouped[c, a])
-                    for a in passes
-                ]
-            for lo, hi, scales, grouped in pieces:
-                nc.vector.quantize_mx(out=w1_codes[c][:, lo:hi].bitcast(FP8X4), scales=scales, in_=grouped)
+            if part == 0:
+                w1_codes[c] = place(f"w1_codes{c}", [P, K_PASSES * P], U32, AT[f"codes{c}"])
+                w1_scales[c] = place(f"w1_scales{c}", [P, K_PASSES * P], U8, SCALES_AT[c])
+            cols = (slice(0, 2 * P), slice(2 * P, 3 * P))[part]
+            nc.vector.quantize_mx(
+                out=w1_codes[c][:, cols].bitcast(FP8X4), scales=w1_scales[c][:, cols], in_=(fronts, backs)[part][c]
+            )
 
-        def multiply_w1(c, half):
-            cols = slice(half * BANK, (half + 1) * BANK)
-            acc = bank(f"feat{half}", [P, BANK])
-            for a in range(K_PASSES):
+        def multiply_w1(c, b, lo, hi):
+            acc = bank(b, hi - lo)
+            for u, a in enumerate(passes_of(c)):
                 nc.tensor.matmul_mx(
                     out=acc[:],
-                    lhsT=w1_codes[c][:, a * P : (a + 1) * P].bitcast(FP8X4),
-                    lhsT_scale=w1_scales[c][a // 2][:, a % 2 * P : (a % 2 + 1) * P],
-                    rhs=v_words[a][:, cols].bitcast(FP8X4),
-                    rhs_scale=v_scales[SCALE_ROWS * a : P, cols],
-                    start=(a == 0),
-                    stop=(a == K_PASSES - 1),
+                    lhsT=w1_codes[c][:, u * P : (u + 1) * P].bitcast(FP8X4),
+                    lhsT_scale=w1_scales[c][:, u * P : (u + 1) * P],
+                    rhs=v_words[a][:, lo:hi].bitcast(FP8X4),
+                    rhs_scale=v_scales[SCALE_ROWS * a : P, lo:hi],
+                    start=(u == 0),
+                    stop=(u == K_PASSES - 1),
                 )
             return acc
 
@@ -246,289 +242,275 @@ def tile_list_session_slot_verdict_kernel(
             nc.scalar.activation(out=dst, in_=acc[:], func=ACT.Gelu_apprx_tanh)
 
         def features(c):
-            h = tile(f"h{c}", [P, S], F32, tag=f"h{c % 2}")
+            h = place(f"h{c}", [P, S], F32, AT["h"] + c % 2 * 4 * KIB if c < LAST else AT["raw0"] + 4 * KIB)
             for half in range(S // BANK):
-                gelu(h[:, half * BANK : (half + 1) * BANK], multiply_w1(c, half))
+                gelu(h[:, half * BANK : (half + 1) * BANK], multiply_w1(c, 6 + half, half * BANK, (half + 1) * BANK))
             return h
 
-        def weigh(dst, c, lo, hi):
-            if c < TURNED:
-                rows, gains = wgs_tile[:, lo:hi], gain_col[:, c : c + 1]
-            else:
-                rows, gains = wgs_dealt[c][:, lo:hi], gain_of(c)
-            nc.scalar.activation(out=dst, in_=rows, func=ACT.Copy, scale=gains)
+        wgs_dealt, weights = {}, {}
 
-        def scatter(h, wg, lo, hi):
-            nc.vector.tensor_tensor(page[:].indirect(entries(idx2, lo, hi)), h, wg, ALU.mult)
+        def weigh(c, step):
+            wg = place(f"wg{c}", [P, S], F32, WEIGHTS_AT[c])
+            rows, gains = (wgs_tile, gain_col[:, c : c + 1]) if c < NATURAL else (wgs_dealt[c], gain_of(c))
+            for lo in range(0, S, step):
+                nc.scalar.activation(out=wg[:, lo : lo + step], in_=rows[:, lo : lo + step], func=ACT.Copy, scale=gains)
+            return wg
+
+        def scatter(c, h, lo, hi):
+            nc.vector.tensor_tensor(pages[c % 2][:].indirect(entries(idx2, lo, hi)), h, weights[c][:, lo:hi], ALU.mult)
 
         def gather(x, c, lo, hi):
-            nc.vector.tensor_tensor(x[:, lo:hi], page[:].indirect(entries(idx3, lo, hi)), sess_tiles[c][:, lo:hi], ALU.add)
-
-        zt_pairs = {}
-        z_grouped = {(1, half): tile(f"z_grouped1_{half}", [P, PACK * M_HALF], BF16)[:] for half in range(2)}
-        z_codes = {}
-        z_scales = tile("z_scales", [P, R_PASSES, M], U8)
-
-        def turn_and_round(c, x, half):
-            if c == 0:
-                zt_pairs[half] = tile(f"zt_pairs{half}", [P, 2, 2, P, 2], BF16)
-            zt = bank(f"sum{half}", [P, 2, P])
-            for t in range(2):
-                m0 = half * M_HALF + t * P
-                nc.tensor.transpose(zt[:, t, :], x[:, m0 : m0 + P], ident[:])
-            quads = P // PACK
-            nc.scalar.copy(
-                out=zt_pairs[half][:, :, :, quads * c : quads * (c + 1), :],
-                in_=zt[:].rearrange("p t (q u e) -> p t u q e", u=2, e=2),
-            )
-
-        def group_z(half):
-            words = zt_pairs[half][:].rearrange("p t u q e -> p (t u q e)").bitcast(F32)
-            turned = bank(f"sum{half}", [P, 4, P])
-            for j in range(4):
-                nc.tensor.transpose(turned[:, j, :], words[:, j * P : (j + 1) * P], ident[:])
-            nc.scalar.copy(
-                out=z_grouped[0, half].bitcast(F32).rearrange("p (t m u) -> p t m u", t=2, u=2),
-                in_=turned[:].rearrange("p (t u) m -> p t m u", u=2),
-            )
-
-        def join_z(m0, m1, lo, hi):
-            half, first = divmod(m0, M_HALF)
-            nc.scalar.copy(
-                out=z_grouped[1, half].rearrange("p (m t) -> p m t", t=PACK)[:, first : first + m1 - m0, lo:hi],
-                in_=z_dealt[:].rearrange("p (t m) -> p m t", t=PACK)[:, m0:m1, lo:hi],
-            )
-
-        def quantize_z(a, half):
-            cols = slice(half * M_HALF, (half + 1) * M_HALF)
-            nc.vector.quantize_mx(
-                out=z_codes[a][:, cols].bitcast(FP8X4), scales=z_scales[:, a, cols], in_=z_grouped[a, half]
-            )
-
-        wb_grouped = {}
-        wb_codes = {}
-        wb_scales = {}
-
-        def group_wb(grouped, a, piece):
-            wb_grouped[a, piece] = grouped
-            interleave(nc, grouped, wb_raw[a][:, :, piece * WB_PIECE : (piece + 1) * WB_PIECE])
-
-        def quantize_wb(a, piece):
-            nc.vector.quantize_mx(
-                out=wb_codes[a, piece].bitcast(FP8X4),
-                scales=wb_scales[a, piece],
-                in_=wb_grouped[a, piece],
-            )
-
-        def multiply_z(acc, codes, scales, a, lo, hi):
-            nc.tensor.matmul_mx(
-                out=acc[:, lo:hi],
-                lhsT=codes,
-                lhsT_scale=scales,
-                rhs=z_codes[a][:, lo:hi].bitcast(FP8X4),
-                rhs_scale=z_scales[:, a, lo:hi],
-                start=(a == 0),
-                stop=(a == R_PASSES - 1 and hi == M),
-            )
-
-        def multiply_wa(acc, n, a):
-            codes = wa_codes[:, a, 2 * n * P : 2 * (n + 1) * P].bitcast(FP4X4)
-            multiply_z(acc, codes, wa_scale_tile[:, a, n * P : (n + 1) * P], a, 0, M)
-
-        def multiply_wb(acc, n, a, lo, hi):
-            piece, sub = divmod(n, WB_PIECE // P)
-            codes = wb_codes[a, piece][:, sub * P : (sub + 1) * P].bitcast(FP8X4)
-            multiply_z(acc, codes, wb_scales[a, piece][:, sub * P : (sub + 1) * P], a, lo, hi)
+            nc.vector.tensor_tensor(x[:, lo:hi], pages[c % 2][:].indirect(entries(idx3, lo, hi)), sess_tiles[c][:, lo:hi], ALU.add)
 
         group_w1(0)
-        make_w1_codes(0)
         for part in range(2):
             quantize_w1(0, part)
-        v_words.append(tile("v_last", [P, S], U32))
-        for lo in range(0, S, BANK):
-            nc.vector.tensor_copy(
-                v_words[K_PASSES - 1][:, lo : lo + BANK],
-                table_words[K_PASSES - 1][:].indirect(entries(idx, lo, lo + BANK)),
-            )
-
-
-        wgs_dealt = {}
+        v_words.append(place("v_words2", [P, S], U32, AT["v2"]))
+        cuts = (0, FIRST_CUT, BANK, S)
+        for lo, hi in zip(cuts, cuts[1:]):
+            nc.vector.tensor_copy(v_words[2][:, lo:hi], table_words[2][:].indirect(entries(idx, lo, hi)))
 
         def load_dealt(c):
-            gains = gain[PASS:H].rearrange("(p t) -> p t", t=PACK)[:, c - TURNED : c - TURNED + 1]
+            gains = gain[PASS:H].rearrange("(p t) -> p t", t=PACK)[:, c - NATURAL : c - NATURAL + 1]
             with nc.allow_non_contiguous_dma(reason="one gain for each partition"):
                 nc.sync.dma_start(out=gain_of(c), in_=gains)
-            wgs_dealt[c] = place(f"wgs_dealt{c}", [P, S], F32, plane(c))
-            rows = wgs.rearrange("(p t) j -> p t j", t=PACK)[:, c - TURNED, :]
+            wgs_dealt[c] = place(f"wgs_dealt{c}", [P, S], F32, PLANE_AT[c])
+            rows = wgs.rearrange("(p t) j -> p t j", t=PACK)[:, c - NATURAL, :]
             for q in (0, 2, 1, 3):
                 nc.sync.dma_start(out=wgs_dealt[c][QUADRANT * q : QUADRANT * (q + 1), :], in_=rows)
 
         def load_wb(a):
-            if a == 0:
-                raw = place(f"wb_raw{a}", [P, PACK, N], F32, WORDS_START)
-            else:
-                raw = tile(f"wb_raw{a}", [P, PACK, N], F32, tag=f"table_words{K_PASSES - 1}")
+            raw = place(f"wb_raw{a}", [P, PACK, N], F32, AT[f"table{a + 1}"])
             nc.sync.dma_start(out=raw[:], in_=wb[a * PASS : (a + 1) * PASS, :].rearrange("(p i) n -> p i n", i=PACK))
             return raw
 
-        wb_raw = []
-        for a in range(R_PASSES):
-            sess_tiles.append(load_sess(TURNED - 1 + a))
-            load_dealt(TURNED + a)
-            wb_raw.append(load_wb(a))
-        sess_tiles.append(load_sess(LAST - 2))
-        load_dealt(LAST - 1)
-        wa_codes = tile("wa_codes", [P, R_PASSES, 2 * N], U8)
+        load_dealt(4)
+        load_sess(4)
+        load_dealt(5)
+        wa_codes = place("wa_codes", [P, R_PASSES, 2 * N], U8, AT["wa"])
         nc.sync.dma_start(out=wa_codes[:].bitcast(I32), in_=wa_words.rearrange("a p n -> p a n").bitcast(I32))
         for q in range(P // QUADRANT):
             nc.sync.dma_start(
                 out=wa_scale_tile[QUADRANT * q : QUADRANT * q + SCALE_ROWS, :, :].bitcast(I32),
                 in_=wa_scales[:, SCALE_ROWS * q : SCALE_ROWS * (q + 1), :].rearrange("a r n -> r a n").bitcast(I32),
             )
-        for c in range(LAST - 1, R_TILES):
-            sess_tiles.append(load_sess(c))
-        load_dealt(LAST)
+        wb_raw = [load_wb(0)]
+        load_dealt(6)
+        load_sess(5)
+        wb_raw.append(load_wb(1))
+        load_dealt(7)
+        load_sess(6)
+        load_sess(7)
 
-        first_sums = [multiply_w1(0, half) for half in range(S // BANK)]
-        wg = tile("wg0", [P, S], F32, tag="wg_even")
-        h_front = tile("h_front", [P, BANK], F32, tag="h0")
-        gelu(h_front[:], first_sums[0])
-        for lo in range(0, S, BANK):
-            weigh(wg[:, lo : lo + BANK], 0, lo, lo + BANK)
-        scatter(h_front[:], wg[:, 0:BANK], 0, BANK)
+        first_sums = [multiply_w1(0, b, lo, hi) for b, lo, hi in zip((0, 1, 6), cuts, cuts[1:])]
+        weights[0] = weigh(0, BANK)
+        h_front = place("h_front", [P, BANK], F32, AT["h"])
+        for u in range(2):
+            lo, hi = cuts[u], cuts[u + 1]
+            gelu(h_front[:, lo:hi], first_sums[u])
+            scatter(0, h_front[:, lo:hi], lo, hi)
         group_w1(1)
-        make_w1_codes(1)
         for part in range(2):
             quantize_w1(1, part)
-        h_back = tile("h_back", [P, BANK], F32, tag="w1_raw1_2")
-        gelu(h_back[:], first_sums[1])
-        scatter(h_back[:], wg[:, BANK:S], BANK, S)
+        h_back = place("h_back", [P, BANK], F32, AT["raw1"] + 4 * KIB)
+        gelu(h_back[:], first_sums[2])
+        scatter(0, h_back[:], BANK, S)
+        group_w1(2)
+        weights[1] = weigh(1, S)
+
+        wb_grouped, wb_codes, wb_scales = {}, {}, {}
+
+        def group_wb(name, offset, keys):
+            staged = place(name, [P, len(keys), PACK * WB_PIECE], BF16, offset)
+            for u, (a, piece) in enumerate(keys):
+                wb_grouped[a, piece] = staged[:, u, :]
+                interleave(nc, staged[:, u, :], wb_raw[a][:, :, piece * WB_PIECE : (piece + 1) * WB_PIECE])
+
+        def quantize_wb(a, piece):
+            nc.vector.quantize_mx(
+                out=wb_codes[a, piece].bitcast(FP8X4), scales=wb_scales[a, piece], in_=wb_grouped[a, piece]
+            )
+
+        z_natural = place("z_natural", [P, PACK * M], F32, AT["raw0"])
+        z_first = {}
+
+        def deal_rows(c, x):
+            for t in range(PACK):
+                nc.sync.dma_start(
+                    out=z_natural[QUADRANT * c : QUADRANT * (c + 1), t * M : (t + 1) * M], in_=x[t:P:PACK, :]
+                )
 
         for c in range(LAST):
             ahead = c + 2
             if c > 0:
-                scatter(h[:], wg[:], 0, S)
+                scatter(c, h[:], 0, S)
             h = features(c + 1)
-            if ahead < TURNED:
-                group_w1(ahead)
-            if c + 1 < TURNED:
-                wg = tile(f"wg{c + 1}", [P, S], F32, tag=("wg_odd", "wg_even")[c % 2])
-                weigh(wg[:], c + 1, 0, S)
-            else:
-                wg = wg_ahead
+            if c == 0:
+                group_w1(3)
             if c == 1:
-                deal(TURNED, 0, tile("w1_dealt4_0", [P, 2, PASS], BF16)[:])
-            if c == 2:
-                deal(TURNED, 1, tile("w1_dealt4_1", [P, 2, PASS], BF16, tag="w1_raw1_1")[:])
-                deal(TURNED, 2, place("w1_dealt4_2", [P, 1, PASS], BF16, 0)[:])
-            if TURNED <= ahead <= LAST:
-                wg_ahead = place(f"wg{ahead}", [P, S], F32, WEIGHTS[ahead])
-                weigh(wg_ahead[:], ahead, 0, S)
+                deal_fronts(4, AT["before_codes2"])
+                deal_backs(AT["codes2"] + 1536 - ALIGN)
+            if c == 3:
+                deal_fronts(6, AT["codes4"])
+            if c == 5:
+                for half in range(2):
+                    offset = (AT["before_codes6"], AT["codes6"] + 1536 - ALIGN)[half]
+                    z_first[half] = place(f"z_first{half}", [P, PACK * M_HALF], BF16, offset)
+                    rows = z_natural[:].rearrange("p (t m) -> p t m", t=PACK)
+                    interleave(nc, z_first[half][:], rows[:, :, half * M_HALF : (half + 1) * M_HALF])
+                group_wb("staged10", AT["plane5"], ((1, 0),))
             if ahead <= LAST:
-                make_w1_codes(ahead)
+                weights[ahead] = weigh(ahead, S)
+            if c == 4:
+                group_wb("staged_early", AT["plane6"] + 448, ((0, 0), (0, 1)))
+            if c == 6:
+                group_wb("staged11", AT["plane7"] + 512, ((1, 1),))
+                group_wb("staged2", AT["plane7"] + 512 + 2 * KIB, ((0, 2), (1, 2)))
+            if ahead <= LAST:
                 quantize_w1(ahead, 0)
             else:
-                early = tile("wb_codes_early", [P, R_PASSES, WB_PIECE], U32, tag="w1_codes")
-                early_scales = place("wb_scales_early", [P, R_PASSES, WB_PIECE], U8, plane(LAST) + 1024)
+                early = place("wb_codes_early", [P, 2, WB_PIECE], U32, AT["codes4"])
+                early_scales = place("wb_scales_early", [P, 2, WB_PIECE], U8, AT["plane7"])
                 for piece in range(2):
                     wb_codes[0, piece] = early[:, piece, :]
                     wb_scales[0, piece] = early_scales[:, piece, :]
                 quantize_wb(0, 0)
-            if c == 0:
-                x = tile("x0", [P, M], F32, tag="w1_raw2_2")
-            elif c == 1:
-                x = place("x1", [P, M], F32, 0)
-            elif c == 2:
-                x = place("x2", [P, M], F32, 0)
-            elif c == 3:
-                x = place("x3", [P, M], F32, plane(TURNED) + 1024)
-            else:
-                x = z_rows(c)
+            x = place(f"x{c}", [P, M], F32, X_AT[c]) if c < NATURAL else z_rows(c)
             gather(x, c, 0, M)
             if ahead <= LAST:
                 quantize_w1(ahead, 1)
             else:
                 quantize_wb(0, 1)
-            if c < TURNED:
-                for half in range(2):
-                    turn_and_round(c, x, half)
-            if c == 2:
-                deal(TURNED + 1, 2, tile("w1_dealt5_2", [P, 1, PASS], BF16, tag="sess2")[:])
-                fronts = behind_weighing("w1_dealt6_01", [P, 4, PASS], 4)
-                for a in range(2):
-                    deal(TURNED + 2, a, fronts[:, 2 * a : 2 * a + 2, :])
-            if c == 3:
-                deal(TURNED + 2, 2, tile("w1_dealt6_2", [P, 2, PASS], BF16, tag="sess3")[:])
-            if c == 4:
-                staged = behind_weighing("staged4", [P, 4, PACK * WB_PIECE], 6)
-                for piece in range(2):
-                    group_wb(staged[:, piece, :], 0, piece)
-                for half in range(2):
-                    z_grouped[0, half] = staged[:, 2 + half, :]
-                    group_z(half)
-            if c == 5:
-                staged = behind_weighing("staged5", [P, 2, PACK * WB_PIECE], 7)
-                for piece in range(2):
-                    group_wb(staged[:, piece, :], 1, piece)
+            if c < NATURAL:
+                deal_rows(c, x)
 
-        staged = place("staged6", [P, 2, PACK * WB_PIECE], BF16, LATE_START + 6 * 1024)
-        for a in range(R_PASSES):
-            group_wb(staged[:, a, :], a, 2)
+        spans = ((0, M_QUARTER), (M_QUARTER, M_HALF), (M_HALF, M))
+        z_last = [place(f"z_last{u}", [P, PACK * (hi - lo)], BF16, AT["table2"] + 2 * PACK * lo) for u, (lo, hi) in enumerate(spans)]
+
+        def join_z(m0, m1, t0, t1):
+            u = min(m0 // M_QUARTER, 2)
+            first = m0 - spans[u][0]
+            nc.scalar.copy(
+                out=z_last[u][:].rearrange("p (m t) -> p m t", t=PACK)[:, first : first + m1 - m0, t0:t1],
+                in_=z_dealt[:].rearrange("p (t m) -> p m t", t=PACK)[:, m0:m1, t0:t1],
+            )
+
+        for lo, hi in spans:
+            join_z(lo, hi, 0, PACK - 1)
+        scatter(LAST, h[:, 0:LAST_CUT], 0, LAST_CUT)
+        codes_first = place("z_codes_first", [P, M], U32, AT["sess"] + 6 * 2 * KIB)
+        scales_first = place("z_scales_first", [P, M], U8, AT["z_scales"])
         for half in range(2):
-            join_z(half * M_HALF, (half + 1) * M_HALF, 0, PACK - 1)
-        scatter(h[:, 0:LAST_CUT], wg[:, 0:LAST_CUT], 0, LAST_CUT)
-        codes = place("late_codes", [P, M + 3 * WB_PIECE], U32, LATE_START + 1024)
-        z_codes[0] = codes[:, 0:M]
+            cols = slice(half * M_HALF, (half + 1) * M_HALF)
+            nc.vector.quantize_mx(out=codes_first[:, cols].bitcast(FP8X4), scales=scales_first[:, cols], in_=z_first[half][:])
+        scatter(LAST, h[:, LAST_CUT:S], LAST_CUT, S)
+
+        z_half = {}
+
+        def z_operand(a, lo, hi):
+            if a == 0:
+                return codes_first[:, lo:hi], scales_first[:, lo:hi]
+            half, first = divmod(lo, M_HALF)
+            codes, scales = z_half[half]
+            return codes[:, first : first + hi - lo], scales[:, first : first + hi - lo]
+
+        def multiply(acc, which, n, a, lo, hi, start, stop):
+            if which == 0:
+                codes = wa_codes[:, a, 2 * n * P : 2 * (n + 1) * P].bitcast(FP4X4)
+                scales = wa_scale_tile[:, a, n * P : (n + 1) * P]
+            else:
+                piece, sub = divmod(n, WB_PIECE // P)
+                codes = wb_codes[a, piece][:, sub * P : (sub + 1) * P].bitcast(FP8X4)
+                scales = wb_scales[a, piece][:, sub * P : (sub + 1) * P]
+            moving, moving_scales = z_operand(a, lo, hi)
+            nc.tensor.matmul_mx(
+                out=acc, lhsT=codes, lhsT_scale=scales, rhs=moving.bitcast(FP8X4), rhs_scale=moving_scales,
+                start=start, stop=stop,
+            )
+
+        paired = {(half, which): bank(2 * half + which) for half in range(2) for which in range(2)}
+        whole = {(n, which): bank(2 * n + which) for n in (2, 3) for which in range(2)}
         for half in range(2):
-            quantize_z(0, half)
-        scatter(h[:, LAST_CUT:S], wg[:, LAST_CUT:S], LAST_CUT, S)
-        banks = ("score0", "score1", "score2", "score3", "sum0", "sum1", "feat0", "feat1")
-        wa_sums = []
-        wb_sums = []
-        for n in range(EARLY):
-            wa_sums.append(bank(banks[2 * n], [P, M]))
-            multiply_wa(wa_sums[n], n, 0)
-            wb_sums.append(bank(banks[2 * n + 1], [P, M]))
-            multiply_wb(wb_sums[n], n, 0, 0, M)
-        late_scales = tile("wb_scales_late", [P, 4, WB_PIECE], U8)
-        for u, key in enumerate(((1, 0), (1, 1), (0, 2), (1, 2))):
-            wb_scales[key] = late_scales[:, u, :]
-            if u < 3:
-                wb_codes[key] = codes[:, M + u * WB_PIECE : M + (u + 1) * WB_PIECE]
-        quantize_wb(1, 0)
+            for which in range(2):
+                for n in range(2):
+                    acc = paired[half, which][:, n * M_HALF : (n + 1) * M_HALF]
+                    multiply(acc, which, n, 0, half * M_HALF, (half + 1) * M_HALF, n == 0, False)
+        for n in (2, 3):
+            for which in range(2):
+                multiply(whole[n, which][:], which, n, 0, 0, M, True, False)
+
+        late_scales = place("wb_scales_late", [P, 4, WB_PIECE], U8, AT["wb_scales"])
+        late_at = {(1, 0): AT["before_codes6"], (1, 1): AT["table2"], (0, 2): AT["table2"] + KIB,
+                   (1, 2): AT["plane7"] + 512 + KIB}
+
+        def quantize_late(key):
+            wb_scales[key] = late_scales[:, list(late_at).index(key), :]
+            wb_codes[key] = place(f"wb_codes{key[0]}{key[1]}", [P, WB_PIECE], U32, late_at[key])[:]
+            quantize_wb(*key)
+
+        quantize_late((1, 0))
         x = z_rows(LAST)
         for lo in range(0, M, M_QUARTER):
             gather(x, LAST, lo, lo + M_QUARTER)
-        z_codes[1] = tile("z_codes1", [P, M], U32)[:]
-        quantize_wb(1, 1)
-        for lo in range(0, M, M_QUARTER):
             join_z(lo, lo + M_QUARTER, PACK - 1, PACK)
-        quantize_z(1, 0)
-        for n in range(EARLY):
-            multiply_wb(wb_sums[n], n, 1, 0, M_HALF)
-        quantize_wb(0, 2)
-        quantize_z(1, 1)
-        wb_codes[1, 2] = tile("wb_codes_last", [P, WB_PIECE], U32, tag="z_grouped1_1")[:]
-        quantize_wb(1, 2)
+        z_half[0] = (place("z_codes_front", [P, M_HALF], U32, AT["z_codes_front"]),
+                     place("z_scales_front", [P, M_HALF], U8, AT["z_scales"] + M))
+        for u in range(2):
+            lo, hi = spans[u]
+            nc.vector.quantize_mx(out=z_half[0][0][:, lo:hi].bitcast(FP8X4), scales=z_half[0][1][:, lo:hi], in_=z_last[u][:])
+            for which in range(2):
+                for n in range(2):
+                    acc = paired[0, which][:, n * M_HALF + lo : n * M_HALF + hi]
+                    multiply(acc, which, n, 1, lo, hi, False, u == 1 and n == 1)
+        quantize_late((1, 1))
+        for which in range(2):
+            for n in (2, 3):
+                multiply(whole[n, which][:, 0:M_HALF], which, n, 1, 0, M_HALF, False, False)
+        quantize_late((0, 2))
+        z_half[1] = (place("z_codes_back", [P, M_HALF], U32, AT["plane7"] + 512),
+                     place("z_scales_back", [P, M_HALF], U8, AT["z_scales"] + M + M_HALF))
+        nc.vector.quantize_mx(out=z_half[1][0][:].bitcast(FP8X4), scales=z_half[1][1][:], in_=z_last[2][:])
+        quantize_late((1, 2))
 
-        spare = ("w1_raw0_0", "w1_raw1_0", "w1_raw1_1", "w1_raw2_0", "w1_raw3_0", "w1_raw3_1")
-        for n in range(N_TILES):
-            if n >= EARLY:
-                wa_sums.append(bank(banks[4 * (n - EARLY)], [P, M]))
-                multiply_wa(wa_sums[n], n, 0)
-            multiply_wa(wa_sums[n], n, 1)
-            ya = tile(f"ya{n}", [P, M], F32, tag=spare[n])
-            width = M_HALF if n in (0, N_TILES - 1) else M
-            for lo in range(0, M, width):
-                nc.scalar.copy(out=ya[:, lo : lo + width], in_=wa_sums[n][:, lo : lo + width])
-            if n >= EARLY:
-                wb_sums.append(bank(banks[4 * (n - EARLY) + 2], [P, M]))
-                for a in range(R_PASSES):
-                    multiply_wb(wb_sums[n], n, a, 0, M)
+        done = []
+
+        def finish(sum_a, sum_b, rows):
+            width = sum_a.shape[1]
+            ya = place(f"ya{len(done)}", [P, width], F32, AT["v01"] + sum(done) * 4)
+            best = place(f"best{len(done)}", [P, width], F32, AT["wide"] + sum(done) * 4)
+            done.append(width)
+            nc.scalar.copy(out=ya[:], in_=sum_a)
+            nc.vector.tensor_tensor(best[:], sum_b, ya[:], ALU.max)
+            if len(rows.shape) == 3:
+                nc.sync.dma_start(out=rows, in_=best[:].rearrange("p (n m) -> p n m", n=2))
             else:
-                multiply_wb(wb_sums[n], n, 1, M_HALF, M)
-            best = tile(f"best{n}", [P, M], F32, tag=("sess0", "sess1", "w1_raw1_2", "w1_raw2_2", "wg_even", "h1")[n])
-            for lo in range(0, M, width):
-                cols = slice(lo, lo + width)
-                nc.vector.tensor_tensor(best[:, cols], wb_sums[n][:, cols], ya[:, cols], ALU.max)
-                nc.sync.dma_start(out=out[n * P : (n + 1) * P, cols], in_=best[:, cols])
+                nc.sync.dma_start(out=rows, in_=best[:])
+
+        def pair_rows(half):
+            return out[0 : 2 * P, half * M_HALF : (half + 1) * M_HALF].rearrange("(n p) m -> p n m", p=P)
+
+        finish(paired[0, 0][:], paired[0, 1][:], pair_rows(0))
+        for which in range(2):
+            for n in range(2):
+                multiply(paired[1, which][:, n * M_HALF : (n + 1) * M_HALF], which, n, 1, M_HALF, M, False, n == 1)
+        finish(paired[1, 0][:], paired[1, 1][:], pair_rows(1))
+        for n in (2, 3):
+            for which in range(2):
+                multiply(whole[n, which][:, M_HALF:M], which, n, 1, M_HALF, M, False, True)
+            finish(whole[n, 0][:], whole[n, 1][:], out[n * P : (n + 1) * P, :])
+        sums = [bank(which) for which in range(2)]
+        for which in range(2):
+            multiply(sums[which][:], which, 4, 0, 0, M, True, False)
+            for lo in range(0, M, M_HALF):
+                multiply(sums[which][:, lo : lo + M_HALF], which, 4, 1, lo, lo + M_HALF, False, lo > 0)
+        finish(sums[0][:], sums[1][:], out[4 * P : 5 * P, :])
+        last_a = bank(2)
+        multiply(last_a[:], 0, 5, 0, 0, M, True, False)
+        for lo in range(0, M, M_HALF):
+            multiply(last_a[:, lo : lo + M_HALF], 0, 5, 1, lo, lo + M_HALF, False, lo > 0)
+        for half in range(2):
+            lo = half * M_HALF
+            last_b = bank(3 + half, M_HALF)
+            for a in range(R_PASSES):
+                multiply(last_b[:], 1, 5, a, lo, lo + M_HALF, a == 0, a == 1)
+            finish(last_a[:, lo : lo + M_HALF], last_b[:], out[5 * P : 6 * P, lo : lo + M_HALF])

@@ -40,14 +40,14 @@ LAST_CUT = 640
 KIB = 1024
 SIZES = (
     ("table0", 16 * KIB), ("table1", 16 * KIB), ("table2", 16 * KIB), ("v01", 8 * KIB), ("v2", 4 * KIB),
-    ("grouped2", 3 * KIB - ALIGN), ("table_scales", 4 * KIB), ("scales2", 384), ("wg0", 4 * KIB),
-    ("h", 8 * KIB), ("raw0", 8 * KIB), ("raw1", 6 * KIB), ("raw2", 6 * KIB), ("raw3", 6 * KIB),
+    ("table_scales", 4 * KIB), ("scales2", 384), ("wg0", 4 * KIB),
+    ("h", 8 * KIB), ("raw0", 8 * KIB), ("raw1", 6 * KIB), ("grouped2", 3 * KIB), ("raw2", 6 * KIB), ("raw3", 6 * KIB),
     ("wide", 24 * KIB), ("wgs", 4 * KIB), ("plane4", 6 * KIB + ALIGN), ("plane5", 4 * KIB),
     ("plane6", 4 * KIB + 512), ("plane7", 6 * KIB + 512), ("sess", 16 * KIB),
     ("wa", 3 * KIB), ("wa_scales", 1536), ("codes0", 1536), ("codes1", 3 * KIB), ("scales1", 384),
-    ("before_codes2", 4 * KIB - ALIGN), ("codes2", 1536), ("after_codes2", 4 * KIB - ALIGN), ("codes3", 1536),
+    ("before_codes2", 12 * KIB - ALIGN), ("codes2", 1536), ("codes3", 1536),
     ("codes4", 4 * KIB), ("scales4", 384), ("codes5", 1536),
-    ("before_codes6", 2 * KIB - ALIGN), ("codes6", 1536), ("after_codes6", 2 * KIB - ALIGN),
+    ("codes6", 4 * KIB),
     ("codes7", 1536),
     ("z_dealt", 8 * KIB), ("z_scales", KIB), ("z_codes_front", KIB), ("wb_scales", KIB),
     ("ident", 512), ("gain_rows", 512), ("gain_col", ALIGN), ("warm", ALIGN),
@@ -105,7 +105,8 @@ def tile_list_session_slot_verdict_kernel(
         def load_w1(c):
             tiles = []
             for a in range(K_PASSES):
-                raw = place(f"w1_raw{c}_{a}", [P, PACK, P], F32, AT[f"raw{c}"] + a * 2 * KIB)
+                spare = 1 if (c, a) == (1, K_PASSES - 1) else 0
+                raw = place(f"w1_raw{c}_{a}", [P, PACK + spare, P], F32, AT[f"raw{c}"] + a * 2 * KIB)[:, 0:PACK, :]
                 rows = w1[a * PASS : (a + 1) * PASS, c * P : (c + 1) * P]
                 nc.sync.dma_start(out=raw[:], in_=rows.rearrange("(p i) c -> p i c", i=PACK))
                 tiles.append(raw)
@@ -119,13 +120,15 @@ def tile_list_session_slot_verdict_kernel(
 
         sess_tiles = {}
 
-        def load_sess(c):
-            sess_tiles[c] = place(f"sess{c}", [P, M], F32, AT["sess"] + c * 2 * KIB)
-            if c < NATURAL:
-                rows = sess[c * P : (c + 1) * P, :]
+        def load_sess(c0, c1):
+            tiles = place(f"sess{c0}", [P, (c1 - c0) * M], F32, AT["sess"] + c0 * 2 * KIB)
+            if c0 < NATURAL:
+                rows = sess[c0 * P : c1 * P, :].rearrange("(c p) m -> p c m", p=P)
             else:
-                rows = sess[PASS:H, :].rearrange("(p t) m -> p t m", t=PACK)[:, c - NATURAL, :]
-            nc.sync.dma_start(out=sess_tiles[c][:], in_=rows)
+                rows = sess[PASS:H, :].rearrange("(p t) m -> p t m", t=PACK)
+            nc.sync.dma_start(out=tiles[:].rearrange("p (c m) -> p c m", m=M), in_=rows)
+            for c in range(c0, c1):
+                sess_tiles[c] = tiles[:, (c - c0) * M : (c - c0 + 1) * M]
 
         table_words = [load_table(0)]
         idx = lists.tile([P, S // LIST_ROWS], U16)
@@ -143,13 +146,12 @@ def tile_list_session_slot_verdict_kernel(
         idx3 = lists.tile([P, M // LIST_ROWS], U16)
         nc.sync.dma_start(idx3[:], offs3)
         w1_raw.append(load_w1(2))
-        load_sess(0)
+        load_sess(0, 1)
         w1_raw.append(load_w1(3))
-        load_sess(1)
+        load_sess(1, 2)
         w1_wide = {a: load_wide(a) for a in (1, 2)}
-        load_sess(2)
         w1_wide[0] = load_wide(0)
-        load_sess(3)
+        load_sess(2, NATURAL)
 
         gain_turned = bank(2, P)
         nc.tensor.transpose(gain_turned[:], gain_rows[:], ident[:])
@@ -173,68 +175,46 @@ def tile_list_session_slot_verdict_kernel(
             column = (c - NATURAL - 1) % PACK * M
             return z_dealt[:, column : column + 1]
 
-        fronts, backs, w1_codes, w1_scales = {}, {}, {}, {}
+        w1_grouped, w1_codes, w1_scales = {}, {}, {}
         SCALES_AT = (AT["table_scales"], AT["scales1"], AT["scales2"], AT["raw1"], AT["scales4"],
                      AT["plane4"], AT["plane5"], AT["plane6"])
         WEIGHTS_AT = (AT["wg0"], AT["raw2"], AT["raw3"], AT["wide"] + 2 * KIB, AT["raw1"],
-                      AT["wide"] + 16 * KIB, AT["plane4"], AT["raw0"])
+                      AT["codes4"], AT["plane4"], AT["raw0"])
         X_AT = (AT["raw2"] + 4 * KIB, AT["raw3"] + 4 * KIB, AT["wide"], AT["plane4"] + 4 * KIB)
         PLANE_AT = {4: AT["plane4"] + ALIGN, 5: AT["plane5"], 6: AT["plane6"], 7: AT["plane7"]}
 
         def group_w1(c):
-            if c == 0:
-                fronts[c] = place("w1_front0", [P, 2 * PASS], BF16, AT["raw0"] + 6 * KIB)[:]
-                backs[c] = place("w1_back0", [P, PASS], BF16, AT["v2"])[:]
-            else:
-                offset = (AT["table_scales"], AT["grouped2"], AT["codes1"])[c - 1]
-                whole = place(f"w1_grouped{c}", [P, K_PASSES * PASS], BF16, offset)
-                fronts[c], backs[c] = whole[:, 0 : 2 * PASS], whole[:, 2 * PASS : 3 * PASS]
-            for a, grouped in enumerate((fronts[c][:, 0:PASS], fronts[c][:, PASS : 2 * PASS], backs[c])):
-                interleave(nc, grouped, w1_raw[c][a][:])
+            offset = (AT["v2"], AT["table_scales"], AT["grouped2"], AT["codes1"])[c]
+            w1_grouped[c] = place(f"w1_grouped{c}", [P, K_PASSES * PASS], BF16, offset)[:]
+            for a in range(K_PASSES):
+                interleave(nc, w1_grouped[c][:, a * PASS : (a + 1) * PASS], w1_raw[c][a][:])
 
-        def deal(a, t0, grouped):
-            count = grouped.shape[1]
-            nc.scalar.copy(
-                out=grouped.rearrange("p t (q e i) -> p q i e t", e=2, i=PACK),
-                in_=w1_wide[a][:].rearrange("p i (q e t) -> p q i e t", e=2, t=PACK)[:, :, :, :, t0 : t0 + count],
-            )
-
-        def deal_fronts(c, offset):
-            pair = place(f"w1_fronts{c}", [P, 2, 2 * PASS], BF16, offset)
-            for a in (1, 2):
-                deal(a, c - NATURAL, pair[:, :, (a - 1) * PASS : a * PASS])
-            for u in range(2):
-                fronts[c + u] = pair[:, u, :]
-
-        def deal_backs(offset):
-            four = place("w1_backs", [P, PACK, PASS], BF16, offset)
-            deal(0, 0, four[:])
+        def deal_w1():
+            dealt = place("w1_dealt", [P, PACK, K_PASSES * PASS], BF16, AT["before_codes2"])
+            for a in (1, 2, 0):
+                nc.scalar.copy(
+                    out=dealt[:, :, a * PASS : (a + 1) * PASS].rearrange("p t (q e i) -> p q i e t", e=2, i=PACK),
+                    in_=w1_wide[a][:].rearrange("p i (q e t) -> p q i e t", e=2, t=PACK),
+                )
             for t in range(PACK):
-                backs[NATURAL + t] = four[:, t, :]
+                w1_grouped[NATURAL + t] = dealt[:, t, :]
 
-        def passes_of(c):
-            return (0, 1, 2) if c < NATURAL else (1, 2, 0)
-
-        def quantize_w1(c, part):
-            if part == 0:
-                w1_codes[c] = place(f"w1_codes{c}", [P, K_PASSES * P], U32, AT[f"codes{c}"])
-                w1_scales[c] = place(f"w1_scales{c}", [P, K_PASSES * P], U8, SCALES_AT[c])
-            cols = (slice(0, 2 * P), slice(2 * P, 3 * P))[part]
-            nc.vector.quantize_mx(
-                out=w1_codes[c][:, cols].bitcast(FP8X4), scales=w1_scales[c][:, cols], in_=(fronts, backs)[part][c]
-            )
+        def quantize_w1(c):
+            w1_codes[c] = place(f"w1_codes{c}", [P, K_PASSES * P], U32, AT[f"codes{c}"])
+            w1_scales[c] = place(f"w1_scales{c}", [P, K_PASSES * P], U8, SCALES_AT[c])
+            nc.vector.quantize_mx(out=w1_codes[c][:].bitcast(FP8X4), scales=w1_scales[c][:], in_=w1_grouped[c])
 
         def multiply_w1(c, b, lo, hi):
             acc = bank(b, hi - lo)
-            for u, a in enumerate(passes_of(c)):
+            for a in range(K_PASSES):
                 nc.tensor.matmul_mx(
                     out=acc[:],
-                    lhsT=w1_codes[c][:, u * P : (u + 1) * P].bitcast(FP8X4),
-                    lhsT_scale=w1_scales[c][:, u * P : (u + 1) * P],
+                    lhsT=w1_codes[c][:, a * P : (a + 1) * P].bitcast(FP8X4),
+                    lhsT_scale=w1_scales[c][:, a * P : (a + 1) * P],
                     rhs=v_words[a][:, lo:hi].bitcast(FP8X4),
                     rhs_scale=v_scales[SCALE_ROWS * a : P, lo:hi],
-                    start=(u == 0),
-                    stop=(u == K_PASSES - 1),
+                    start=(a == 0),
+                    stop=(a == K_PASSES - 1),
                 )
             return acc
 
@@ -263,11 +243,10 @@ def tile_list_session_slot_verdict_kernel(
             nc.vector.tensor_tensor(x[:, lo:hi], pages[c % 2][:].indirect(entries(idx3, lo, hi)), sess_tiles[c][:, lo:hi], ALU.add)
 
         group_w1(0)
-        for part in range(2):
-            quantize_w1(0, part)
+        quantize_w1(0)
         v_words.append(place("v_words2", [P, S], U32, AT["v2"]))
         cuts = (0, FIRST_CUT, BANK, S)
-        for lo, hi in zip(cuts, cuts[1:]):
+        for lo, hi in ((0, FIRST_CUT), (FIRST_CUT, S)):
             nc.vector.tensor_copy(v_words[2][:, lo:hi], table_words[2][:].indirect(entries(idx, lo, hi)))
 
         def load_dealt(c):
@@ -285,8 +264,8 @@ def tile_list_session_slot_verdict_kernel(
             return raw
 
         load_dealt(4)
-        load_sess(4)
         load_dealt(5)
+        load_sess(NATURAL, R_TILES)
         wa_codes = place("wa_codes", [P, R_PASSES, 2 * N], U8, AT["wa"])
         nc.sync.dma_start(out=wa_codes[:].bitcast(I32), in_=wa_words.rearrange("a p n -> p a n").bitcast(I32))
         for q in range(P // QUADRANT):
@@ -296,11 +275,8 @@ def tile_list_session_slot_verdict_kernel(
             )
         wb_raw = [load_wb(0)]
         load_dealt(6)
-        load_sess(5)
-        wb_raw.append(load_wb(1))
         load_dealt(7)
-        load_sess(6)
-        load_sess(7)
+        wb_raw.append(load_wb(1))
 
         first_sums = [multiply_w1(0, b, lo, hi) for b, lo, hi in zip((0, 1, 6), cuts, cuts[1:])]
         weights[0] = weigh(0, BANK)
@@ -310,8 +286,7 @@ def tile_list_session_slot_verdict_kernel(
             gelu(h_front[:, lo:hi], first_sums[u])
             scatter(0, h_front[:, lo:hi], lo, hi)
         group_w1(1)
-        for part in range(2):
-            quantize_w1(1, part)
+        quantize_w1(1)
         h_back = place("h_back", [P, BANK], F32, AT["raw1"] + 4 * KIB)
         gelu(h_back[:], first_sums[2])
         scatter(0, h_back[:], BANK, S)
@@ -325,6 +300,7 @@ def tile_list_session_slot_verdict_kernel(
             for u, (a, piece) in enumerate(keys):
                 wb_grouped[a, piece] = staged[:, u, :]
                 interleave(nc, staged[:, u, :], wb_raw[a][:, :, piece * WB_PIECE : (piece + 1) * WB_PIECE])
+            return staged
 
         def quantize_wb(a, piece):
             nc.vector.quantize_mx(
@@ -332,7 +308,6 @@ def tile_list_session_slot_verdict_kernel(
             )
 
         z_natural = place("z_natural", [P, PACK * M], F32, AT["raw0"])
-        z_first = {}
 
         def deal_rows(c, x):
             for t in range(PACK):
@@ -348,39 +323,33 @@ def tile_list_session_slot_verdict_kernel(
             if c == 0:
                 group_w1(3)
             if c == 1:
-                deal_fronts(4, AT["before_codes2"])
-                deal_backs(AT["codes2"] + 1536 - ALIGN)
-            if c == 3:
-                deal_fronts(6, AT["codes4"])
+                deal_w1()
             if c == 5:
-                for half in range(2):
-                    offset = (AT["before_codes6"], AT["codes6"] + 1536 - ALIGN)[half]
-                    z_first[half] = place(f"z_first{half}", [P, PACK * M_HALF], BF16, offset)
-                    rows = z_natural[:].rearrange("p (t m) -> p t m", t=PACK)
-                    interleave(nc, z_first[half][:], rows[:, :, half * M_HALF : (half + 1) * M_HALF])
+                z_first = place("z_first", [P, PACK * M], BF16, AT["codes6"])
+                interleave(nc, z_first[:], z_natural[:].rearrange("p (t m) -> p t m", t=PACK))
                 group_wb("staged10", AT["plane5"], ((1, 0),))
             if ahead <= LAST:
                 weights[ahead] = weigh(ahead, S)
             if c == 4:
-                group_wb("staged_early", AT["plane6"] + 448, ((0, 0), (0, 1)))
+                staged_early = group_wb("staged_early", AT["plane6"] + 448, ((0, 0), (0, 1)))
             if c == 6:
                 group_wb("staged11", AT["plane7"] + 512, ((1, 1),))
                 group_wb("staged2", AT["plane7"] + 512 + 2 * KIB, ((0, 2), (1, 2)))
             if ahead <= LAST:
-                quantize_w1(ahead, 0)
+                quantize_w1(ahead)
             else:
                 early = place("wb_codes_early", [P, 2, WB_PIECE], U32, AT["codes4"])
                 early_scales = place("wb_scales_early", [P, 2, WB_PIECE], U8, AT["plane7"])
                 for piece in range(2):
                     wb_codes[0, piece] = early[:, piece, :]
                     wb_scales[0, piece] = early_scales[:, piece, :]
-                quantize_wb(0, 0)
+                nc.vector.quantize_mx(
+                    out=early[:].rearrange("p u n -> p (u n)").bitcast(FP8X4),
+                    scales=early_scales[:].rearrange("p u n -> p (u n)"),
+                    in_=staged_early[:].rearrange("p u n -> p (u n)"),
+                )
             x = place(f"x{c}", [P, M], F32, X_AT[c]) if c < NATURAL else z_rows(c)
             gather(x, c, 0, M)
-            if ahead <= LAST:
-                quantize_w1(ahead, 1)
-            else:
-                quantize_wb(0, 1)
             if c < NATURAL:
                 deal_rows(c, x)
 
@@ -398,11 +367,9 @@ def tile_list_session_slot_verdict_kernel(
         for lo, hi in spans:
             join_z(lo, hi, 0, PACK - 1)
         scatter(LAST, h[:, 0:LAST_CUT], 0, LAST_CUT)
-        codes_first = place("z_codes_first", [P, M], U32, AT["sess"] + 6 * 2 * KIB)
+        codes_first = place("z_codes_first", [P, M], U32, AT["table0"])
         scales_first = place("z_scales_first", [P, M], U8, AT["z_scales"])
-        for half in range(2):
-            cols = slice(half * M_HALF, (half + 1) * M_HALF)
-            nc.vector.quantize_mx(out=codes_first[:, cols].bitcast(FP8X4), scales=scales_first[:, cols], in_=z_first[half][:])
+        nc.vector.quantize_mx(out=codes_first[:].bitcast(FP8X4), scales=scales_first[:], in_=z_first[:])
         scatter(LAST, h[:, LAST_CUT:S], LAST_CUT, S)
 
         z_half = {}
@@ -440,7 +407,7 @@ def tile_list_session_slot_verdict_kernel(
                 multiply(whole[n, which][:], which, n, 0, 0, M, True, False)
 
         late_scales = place("wb_scales_late", [P, 4, WB_PIECE], U8, AT["wb_scales"])
-        late_at = {(1, 0): AT["before_codes6"], (1, 1): AT["table2"], (0, 2): AT["table2"] + KIB,
+        late_at = {(1, 0): AT["codes6"], (1, 1): AT["table2"], (0, 2): AT["table2"] + KIB,
                    (1, 2): AT["plane7"] + 512 + KIB}
 
         def quantize_late(key):

@@ -28,28 +28,25 @@ ALIGN = 64
 K_PASSES = K // PASS
 R_PASSES = H // PASS
 R_TILES = H // P
-N_TILES = N // P
 NATURAL = PASS // P
 LAST = R_TILES - 1
-M_HALF = M // 2
-M_QUARTER = M // 4
-WB_PIECE = 256
+HALF = M // 2
+QUARTER = M // 4
+PAIR = 2 * P
 FIRST_CUT = 256
 LAST_CUT = 640
+W1_CODES = K_PASSES * P
 
 KIB = 1024
 SIZES = (
-    ("table0", 16 * KIB), ("table1", 16 * KIB), ("table2", 16 * KIB), ("v01", 8 * KIB), ("v2", 4 * KIB),
-    ("table_scales", 4 * KIB), ("scales2", 384), ("wg0", 4 * KIB),
-    ("h", 8 * KIB), ("raw0", 8 * KIB), ("raw1", 6 * KIB), ("grouped2", 3 * KIB), ("raw2", 6 * KIB), ("raw3", 6 * KIB),
-    ("wide", 24 * KIB), ("wgs", 4 * KIB), ("plane4", 6 * KIB + ALIGN), ("plane5", 4 * KIB),
-    ("plane6", 4 * KIB + 512), ("plane7", 6 * KIB + 512), ("sess", 16 * KIB),
-    ("wa", 3 * KIB), ("wa_scales", 1536), ("codes0", 1536), ("codes1", 3 * KIB), ("scales1", 384),
-    ("before_codes2", 12 * KIB - ALIGN), ("codes2", 1536), ("codes3", 1536),
-    ("codes4", 4 * KIB), ("scales4", 384), ("codes5", 1536),
-    ("codes6", 4 * KIB),
-    ("codes7", 1536),
-    ("z_dealt", 8 * KIB), ("z_scales", KIB), ("z_codes_front", KIB), ("wb_scales", KIB),
+    ("table0", 16 * KIB), ("table1", 16 * KIB), ("table2", 16 * KIB), ("z_natural", 8 * KIB),
+    ("v01", 8 * KIB), ("table_scales", 4 * KIB),
+    ("grouped0", 3 * KIB), ("codes0", 3 * KIB), ("wgs", 4 * KIB), ("weights0", 4 * KIB), ("h0", 2 * KIB),
+    ("raw1", 6 * KIB), ("grouped2", 3 * KIB), ("codes1", 3 * KIB),
+    ("raw2", 6 * KIB), ("h_odd", 4 * KIB), ("codes2", 2 * KIB), ("raw3", 6 * KIB), ("wide", 24 * KIB),
+    ("gain2", 6 * KIB), ("gain3", 6 * KIB), ("gain4", 6 * KIB), ("gain5", 6 * KIB), ("gain6", 4 * KIB),
+    ("gain7", 2 * KIB), ("z_codes", 2 * KIB), ("front", 4 * KIB), ("back", 6 * KIB), ("z_dealt", 8 * KIB),
+    ("planes", 16 * KIB), ("sess", 16 * KIB), ("wa", 3 * KIB), ("wa_scales", 1536),
     ("ident", 512), ("gain_rows", 512), ("gain_col", ALIGN), ("warm", ALIGN),
 )
 AT = {name: sum(size for other, size in SIZES[:i]) for i, (name, width) in enumerate(SIZES)}
@@ -81,6 +78,13 @@ def tile_list_session_slot_verdict_kernel(
         def bank(b, width=BANK):
             return psum.tile([P, width], F32, name=f"bank{b}", tag=f"bank{b}")
 
+        def quantize(name, grouped, codes_at, scales_at):
+            width = grouped.shape[1] // PACK
+            codes = place(f"{name}_codes", [P, width], U32, codes_at)
+            scales = place(f"{name}_scales", [P, width], U8, scales_at)
+            nc.vector.quantize_mx(out=codes[:].bitcast(FP8X4), scales=scales[:], in_=grouped)
+            return codes, scales
+
         table_scales = place("table_scales", [P, T], U8, AT["table_scales"])
         nc.vector.memset(table_scales[:].bitcast(I32), 0)
         for q in range(P // QUADRANT):
@@ -102,13 +106,14 @@ def tile_list_session_slot_verdict_kernel(
             nc.sync.dma_start(out=words[:].bitcast(I32), in_=tab_words[a].rearrange("p t i -> p (t i)").bitcast(I32))
             return words
 
-        def load_w1(c):
+        def load_w1(c, offset):
             tiles = []
             for a in range(K_PASSES):
-                spare = 1 if (c, a) == (1, K_PASSES - 1) else 0
-                raw = place(f"w1_raw{c}_{a}", [P, PACK + spare, P], F32, AT[f"raw{c}"] + a * 2 * KIB)[:, 0:PACK, :]
+                spare = ALIGN // 4 if c in (1, 2) and a == K_PASSES - 1 else 0
+                raw = place(f"w1_raw{c}_{a}", [P, PASS + spare], F32, offset + a * 2 * KIB)[:, 0:PASS]
+                raw = raw.rearrange("p (i c) -> p i c", i=PACK)
                 rows = w1[a * PASS : (a + 1) * PASS, c * P : (c + 1) * P]
-                nc.sync.dma_start(out=raw[:], in_=rows.rearrange("(p i) c -> p i c", i=PACK))
+                nc.sync.dma_start(out=raw, in_=rows.rearrange("(p i) c -> p i c", i=PACK))
                 tiles.append(raw)
             return tiles
 
@@ -130,87 +135,98 @@ def tile_list_session_slot_verdict_kernel(
             for c in range(c0, c1):
                 sess_tiles[c] = tiles[:, (c - c0) * M : (c - c0 + 1) * M]
 
+        gains, wgs_rows = {}, {}
+
+        def load_gain(c):
+            width = PAIR if c == LAST else ALIGN // 4
+            gains[c] = place(f"gain{c}", [P, width], F32, AT[f"gain{c}"])[:, 0:1]
+            if c < NATURAL:
+                column = gain[c * P : (c + 1) * P].rearrange("(p o) -> p o", o=1)
+            else:
+                column = gain[PASS:H].rearrange("(p t) -> p t", t=PACK)[:, c - NATURAL : c - NATURAL + 1]
+            with nc.allow_non_contiguous_dma(reason="one gain for each partition"):
+                nc.sync.dma_start(out=gains[c], in_=column)
+
+        def load_plane(c):
+            wgs_rows[c] = place(f"wgs_dealt{c}", [P, S], F32, AT["planes"] + (c - NATURAL) * 4 * KIB)
+            rows = wgs.rearrange("(p t) j -> p t j", t=PACK)[:, c - NATURAL, :]
+            for q in (0, 2, 1, 3):
+                nc.sync.dma_start(out=wgs_rows[c][QUADRANT * q : QUADRANT * (q + 1), :], in_=rows)
+            load_gain(c)
+
+        def load_wb(a, offset):
+            raw = place(f"wb_raw{a}", [P, PACK, N], F32, offset)
+            nc.sync.dma_start(out=raw[:], in_=wb[a * PASS : (a + 1) * PASS, :].rearrange("(p i) n -> p i n", i=PACK))
+            return raw
+
         table_words = [load_table(0)]
         idx = lists.tile([P, S // LIST_ROWS], U16)
         nc.sync.dma_start(idx[:], offs)
         table_words.append(load_table(1))
-        nc.sync.dma_start(out=gain_rows[0:NATURAL, :], in_=gain[0:PASS].rearrange("(c p) -> c p", p=P))
-        w1_raw = [load_w1(0)]
+        nc.sync.dma_start(out=gain_rows[0:2, :], in_=gain[0 : 2 * P].rearrange("(c p) -> c p", p=P))
+        w1_raw = [load_w1(0, AT["z_natural"])]
         table_words.append(load_table(2))
         wgs_tile = place("wgs_tile", [P, S], F32, AT["wgs"])
         for lo in range(0, S, BANK):
             nc.sync.dma_start(out=wgs_tile[:, lo : lo + BANK], in_=wgs[:, lo : lo + BANK])
+        for c in range(NATURAL):
+            wgs_rows[c] = wgs_tile
         idx2 = lists.tile([P, S // LIST_ROWS], U16)
         nc.sync.dma_start(idx2[:], offs2)
-        w1_raw.append(load_w1(1))
+        w1_raw.append(load_w1(1, AT["raw1"]))
         idx3 = lists.tile([P, M // LIST_ROWS], U16)
         nc.sync.dma_start(idx3[:], offs3)
-        w1_raw.append(load_w1(2))
+        w1_raw.append(load_w1(2, AT["raw2"]))
         load_sess(0, 1)
-        w1_raw.append(load_w1(3))
+        w1_raw.append(load_w1(3, AT["raw3"]))
+        load_gain(2)
+        w1_wide = [load_wide(a) for a in range(K_PASSES)]
         load_sess(1, 2)
-        w1_wide = {a: load_wide(a) for a in (1, 2)}
-        w1_wide[0] = load_wide(0)
-        load_sess(2, NATURAL)
+        load_gain(3)
 
         gain_turned = bank(2, P)
         nc.tensor.transpose(gain_turned[:], gain_rows[:], ident[:])
-        gain_col = place("gain_col", [P, NATURAL], F32, AT["gain_col"])
-        nc.scalar.copy(out=gain_col[:], in_=gain_turned[:, 0:NATURAL])
+        gain_col = place("gain_col", [P, 2], F32, AT["gain_col"])
+        nc.scalar.copy(out=gain_col[:], in_=gain_turned[:, 0:2])
 
         v_words = [place(f"v_words{a}", [P, S], U32, AT["v01"] + a * 4 * KIB) for a in range(2)]
         nc.vector.tensor_copy(v_words[0][:], table_words[0][:].indirect(idx[:]))
         pages = [place(f"page{u}", [P, T2], F32, AT["table0"] + u * 8 * KIB) for u in range(2)]
         for page in pages:
             nc.vector.memset(page[:].bitcast(I32), 0)
-        z_dealt = place("z_dealt", [P, PACK * M], F32, AT["z_dealt"])
         nc.vector.tensor_copy(v_words[1][:], table_words[1][:].indirect(idx[:]))
         v_scales = place("v_scales", [P, S], U8, AT["table1"] + 12 * KIB)
         nc.vector.tensor_copy(v_scales[:], table_scales[:].indirect(idx[:]))
 
-        def z_rows(c):
-            return z_dealt[:, (c - NATURAL) * M : (c - NATURAL + 1) * M]
+        w1_grouped, w1_mx = {}, {}
 
-        def gain_of(c):
-            column = (c - NATURAL - 1) % PACK * M
-            return z_dealt[:, column : column + 1]
-
-        w1_grouped, w1_codes, w1_scales = {}, {}, {}
-        SCALES_AT = (AT["table_scales"], AT["scales1"], AT["scales2"], AT["raw1"], AT["scales4"],
-                     AT["plane4"], AT["plane5"], AT["plane6"])
-        WEIGHTS_AT = (AT["wg0"], AT["raw2"], AT["raw3"], AT["wide"] + 2 * KIB, AT["raw1"],
-                      AT["codes4"], AT["plane4"], AT["raw0"])
-        X_AT = (AT["raw2"] + 4 * KIB, AT["raw3"] + 4 * KIB, AT["wide"], AT["plane4"] + 4 * KIB)
-        PLANE_AT = {4: AT["plane4"] + ALIGN, 5: AT["plane5"], 6: AT["plane6"], 7: AT["plane7"]}
-
-        def group_w1(c):
-            offset = (AT["v2"], AT["table_scales"], AT["grouped2"], AT["codes1"])[c]
+        def group_w1(c, offset):
             w1_grouped[c] = place(f"w1_grouped{c}", [P, K_PASSES * PASS], BF16, offset)[:]
             for a in range(K_PASSES):
-                interleave(nc, w1_grouped[c][:, a * PASS : (a + 1) * PASS], w1_raw[c][a][:])
+                interleave(nc, w1_grouped[c][:, a * PASS : (a + 1) * PASS], w1_raw[c][a])
 
-        def deal_w1():
-            dealt = place("w1_dealt", [P, PACK, K_PASSES * PASS], BF16, AT["before_codes2"])
-            for a in (1, 2, 0):
+        def deal_w1(c, offset):
+            dealt = place(f"w1_dealt{c}", [P, 2, K_PASSES * PASS], BF16, offset)
+            t = c - NATURAL
+            for a in range(K_PASSES):
                 nc.scalar.copy(
                     out=dealt[:, :, a * PASS : (a + 1) * PASS].rearrange("p t (q e i) -> p q i e t", e=2, i=PACK),
-                    in_=w1_wide[a][:].rearrange("p i (q e t) -> p q i e t", e=2, t=PACK),
+                    in_=w1_wide[a][:].rearrange("p i (q e t) -> p q i e t", e=2, t=PACK)[:, :, :, :, t : t + 2],
                 )
-            for t in range(PACK):
-                w1_grouped[NATURAL + t] = dealt[:, t, :]
+            for u in range(2):
+                w1_grouped[c + u] = dealt[:, u, :]
 
-        def quantize_w1(c):
-            w1_codes[c] = place(f"w1_codes{c}", [P, K_PASSES * P], U32, AT[f"codes{c}"])
-            w1_scales[c] = place(f"w1_scales{c}", [P, K_PASSES * P], U8, SCALES_AT[c])
-            nc.vector.quantize_mx(out=w1_codes[c][:].bitcast(FP8X4), scales=w1_scales[c][:], in_=w1_grouped[c])
+        def quantize_w1(c, offset):
+            w1_mx[c] = quantize(f"w1_{c}", w1_grouped[c], offset, offset + 4 * W1_CODES)
 
         def multiply_w1(c, b, lo, hi):
+            codes, scales = w1_mx[c]
             acc = bank(b, hi - lo)
             for a in range(K_PASSES):
                 nc.tensor.matmul_mx(
                     out=acc[:],
-                    lhsT=w1_codes[c][:, a * P : (a + 1) * P].bitcast(FP8X4),
-                    lhsT_scale=w1_scales[c][:, a * P : (a + 1) * P],
+                    lhsT=codes[:, a * P : (a + 1) * P].bitcast(FP8X4),
+                    lhsT_scale=scales[:, a * P : (a + 1) * P],
                     rhs=v_words[a][:, lo:hi].bitcast(FP8X4),
                     rhs_scale=v_scales[SCALE_ROWS * a : P, lo:hi],
                     start=(a == 0),
@@ -221,51 +237,27 @@ def tile_list_session_slot_verdict_kernel(
         def gelu(dst, acc):
             nc.scalar.activation(out=dst, in_=acc[:], func=ACT.Gelu_apprx_tanh)
 
-        def features(c):
-            h = place(f"h{c}", [P, S], F32, AT["h"] + c % 2 * 4 * KIB if c < LAST else AT["raw0"] + 4 * KIB)
-            for half in range(S // BANK):
-                gelu(h[:, half * BANK : (half + 1) * BANK], multiply_w1(c, 6 + half, half * BANK, (half + 1) * BANK))
-            return h
+        def scale(dst, src, column):
+            nc.scalar.activation(out=dst, in_=src, func=ACT.Copy, scale=column)
 
-        wgs_dealt, weights = {}, {}
-
-        def weigh(c, step):
-            wg = place(f"wg{c}", [P, S], F32, WEIGHTS_AT[c])
-            rows, gains = (wgs_tile, gain_col[:, c : c + 1]) if c < NATURAL else (wgs_dealt[c], gain_of(c))
-            for lo in range(0, S, step):
-                nc.scalar.activation(out=wg[:, lo : lo + step], in_=rows[:, lo : lo + step], func=ACT.Copy, scale=gains)
-            return wg
-
-        def scatter(c, h, lo, hi):
-            nc.vector.tensor_tensor(pages[c % 2][:].indirect(entries(idx2, lo, hi)), h, weights[c][:, lo:hi], ALU.mult)
+        def scatter(c, h, weights, lo, hi):
+            nc.vector.tensor_tensor(pages[c % 2][:].indirect(entries(idx2, lo, hi)), h, weights[:, lo:hi], ALU.mult)
 
         def gather(x, c, lo, hi):
             nc.vector.tensor_tensor(x[:, lo:hi], pages[c % 2][:].indirect(entries(idx3, lo, hi)), sess_tiles[c][:, lo:hi], ALU.add)
 
-        group_w1(0)
-        quantize_w1(0)
-        v_words.append(place("v_words2", [P, S], U32, AT["v2"]))
-        cuts = (0, FIRST_CUT, BANK, S)
+        group_w1(0, AT["grouped0"])
+        quantize_w1(0, AT["codes0"])
+        v_words.append(place("v_words2", [P, S], U32, AT["table_scales"]))
         for lo, hi in ((0, FIRST_CUT), (FIRST_CUT, S)):
             nc.vector.tensor_copy(v_words[2][:, lo:hi], table_words[2][:].indirect(entries(idx, lo, hi)))
 
-        def load_dealt(c):
-            gains = gain[PASS:H].rearrange("(p t) -> p t", t=PACK)[:, c - NATURAL : c - NATURAL + 1]
-            with nc.allow_non_contiguous_dma(reason="one gain for each partition"):
-                nc.sync.dma_start(out=gain_of(c), in_=gains)
-            wgs_dealt[c] = place(f"wgs_dealt{c}", [P, S], F32, PLANE_AT[c])
-            rows = wgs.rearrange("(p t) j -> p t j", t=PACK)[:, c - NATURAL, :]
-            for q in (0, 2, 1, 3):
-                nc.sync.dma_start(out=wgs_dealt[c][QUADRANT * q : QUADRANT * (q + 1), :], in_=rows)
-
-        def load_wb(a):
-            raw = place(f"wb_raw{a}", [P, PACK, N], F32, AT[f"table{a + 1}"])
-            nc.sync.dma_start(out=raw[:], in_=wb[a * PASS : (a + 1) * PASS, :].rearrange("(p i) n -> p i n", i=PACK))
-            return raw
-
-        load_dealt(4)
-        load_dealt(5)
+        wb_raw = [load_wb(0, AT["table1"])]
+        load_sess(2, NATURAL)
+        load_plane(4)
+        wb_raw.append(load_wb(1, AT["table2"] + 4 * KIB))
         load_sess(NATURAL, R_TILES)
+        load_plane(5)
         wa_codes = place("wa_codes", [P, R_PASSES, 2 * N], U8, AT["wa"])
         nc.sync.dma_start(out=wa_codes[:].bitcast(I32), in_=wa_words.rearrange("a p n -> p a n").bitcast(I32))
         for q in range(P // QUADRANT):
@@ -273,211 +265,225 @@ def tile_list_session_slot_verdict_kernel(
                 out=wa_scale_tile[QUADRANT * q : QUADRANT * q + SCALE_ROWS, :, :].bitcast(I32),
                 in_=wa_scales[:, SCALE_ROWS * q : SCALE_ROWS * (q + 1), :].rearrange("a r n -> r a n").bitcast(I32),
             )
-        wb_raw = [load_wb(0)]
-        load_dealt(6)
-        load_dealt(7)
-        wb_raw.append(load_wb(1))
+        load_plane(6)
+        load_plane(7)
 
+        cuts = (0, FIRST_CUT, BANK, S)
         first_sums = [multiply_w1(0, b, lo, hi) for b, lo, hi in zip((0, 1, 6), cuts, cuts[1:])]
-        weights[0] = weigh(0, BANK)
-        h_front = place("h_front", [P, BANK], F32, AT["h"])
+        weights = place("weights0", [P, S], F32, AT["weights0"])
+        for lo in range(0, S, BANK):
+            scale(weights[:, lo : lo + BANK], wgs_tile[:, lo : lo + BANK], gain_col[:, 0:1])
+        h_front = place("h0_front", [P, BANK], F32, AT["h0"])
         for u in range(2):
             lo, hi = cuts[u], cuts[u + 1]
             gelu(h_front[:, lo:hi], first_sums[u])
-            scatter(0, h_front[:, lo:hi], lo, hi)
-        group_w1(1)
-        quantize_w1(1)
-        h_back = place("h_back", [P, BANK], F32, AT["raw1"] + 4 * KIB)
+            scatter(0, h_front[:, lo:hi], weights, lo, hi)
+        group_w1(1, AT["codes0"])
+        quantize_w1(1, AT["codes1"])
+        h_back = place("h0_back", [P, BANK], F32, AT["raw1"] + 4 * KIB)
         gelu(h_back[:], first_sums[2])
-        scatter(0, h_back[:], BANK, S)
-        group_w1(2)
-        weights[1] = weigh(1, S)
+        scatter(0, h_back[:], weights, BANK, S)
+        group_w1(2, AT["grouped2"])
+        quantize_w1(2, AT["codes2"])
 
-        wb_grouped, wb_codes, wb_scales = {}, {}, {}
+        z_natural = place("z_natural", [P, PACK * M], F32, AT["z_natural"])
 
-        def group_wb(name, offset, keys):
-            staged = place(name, [P, len(keys), PACK * WB_PIECE], BF16, offset)
-            for u, (a, piece) in enumerate(keys):
-                wb_grouped[a, piece] = staged[:, u, :]
-                interleave(nc, staged[:, u, :], wb_raw[a][:, :, piece * WB_PIECE : (piece + 1) * WB_PIECE])
-            return staged
-
-        def quantize_wb(a, piece):
-            nc.vector.quantize_mx(
-                out=wb_codes[a, piece].bitcast(FP8X4), scales=wb_scales[a, piece], in_=wb_grouped[a, piece]
-            )
-
-        z_natural = place("z_natural", [P, PACK * M], F32, AT["raw0"])
-
-        def deal_rows(c, x):
+        def pick_natural(c, x):
+            gather(x, c, 0, M)
             for t in range(PACK):
                 nc.sync.dma_start(
                     out=z_natural[QUADRANT * c : QUADRANT * (c + 1), t * M : (t + 1) * M], in_=x[t:P:PACK, :]
                 )
 
-        for c in range(LAST):
-            ahead = c + 2
-            if c > 0:
-                scatter(c, h[:], 0, S)
-            h = features(c + 1)
-            if c == 0:
-                group_w1(3)
-            if c == 1:
-                deal_w1()
-            if c == 5:
-                z_first = place("z_first", [P, PACK * M], BF16, AT["codes6"])
-                interleave(nc, z_first[:], z_natural[:].rearrange("p (t m) -> p t m", t=PACK))
-                group_wb("staged10", AT["plane5"], ((1, 0),))
-            if ahead <= LAST:
-                weights[ahead] = weigh(ahead, S)
-            if c == 4:
-                staged_early = group_wb("staged_early", AT["plane6"] + 448, ((0, 0), (0, 1)))
-            if c == 6:
-                group_wb("staged11", AT["plane7"] + 512, ((1, 1),))
-                group_wb("staged2", AT["plane7"] + 512 + 2 * KIB, ((0, 2), (1, 2)))
-            if ahead <= LAST:
-                quantize_w1(ahead)
+        x0 = place("x0", [P, M], F32, AT["raw2"] + 4 * KIB)
+        pick_natural(0, x0)
+        weights = place("weights1", [P, S], F32, AT["raw2"])
+        scale(weights[:], wgs_tile[:], gain_col[:, 1:2])
+        h = place("h1", [P, S], F32, AT["h_odd"])
+        for half in range(2):
+            gelu(h[:, half * BANK : (half + 1) * BANK], multiply_w1(1, 6 + half, half * BANK, (half + 1) * BANK))
+        scatter(1, h[:], weights, 0, S)
+        group_w1(3, AT["codes1"])
+
+        z_dealt = place("z_dealt", [P, (PACK - 1) * M], F32, AT["z_dealt"])
+        H_AT = {2: AT["raw3"] + 2 * KIB, 3: AT["h_odd"], 4: AT["raw3"] + 2 * KIB, 5: AT["wide"],
+                6: AT["table1"], 7: AT["z_natural"] - 2 * KIB}
+        wb_grouped, wb_mx = {}, {}
+
+        def group_wb(a, offset):
+            wb_grouped[a] = place(f"wb_grouped{a}", [P, PACK * N], BF16, offset)
+            for lo in range(0, N, PAIR):
+                interleave(nc, wb_grouped[a][:, PACK * lo : PACK * (lo + PAIR)], wb_raw[a][:, :, lo : lo + PAIR])
+
+        def quantize_wb(a, lo, hi, codes_at, scales_at):
+            codes, scales = quantize(f"wb{a}_{lo}", wb_grouped[a][:, PACK * lo : PACK * hi], codes_at, scales_at)
+            for n in range(lo // P, hi // P):
+                first = n * P - lo
+                wb_mx[a, n] = (codes[:, first : first + P], scales[:, first : first + P])
+
+        def z_plane(c):
+            return z_dealt[:, (c - NATURAL) * M : (c - NATURAL + 1) * M]
+
+        for c in range(2, R_TILES):
+            front_at = AT["front"] + c % 2 * 2 * KIB
+            front = place(f"front{c}", [P, BANK], F32, front_at)
+            if c <= NATURAL:
+                back = place(f"back{c}", [P, BANK], F32, AT["back"] + (c - 2) * 2 * KIB)[:]
             else:
-                early = place("wb_codes_early", [P, 2, WB_PIECE], U32, AT["codes4"])
-                early_scales = place("wb_scales_early", [P, 2, WB_PIECE], U8, AT["plane7"])
-                for piece in range(2):
-                    wb_codes[0, piece] = early[:, piece, :]
-                    wb_scales[0, piece] = early_scales[:, piece, :]
-                nc.vector.quantize_mx(
-                    out=early[:].rearrange("p u n -> p (u n)").bitcast(FP8X4),
-                    scales=early_scales[:].rearrange("p u n -> p (u n)"),
-                    in_=staged_early[:].rearrange("p u n -> p (u n)"),
-                )
-            x = place(f"x{c}", [P, M], F32, X_AT[c]) if c < NATURAL else z_rows(c)
-            gather(x, c, 0, M)
-            if c < NATURAL:
-                deal_rows(c, x)
+                back = z_plane(c - 1)
+            gelu(front[:], multiply_w1(c, 6, 0, BANK))
+            gelu(back, multiply_w1(c, 7, BANK, S))
+            h = place(f"h{c}", [P, S], F32, H_AT[c])
+            scale(h[:, 0:BANK], front[:], gains[c])
+            scale(h[:, BANK:S], back, gains[c])
+            if c < LAST:
+                quantize_w1(c + 1, front_at)
+                scatter(c, h[:], wgs_rows[c], 0, S)
+            else:
+                quantize_wb(0, 0, PAIR, front_at, front_at + 4 * PAIR)
+                scatter(c, h[:, 0:LAST_CUT], wgs_rows[c], 0, LAST_CUT)
+            if c <= NATURAL:
+                pick_natural(c - 1, back)
+            else:
+                gather(back, c - 1, 0, M)
+            if c in (2, 3):
+                deal_w1(2 * c, AT[f"gain{c}"])
+            elif c in (4, 5):
+                group_wb(c - 4, AT[f"gain{c}"])
+            elif c == 6:
+                z_first = place("z_first", [P, PACK * M], BF16, AT["gain6"])
+                interleave(nc, z_first[:], z_natural[:].rearrange("p (t m) -> p t m", t=PACK))
 
-        spans = ((0, M_QUARTER), (M_QUARTER, M_HALF), (M_HALF, M))
-        z_last = [place(f"z_last{u}", [P, PACK * (hi - lo)], BF16, AT["table2"] + 2 * PACK * lo) for u, (lo, hi) in enumerate(spans)]
+        first_mx = quantize("z_first", z_first[:], AT["z_codes"], AT["gain7"])
+        spans = ((0, QUARTER), (QUARTER, HALF), (HALF, M))
+        z_last = [place(f"z_last{u}", [P, PACK * (hi - lo)], BF16, AT["planes"] + 8 * KIB + 2 * PACK * lo)
+                  for u, (lo, hi) in enumerate(spans)]
 
-        def join_z(m0, m1, t0, t1):
-            u = min(m0 // M_QUARTER, 2)
-            first = m0 - spans[u][0]
-            nc.scalar.copy(
-                out=z_last[u][:].rearrange("p (m t) -> p m t", t=PACK)[:, first : first + m1 - m0, t0:t1],
-                in_=z_dealt[:].rearrange("p (t m) -> p m t", t=PACK)[:, m0:m1, t0:t1],
-            )
+        def z_columns(lo, hi):
+            u = min(lo // QUARTER, 2)
+            first = lo - spans[u][0]
+            return z_last[u][:].rearrange("p (m t) -> p m t", t=PACK)[:, first : first + hi - lo, :]
 
         for lo, hi in spans:
-            join_z(lo, hi, 0, PACK - 1)
-        scatter(LAST, h[:, 0:LAST_CUT], 0, LAST_CUT)
-        codes_first = place("z_codes_first", [P, M], U32, AT["table0"])
-        scales_first = place("z_scales_first", [P, M], U8, AT["z_scales"])
-        nc.vector.quantize_mx(out=codes_first[:].bitcast(FP8X4), scales=scales_first[:], in_=z_first[:])
-        scatter(LAST, h[:, LAST_CUT:S], LAST_CUT, S)
+            nc.scalar.copy(
+                out=z_columns(lo, hi)[:, :, 0 : PACK - 1],
+                in_=z_dealt[:].rearrange("p (t m) -> p m t", t=PACK - 1)[:, lo:hi, :],
+            )
+        scatter(LAST, h[:, LAST_CUT:S], wgs_rows[LAST], LAST_CUT, S)
 
-        z_half = {}
-
-        def z_operand(a, lo, hi):
-            if a == 0:
-                return codes_first[:, lo:hi], scales_first[:, lo:hi]
-            half, first = divmod(lo, M_HALF)
-            codes, scales = z_half[half]
-            return codes[:, first : first + hi - lo], scales[:, first : first + hi - lo]
+        z_half = [(place(f"z_codes{half}", [P, HALF], U32, AT["gain2"] + half * 2 * KIB),
+                   place(f"z_scales{half}", [P, HALF], U8, AT["gain2"] + half * 2 * KIB + KIB)) for half in range(2)]
 
         def multiply(acc, which, n, a, lo, hi, start, stop):
             if which == 0:
                 codes = wa_codes[:, a, 2 * n * P : 2 * (n + 1) * P].bitcast(FP4X4)
                 scales = wa_scale_tile[:, a, n * P : (n + 1) * P]
             else:
-                piece, sub = divmod(n, WB_PIECE // P)
-                codes = wb_codes[a, piece][:, sub * P : (sub + 1) * P].bitcast(FP8X4)
-                scales = wb_scales[a, piece][:, sub * P : (sub + 1) * P]
-            moving, moving_scales = z_operand(a, lo, hi)
+                codes, scales = wb_mx[a, n]
+                codes = codes.bitcast(FP8X4)
+            if a == 0:
+                moving, moving_scales = first_mx[0][:, lo:hi], first_mx[1][:, lo:hi]
+            else:
+                half, first = divmod(lo, HALF)
+                moving = z_half[half][0][:, first : first + hi - lo]
+                moving_scales = z_half[half][1][:, first : first + hi - lo]
             nc.tensor.matmul_mx(
                 out=acc, lhsT=codes, lhsT_scale=scales, rhs=moving.bitcast(FP8X4), rhs_scale=moving_scales,
                 start=start, stop=stop,
             )
 
-        paired = {(half, which): bank(2 * half + which) for half in range(2) for which in range(2)}
-        whole = {(n, which): bank(2 * n + which) for n in (2, 3) for which in range(2)}
-        for half in range(2):
-            for which in range(2):
-                for n in range(2):
-                    acc = paired[half, which][:, n * M_HALF : (n + 1) * M_HALF]
-                    multiply(acc, which, n, 0, half * M_HALF, (half + 1) * M_HALF, n == 0, False)
-        for n in (2, 3):
-            for which in range(2):
-                multiply(whole[n, which][:], which, n, 0, 0, M, True, False)
+        def pair_pass(acc, which, pair, a, lo, hi, start, stop):
+            first = lo % HALF
+            for u in range(2):
+                multiply(acc[:, u * HALF + first : u * HALF + first + hi - lo], which, 2 * pair + u, a, lo, hi,
+                         start and u == 0, stop and u == 1)
 
-        late_scales = place("wb_scales_late", [P, 4, WB_PIECE], U8, AT["wb_scales"])
-        late_at = {(1, 0): AT["codes6"], (1, 1): AT["table2"], (0, 2): AT["table2"] + KIB,
-                   (1, 2): AT["plane7"] + 512 + KIB}
+        EARLY = ((0, 0, 0), (1, 0, 0), (0, 1, 0), (0, 2, 0), (0, 0, 1), (1, 0, 1), (0, 2, 1), (0, 1, 1))
+        sums = {}
+        for b, key in enumerate(EARLY):
+            which, pair, half = key
+            sums[key] = bank(b)
+            pair_pass(sums[key], which, pair, 0, half * HALF, (half + 1) * HALF, True, False)
 
-        def quantize_late(key):
-            wb_scales[key] = late_scales[:, list(late_at).index(key), :]
-            wb_codes[key] = place(f"wb_codes{key[0]}{key[1]}", [P, WB_PIECE], U32, late_at[key])[:]
-            quantize_wb(*key)
-
-        quantize_late((1, 0))
-        x = z_rows(LAST)
-        for lo in range(0, M, M_QUARTER):
-            gather(x, LAST, lo, lo + M_QUARTER)
-            join_z(lo, lo + M_QUARTER, PACK - 1, PACK)
-        z_half[0] = (place("z_codes_front", [P, M_HALF], U32, AT["z_codes_front"]),
-                     place("z_scales_front", [P, M_HALF], U8, AT["z_scales"] + M))
-        for u in range(2):
+        def quantize_z(u):
             lo, hi = spans[u]
-            nc.vector.quantize_mx(out=z_half[0][0][:, lo:hi].bitcast(FP8X4), scales=z_half[0][1][:, lo:hi], in_=z_last[u][:])
-            for which in range(2):
-                for n in range(2):
-                    acc = paired[0, which][:, n * M_HALF + lo : n * M_HALF + hi]
-                    multiply(acc, which, n, 1, lo, hi, False, u == 1 and n == 1)
-        quantize_late((1, 1))
-        for which in range(2):
-            for n in (2, 3):
-                multiply(whole[n, which][:, 0:M_HALF], which, n, 1, 0, M_HALF, False, False)
-        quantize_late((0, 2))
-        z_half[1] = (place("z_codes_back", [P, M_HALF], U32, AT["plane7"] + 512),
-                     place("z_scales_back", [P, M_HALF], U8, AT["z_scales"] + M + M_HALF))
-        nc.vector.quantize_mx(out=z_half[1][0][:].bitcast(FP8X4), scales=z_half[1][1][:], in_=z_last[2][:])
-        quantize_late((1, 2))
+            half, first = divmod(lo, HALF)
+            codes, scales = z_half[half]
+            nc.vector.quantize_mx(out=codes[:, first : first + hi - lo].bitcast(FP8X4),
+                                  scales=scales[:, first : first + hi - lo], in_=z_last[u][:])
 
-        done = []
+        x_last_at = AT["z_dealt"] + 6 * KIB
+        x_last = {}
 
-        def finish(sum_a, sum_b, rows):
-            width = sum_a.shape[1]
-            ya = place(f"ya{len(done)}", [P, width], F32, AT["v01"] + sum(done) * 4)
+        def last_quarter(u):
+            lo, hi = u * QUARTER, (u + 1) * QUARTER
+            x = place(f"x_last{u}", [P, QUARTER], F32, x_last_at + 4 * lo)
+            x_last[u] = x
+            nc.vector.tensor_tensor(x[:], pages[LAST % 2][:].indirect(entries(idx3, lo, hi)), sess_tiles[LAST][:, lo:hi], ALU.add)
+            nc.scalar.copy(out=z_columns(lo, hi)[:, :, PACK - 1], in_=x[:])
+
+        copied, done = {}, []
+
+        def copy_out(pair, half):
+            ya = place(f"ya{pair}{half}", [P, BANK], F32, AT["v01"] + len(copied) * 2 * KIB)
+            copied[pair, half] = ya
+            nc.scalar.copy(out=ya[:], in_=sums[0, pair, half][:])
+
+        def finish(sum_b, ya, rows):
+            width = sum_b.shape[1]
             best = place(f"best{len(done)}", [P, width], F32, AT["wide"] + sum(done) * 4)
             done.append(width)
-            nc.scalar.copy(out=ya[:], in_=sum_a)
-            nc.vector.tensor_tensor(best[:], sum_b, ya[:], ALU.max)
+            nc.vector.tensor_tensor(best[:], sum_b, ya, ALU.max)
             if len(rows.shape) == 3:
                 nc.sync.dma_start(out=rows, in_=best[:].rearrange("p (n m) -> p n m", n=2))
             else:
                 nc.sync.dma_start(out=rows, in_=best[:])
+            return best
 
-        def pair_rows(half):
-            return out[0 : 2 * P, half * M_HALF : (half + 1) * M_HALF].rearrange("(n p) m -> p n m", p=P)
+        def finish_pair(pair, half):
+            rows = out[pair * PAIR : (pair + 1) * PAIR, half * HALF : (half + 1) * HALF]
+            return finish(sums[1, pair, half][:], copied[pair, half][:], rows.rearrange("(n p) m -> p n m", p=P))
 
-        finish(paired[0, 0][:], paired[0, 1][:], pair_rows(0))
-        for which in range(2):
-            for n in range(2):
-                multiply(paired[1, which][:, n * M_HALF : (n + 1) * M_HALF], which, n, 1, M_HALF, M, False, n == 1)
-        finish(paired[1, 0][:], paired[1, 1][:], pair_rows(1))
-        for n in (2, 3):
-            for which in range(2):
-                multiply(whole[n, which][:, M_HALF:M], which, n, 1, M_HALF, M, False, True)
-            finish(whole[n, 0][:], whole[n, 1][:], out[n * P : (n + 1) * P, :])
-        sums = [bank(which) for which in range(2)]
-        for which in range(2):
-            multiply(sums[which][:], which, 4, 0, 0, M, True, False)
-            for lo in range(0, M, M_HALF):
-                multiply(sums[which][:, lo : lo + M_HALF], which, 4, 1, lo, lo + M_HALF, False, lo > 0)
-        finish(sums[0][:], sums[1][:], out[4 * P : 5 * P, :])
-        last_a = bank(2)
-        multiply(last_a[:], 0, 5, 0, 0, M, True, False)
-        for lo in range(0, M, M_HALF):
-            multiply(last_a[:, lo : lo + M_HALF], 0, 5, 1, lo, lo + M_HALF, False, lo > 0)
-        for half in range(2):
-            lo = half * M_HALF
-            last_b = bank(3 + half, M_HALF)
+        def late_pair(b, pair, half):
+            sums[1, pair, half] = bank(b)
             for a in range(R_PASSES):
-                multiply(last_b[:], 1, 5, a, lo, lo + M_HALF, a == 0, a == 1)
-            finish(last_a[:, lo : lo + M_HALF], last_b[:], out[5 * P : 6 * P, lo : lo + M_HALF])
+                pair_pass(sums[1, pair, half], 1, pair, a, half * HALF, (half + 1) * HALF, a == 0, a == 1)
+
+        wb_codes_at = AT["planes"]
+        quantize_wb(1, 0, PAIR, wb_codes_at, AT["gain7"] + 512)
+        for u in range(3):
+            last_quarter(u)
+        quantize_z(0)
+        for key in EARLY[0:2]:
+            pair_pass(sums[key], key[0], key[1], 1, 0, QUARTER, False, False)
+        last_quarter(3)
+        quantize_z(1)
+        for key in EARLY[0:2]:
+            pair_pass(sums[key], key[0], key[1], 1, QUARTER, HALF, False, True)
+        for pair in (1, 2):
+            pair_pass(sums[0, pair, 0], 0, pair, 1, 0, HALF, False, True)
+        copy_out(0, 0)
+        copy_out(1, 0)
+        quantize_wb(0, PAIR, N, wb_codes_at + KIB, x_last_at + 4 * QUARTER)
+        quantize_z(2)
+        pair_pass(sums[0, 0, 1], 0, 0, 1, HALF, M, False, True)
+        quantize_wb(1, PAIR, 2 * PAIR, wb_codes_at + 3 * KIB, x_last_at + 12 * QUARTER)
+        finish_pair(0, 0)
+        late_pair(0, 1, 0)
+        pair_pass(sums[1, 0, 1], 1, 0, 1, HALF, M, False, True)
+        copy_out(0, 1)
+        quantize_wb(1, 2 * PAIR, N, wb_codes_at + 4 * KIB, x_last_at + 12 * QUARTER + PAIR)
+        finish_pair(1, 0)
+        late_pair(2, 2, 0)
+        copy_out(2, 0)
+        finish_pair(0, 1)
+        for pair in (2, 1):
+            pair_pass(sums[0, pair, 1], 0, pair, 1, HALF, M, False, True)
+            copy_out(pair, 1)
+        finish_pair(2, 0)
+        for b, n in zip((1, 4, 0, 5), (4, 5, 2, 3)):
+            acc = bank(b, HALF)
+            for a in range(R_PASSES):
+                multiply(acc[:], 1, n, a, HALF, M, a == 0, a == 1)
+            u = n % 2
+            finish(acc[:], copied[n // 2, 1][:, u * HALF : (u + 1) * HALF], out[n * P : (n + 1) * P, HALF:M])

@@ -398,12 +398,16 @@ def tile_list_session_slot_verdict_kernel(
                 multiply(acc[:, u * HALF + first : u * HALF + first + hi - lo], which, 2 * pair + u, a, lo, hi,
                          start and u == 0, stop and u == 1)
 
-        EARLY = ((0, 0, 0), (1, 0, 0), (0, 1, 0), (0, 2, 0), (0, 0, 1), (1, 0, 1), (0, 2, 1), (0, 1, 1))
-        sums = {}
-        for b, key in enumerate(EARLY):
-            which, pair, half = key
-            sums[key] = bank(b)
-            pair_pass(sums[key], which, pair, 0, half * HALF, (half + 1) * HALF, True, False)
+        pair_sums, row_sums = {}, {}
+        for half in range(2):
+            for which in range(2):
+                acc = bank(6 * half + which)
+                pair_sums[which, half] = acc
+                pair_pass(acc, which, 0, 0, half * HALF, (half + 1) * HALF, True, False)
+            if half == 0:
+                for n in range(2, N // P):
+                    row_sums[n] = bank(n)
+                    multiply(row_sums[n][:], 0, n, 0, 0, M, True, False)
 
         def quantize_z(u):
             lo, hi = spans[u]
@@ -422,68 +426,47 @@ def tile_list_session_slot_verdict_kernel(
             nc.vector.tensor_tensor(x[:], pages[LAST % 2][:].indirect(entries(idx3, lo, hi)), sess_tiles[LAST][:, lo:hi], ALU.add)
             nc.scalar.copy(out=z_columns(lo, hi)[:, :, PACK - 1], in_=x[:])
 
-        copied, done = {}, []
+        copied = []
 
-        def copy_out(pair, half):
-            ya = place(f"ya{pair}{half}", [P, BANK], F32, AT["v01"] + len(copied) * 2 * KIB)
-            copied[pair, half] = ya
-            nc.scalar.copy(out=ya[:], in_=sums[0, pair, half][:])
+        def finish(sum_a, sum_b, rows):
+            ya = place(f"ya{len(copied)}", [P, BANK], F32, AT["v01"] + len(copied) * 2 * KIB)
+            best = place(f"best{len(copied)}", [P, BANK], F32, AT["wide"] + len(copied) * 2 * KIB)
+            copied.append(ya)
+            nc.scalar.copy(out=ya[:], in_=sum_a[:])
+            nc.vector.tensor_tensor(best[:], sum_b[:], ya[:], ALU.max)
+            nc.sync.dma_start(out=rows, in_=best[:].rearrange("p (n m) -> p n m", m=rows.shape[2]))
 
-        def finish(sum_b, ya, rows):
-            width = sum_b.shape[1]
-            best = place(f"best{len(done)}", [P, width], F32, AT["wide"] + sum(done) * 4)
-            done.append(width)
-            nc.vector.tensor_tensor(best[:], sum_b, ya, ALU.max)
-            if len(rows.shape) == 3:
-                nc.sync.dma_start(out=rows, in_=best[:].rearrange("p (n m) -> p n m", n=2))
-            else:
-                nc.sync.dma_start(out=rows, in_=best[:])
-            return best
-
-        def finish_pair(pair, half):
-            rows = out[pair * PAIR : (pair + 1) * PAIR, half * HALF : (half + 1) * HALF]
-            return finish(sums[1, pair, half][:], copied[pair, half][:], rows.rearrange("(n p) m -> p n m", p=P))
-
-        def late_pair(b, pair, half):
-            sums[1, pair, half] = bank(b)
-            for a in range(R_PASSES):
-                pair_pass(sums[1, pair, half], 1, pair, a, half * HALF, (half + 1) * HALF, a == 0, a == 1)
+        def finish_pair(half):
+            rows = out[0:PAIR, half * HALF : (half + 1) * HALF].rearrange("(n p) m -> p n m", p=P)
+            finish(pair_sums[0, half], pair_sums[1, half], rows)
 
         wb_codes_at = AT["planes"]
         quantize_wb(1, 0, PAIR, wb_codes_at, AT["gain7"] + 512)
         for u in range(3):
             last_quarter(u)
         quantize_z(0)
-        for key in EARLY[0:2]:
-            pair_pass(sums[key], key[0], key[1], 1, 0, QUARTER, False, False)
+        for which in range(2):
+            pair_pass(pair_sums[which, 0], which, 0, 1, 0, QUARTER, False, False)
         last_quarter(3)
         quantize_z(1)
-        for key in EARLY[0:2]:
-            pair_pass(sums[key], key[0], key[1], 1, QUARTER, HALF, False, True)
-        for pair in (1, 2):
-            pair_pass(sums[0, pair, 0], 0, pair, 1, 0, HALF, False, True)
-        copy_out(0, 0)
-        copy_out(1, 0)
+        for which in range(2):
+            pair_pass(pair_sums[which, 0], which, 0, 1, QUARTER, HALF, False, True)
+        for n in row_sums:
+            multiply(row_sums[n][:, 0:HALF], 0, n, 1, 0, HALF, False, False)
         quantize_wb(0, PAIR, N, wb_codes_at + KIB, x_last_at + 4 * QUARTER)
         quantize_z(2)
-        pair_pass(sums[0, 0, 1], 0, 0, 1, HALF, M, False, True)
+        for which in range(2):
+            pair_pass(pair_sums[which, 1], which, 0, 1, HALF, M, False, True)
+        for n in row_sums:
+            multiply(row_sums[n][:, HALF:M], 0, n, 1, HALF, M, False, True)
         quantize_wb(1, PAIR, 2 * PAIR, wb_codes_at + 3 * KIB, x_last_at + 12 * QUARTER)
-        finish_pair(0, 0)
-        late_pair(0, 1, 0)
-        pair_pass(sums[1, 0, 1], 1, 0, 1, HALF, M, False, True)
-        copy_out(0, 1)
+        finish_pair(0)
         quantize_wb(1, 2 * PAIR, N, wb_codes_at + 4 * KIB, x_last_at + 12 * QUARTER + PAIR)
-        finish_pair(1, 0)
-        late_pair(2, 2, 0)
-        copy_out(2, 0)
-        finish_pair(0, 1)
-        for pair in (2, 1):
-            pair_pass(sums[0, pair, 1], 0, pair, 1, HALF, M, False, True)
-            copy_out(pair, 1)
-        finish_pair(2, 0)
-        for b, n in zip((1, 4, 0, 5), (4, 5, 2, 3)):
-            acc = bank(b, HALF)
-            for a in range(R_PASSES):
-                multiply(acc[:], 1, n, a, HALF, M, a == 0, a == 1)
-            u = n % 2
-            finish(acc[:], copied[n // 2, 1][:, u * HALF : (u + 1) * HALF], out[n * P : (n + 1) * P, HALF:M])
+        finish_pair(1)
+        for b, n in zip((0, 1, 6, 2), row_sums):
+            late = bank(b)
+            multiply(late[:], 1, n, 0, 0, M, True, False)
+            for half in range(2):
+                lo, hi = half * HALF, (half + 1) * HALF
+                multiply(late[:, lo:hi], 1, n, 1, lo, hi, False, half == 1)
+            finish(row_sums[n], late, out[n * P : (n + 1) * P, :].rearrange("(o p) m -> p o m", o=1))

@@ -36,6 +36,7 @@ PAIR = 2 * P
 FIRST_CUT = 256
 LAST_CUT = 640
 W1_CODES = K_PASSES * P
+PAGES = 3
 
 KIB = 1024
 SIZES = (
@@ -47,7 +48,7 @@ SIZES = (
     ("gain2", 6 * KIB), ("gain3", 6 * KIB), ("gain4", 6 * KIB), ("gain5", 6 * KIB), ("gain6", 4 * KIB),
     ("gain7", 2 * KIB), ("z_codes", 2 * KIB), ("front", 4 * KIB), ("back", 6 * KIB), ("z_dealt", 8 * KIB),
     ("planes", 16 * KIB), ("sess", 16 * KIB), ("wa", 3 * KIB), ("wa_scales", 1536),
-    ("ident", 512), ("gain_rows", 512), ("gain_col", ALIGN), ("warm", ALIGN),
+    ("wb_raw0", 12 * KIB), ("ident", 512), ("gain_rows", 512), ("gain_col", ALIGN), ("warm", ALIGN),
 )
 AT = {name: sum(size for other, size in SIZES[:i]) for i, (name, width) in enumerate(SIZES)}
 
@@ -195,6 +196,8 @@ def tile_list_session_slot_verdict_kernel(
         for page in pages:
             nc.vector.memset(page[:].bitcast(I32), 0)
         nc.vector.tensor_copy(v_words[1][:], table_words[1][:].indirect(idx[:]))
+        pages.append(place("page2", [P, T2], F32, AT["table1"]))
+        nc.vector.memset(pages[2][:].bitcast(I32), 0)
         v_scales = place("v_scales", [P, S], U8, AT["table1"] + 12 * KIB)
         nc.vector.tensor_copy(v_scales[:], table_scales[:].indirect(idx[:]))
 
@@ -241,10 +244,10 @@ def tile_list_session_slot_verdict_kernel(
             nc.scalar.activation(out=dst, in_=src, func=ACT.Copy, scale=column)
 
         def scatter(c, h, weights, lo, hi):
-            nc.vector.tensor_tensor(pages[c % 2][:].indirect(entries(idx2, lo, hi)), h, weights[:, lo:hi], ALU.mult)
+            nc.vector.tensor_tensor(pages[c % PAGES][:].indirect(entries(idx2, lo, hi)), h, weights[:, lo:hi], ALU.mult)
 
         def gather(x, c, lo, hi):
-            nc.vector.tensor_tensor(x[:, lo:hi], pages[c % 2][:].indirect(entries(idx3, lo, hi)), sess_tiles[c][:, lo:hi], ALU.add)
+            nc.vector.tensor_tensor(x[:, lo:hi], pages[c % PAGES][:].indirect(entries(idx3, lo, hi)), sess_tiles[c][:, lo:hi], ALU.add)
 
         group_w1(0, AT["grouped0"])
         quantize_w1(0, AT["codes0"])
@@ -252,7 +255,7 @@ def tile_list_session_slot_verdict_kernel(
         for lo, hi in ((0, FIRST_CUT), (FIRST_CUT, S)):
             nc.vector.tensor_copy(v_words[2][:, lo:hi], table_words[2][:].indirect(entries(idx, lo, hi)))
 
-        wb_raw = [load_wb(0, AT["table1"])]
+        wb_raw = [load_wb(0, AT["wb_raw0"])]
         load_sess(2, NATURAL)
         load_plane(4)
         wb_raw.append(load_wb(1, AT["table2"] + 4 * KIB))
@@ -307,7 +310,7 @@ def tile_list_session_slot_verdict_kernel(
 
         z_dealt = place("z_dealt", [P, (PACK - 1) * M], F32, AT["z_dealt"])
         H_AT = {2: AT["raw3"] + 2 * KIB, 3: AT["h_odd"], 4: AT["raw3"] + 2 * KIB, 5: AT["wide"],
-                6: AT["table1"], 7: AT["z_natural"] - 2 * KIB}
+                6: AT["wb_raw0"], 7: AT["z_natural"] - 2 * KIB}
         wb_grouped, wb_mx = {}, {}
 
         def group_wb(a, offset):
@@ -423,7 +426,7 @@ def tile_list_session_slot_verdict_kernel(
             lo, hi = u * QUARTER, (u + 1) * QUARTER
             x = place(f"x_last{u}", [P, QUARTER], F32, x_last_at + 4 * lo)
             x_last[u] = x
-            nc.vector.tensor_tensor(x[:], pages[LAST % 2][:].indirect(entries(idx3, lo, hi)), sess_tiles[LAST][:, lo:hi], ALU.add)
+            nc.vector.tensor_tensor(x[:], pages[LAST % PAGES][:].indirect(entries(idx3, lo, hi)), sess_tiles[LAST][:, lo:hi], ALU.add)
             nc.scalar.copy(out=z_columns(lo, hi)[:, :, PACK - 1], in_=x[:])
 
         copied = []

@@ -44,7 +44,7 @@ SIZES = (
     ("v01", 8 * KIB), ("table_scales", 4 * KIB),
     ("grouped0", 3 * KIB), ("codes0", 3 * KIB), ("wgs", 4 * KIB), ("weights0", 4 * KIB), ("h0", 2 * KIB),
     ("raw1", 6 * KIB), ("grouped2", 3 * KIB), ("codes1", 3 * KIB),
-    ("raw2", 6 * KIB), ("h_odd", 4 * KIB), ("codes2", 2 * KIB), ("raw3", 6 * KIB), ("wide", 24 * KIB),
+    ("raw2", 6 * KIB), ("h_odd", 4 * KIB), ("codes2", 2 * KIB), ("raw3", 6 * KIB), ("pages", 24 * KIB),
     ("gain2", 6 * KIB), ("gain3", 6 * KIB), ("gain4", 6 * KIB), ("gain5", 6 * KIB), ("gain6", 4 * KIB),
     ("gain7", 2 * KIB), ("z_codes", 2 * KIB), ("front", 4 * KIB), ("back", 6 * KIB), ("z_dealt", 8 * KIB),
     ("planes", 16 * KIB), ("sess", 16 * KIB), ("wa", 3 * KIB), ("wa_scales", 1536),
@@ -119,7 +119,7 @@ def tile_list_session_slot_verdict_kernel(
             return tiles
 
         def load_wide(a):
-            wide = place(f"w1_wide{a}", [P, PACK, PASS], F32, AT["wide"] + a * 8 * KIB)
+            wide = place(f"w1_wide{a}", [P, PACK, PASS], F32, AT["table0"] + a * 8 * KIB)
             rows = w1[a * PASS : (a + 1) * PASS, PASS:H]
             nc.sync.dma_start(out=wide[:], in_=rows.rearrange("(p i) c -> p i c", i=PACK))
             return wide
@@ -164,23 +164,23 @@ def tile_list_session_slot_verdict_kernel(
         idx = lists.tile([P, S // LIST_ROWS], U16)
         nc.sync.dma_start(idx[:], offs)
         table_words.append(load_table(1))
-        nc.sync.dma_start(out=gain_rows[0:2, :], in_=gain[0 : 2 * P].rearrange("(c p) -> c p", p=P))
         w1_raw = [load_w1(0, AT["z_natural"])]
+        idx2 = lists.tile([P, S // LIST_ROWS], U16)
+        nc.sync.dma_start(idx2[:], offs2)
+        idx3 = lists.tile([P, M // LIST_ROWS], U16)
+        nc.sync.dma_start(idx3[:], offs3)
+        nc.sync.dma_start(out=gain_rows[0:2, :], in_=gain[0 : 2 * P].rearrange("(c p) -> c p", p=P))
+        load_gain(2)
         table_words.append(load_table(2))
         wgs_tile = place("wgs_tile", [P, S], F32, AT["wgs"])
         for lo in range(0, S, BANK):
             nc.sync.dma_start(out=wgs_tile[:, lo : lo + BANK], in_=wgs[:, lo : lo + BANK])
         for c in range(NATURAL):
             wgs_rows[c] = wgs_tile
-        idx2 = lists.tile([P, S // LIST_ROWS], U16)
-        nc.sync.dma_start(idx2[:], offs2)
         w1_raw.append(load_w1(1, AT["raw1"]))
-        idx3 = lists.tile([P, M // LIST_ROWS], U16)
-        nc.sync.dma_start(idx3[:], offs3)
         w1_raw.append(load_w1(2, AT["raw2"]))
         load_sess(0, 1)
         w1_raw.append(load_w1(3, AT["raw3"]))
-        load_gain(2)
         w1_wide = [load_wide(a) for a in range(K_PASSES)]
         load_sess(1, 2)
         load_gain(3)
@@ -192,12 +192,10 @@ def tile_list_session_slot_verdict_kernel(
 
         v_words = [place(f"v_words{a}", [P, S], U32, AT["v01"] + a * 4 * KIB) for a in range(2)]
         nc.vector.tensor_copy(v_words[0][:], table_words[0][:].indirect(idx[:]))
-        pages = [place(f"page{u}", [P, T2], F32, AT["table0"] + u * 8 * KIB) for u in range(2)]
+        pages = [place(f"page{u}", [P, T2], F32, AT["pages"] + u * 8 * KIB) for u in range(PAGES)]
         for page in pages:
             nc.vector.memset(page[:].bitcast(I32), 0)
         nc.vector.tensor_copy(v_words[1][:], table_words[1][:].indirect(idx[:]))
-        pages.append(place("page2", [P, T2], F32, AT["table1"]))
-        nc.vector.memset(pages[2][:].bitcast(I32), 0)
         v_scales = place("v_scales", [P, S], U8, AT["table1"] + 12 * KIB)
         nc.vector.tensor_copy(v_scales[:], table_scales[:].indirect(idx[:]))
 
@@ -272,7 +270,7 @@ def tile_list_session_slot_verdict_kernel(
         load_plane(7)
 
         cuts = (0, FIRST_CUT, BANK, S)
-        first_sums = [multiply_w1(0, b, lo, hi) for b, lo, hi in zip((0, 1, 6), cuts, cuts[1:])]
+        first_sums = [multiply_w1(0, u, cuts[u], cuts[u + 1]) for u in range(2)]
         weights = place("weights0", [P, S], F32, AT["weights0"])
         for lo in range(0, S, BANK):
             scale(weights[:, lo : lo + BANK], wgs_tile[:, lo : lo + BANK], gain_col[:, 0:1])
@@ -281,10 +279,11 @@ def tile_list_session_slot_verdict_kernel(
             lo, hi = cuts[u], cuts[u + 1]
             gelu(h_front[:, lo:hi], first_sums[u])
             scatter(0, h_front[:, lo:hi], weights, lo, hi)
-        group_w1(1, AT["codes0"])
+        last_sum = multiply_w1(0, 0, BANK, S)
+        group_w1(1, AT["grouped0"])
         quantize_w1(1, AT["codes1"])
         h_back = place("h0_back", [P, BANK], F32, AT["raw1"] + 4 * KIB)
-        gelu(h_back[:], first_sums[2])
+        gelu(h_back[:], last_sum)
         scatter(0, h_back[:], weights, BANK, S)
         group_w1(2, AT["grouped2"])
         quantize_w1(2, AT["codes2"])
@@ -309,7 +308,7 @@ def tile_list_session_slot_verdict_kernel(
         group_w1(3, AT["codes1"])
 
         z_dealt = place("z_dealt", [P, (PACK - 1) * M], F32, AT["z_dealt"])
-        H_AT = {2: AT["raw3"] + 2 * KIB, 3: AT["h_odd"], 4: AT["raw3"] + 2 * KIB, 5: AT["wide"],
+        H_AT = {2: AT["raw3"] + 2 * KIB, 3: AT["h_odd"], 4: AT["raw3"] + 2 * KIB, 5: AT["table0"],
                 6: AT["wb_raw0"], 7: AT["z_natural"] - 2 * KIB}
         wb_grouped, wb_mx = {}, {}
 
@@ -433,7 +432,7 @@ def tile_list_session_slot_verdict_kernel(
 
         def finish(sum_a, sum_b, rows):
             ya = place(f"ya{len(copied)}", [P, BANK], F32, AT["v01"] + len(copied) * 2 * KIB)
-            best = place(f"best{len(copied)}", [P, BANK], F32, AT["wide"] + len(copied) * 2 * KIB)
+            best = place(f"best{len(copied)}", [P, BANK], F32, AT["table0"] + len(copied) * 2 * KIB)
             copied.append(ya)
             nc.scalar.copy(out=ya[:], in_=sum_a[:])
             nc.vector.tensor_tensor(best[:], sum_b[:], ya[:], ALU.max)

@@ -107,14 +107,16 @@ def tile_list_session_slot_verdict_kernel(
             nc.sync.dma_start(out=words[:].bitcast(I32), in_=tab_words[a].rearrange("p t i -> p (t i)").bitcast(I32))
             return words
 
-        def load_w1(c, offset):
+        def load_w1(c, offset, parts=1):
             tiles = []
             for a in range(K_PASSES):
                 spare = ALIGN // 4 if c in (1, 2) and a == K_PASSES - 1 else 0
                 raw = place(f"w1_raw{c}_{a}", [P, PASS + spare], F32, offset + a * 2 * KIB)[:, 0:PASS]
                 raw = raw.rearrange("p (i c) -> p i c", i=PACK)
                 rows = w1[a * PASS : (a + 1) * PASS, c * P : (c + 1) * P]
-                nc.sync.dma_start(out=raw, in_=rows.rearrange("(p i) c -> p i c", i=PACK))
+                rows = rows.rearrange("(p i) c -> p i c", i=PACK)
+                for lo in range(0, P, P // parts):
+                    nc.sync.dma_start(out=raw[:, :, lo : lo + P // parts], in_=rows[:, :, lo : lo + P // parts])
                 tiles.append(raw)
             return tiles
 
@@ -164,14 +166,11 @@ def tile_list_session_slot_verdict_kernel(
         idx = lists.tile([P, S // LIST_ROWS], U16)
         nc.sync.dma_start(idx[:], offs)
         table_words.append(load_table(1))
-        w1_raw = [load_w1(0, AT["z_natural"])]
+        w1_raw = [load_w1(0, AT["z_natural"], 2)]
+        nc.sync.dma_start(out=gain_rows[0:2, :], in_=gain[0 : 2 * P].rearrange("(c p) -> c p", p=P))
+        table_words.append(load_table(2))
         idx2 = lists.tile([P, S // LIST_ROWS], U16)
         nc.sync.dma_start(idx2[:], offs2)
-        idx3 = lists.tile([P, M // LIST_ROWS], U16)
-        nc.sync.dma_start(idx3[:], offs3)
-        nc.sync.dma_start(out=gain_rows[0:2, :], in_=gain[0 : 2 * P].rearrange("(c p) -> c p", p=P))
-        load_gain(2)
-        table_words.append(load_table(2))
         wgs_tile = place("wgs_tile", [P, S], F32, AT["wgs"])
         for lo in range(0, S, BANK):
             nc.sync.dma_start(out=wgs_tile[:, lo : lo + BANK], in_=wgs[:, lo : lo + BANK])
@@ -179,8 +178,11 @@ def tile_list_session_slot_verdict_kernel(
             wgs_rows[c] = wgs_tile
         w1_raw.append(load_w1(1, AT["raw1"]))
         w1_raw.append(load_w1(2, AT["raw2"]))
+        idx3 = lists.tile([P, M // LIST_ROWS], U16)
+        nc.sync.dma_start(idx3[:], offs3)
         load_sess(0, 1)
         w1_raw.append(load_w1(3, AT["raw3"]))
+        load_gain(2)
         w1_wide = [load_wide(a) for a in range(K_PASSES)]
         load_sess(1, 2)
         load_gain(3)

@@ -107,7 +107,7 @@ def tile_list_session_slot_verdict_kernel(
             nc.sync.dma_start(out=words[:].bitcast(I32), in_=tab_words[a].rearrange("p t i -> p (t i)").bitcast(I32))
             return words
 
-        def load_w1(c, offset, parts=1):
+        def load_w1(c, offset, halved=0):
             tiles = []
             for a in range(K_PASSES):
                 spare = ALIGN // 4 if c in (1, 2) and a == K_PASSES - 1 else 0
@@ -115,8 +115,9 @@ def tile_list_session_slot_verdict_kernel(
                 raw = raw.rearrange("p (i c) -> p i c", i=PACK)
                 rows = w1[a * PASS : (a + 1) * PASS, c * P : (c + 1) * P]
                 rows = rows.rearrange("(p i) c -> p i c", i=PACK)
-                for lo in range(0, P, P // parts):
-                    nc.sync.dma_start(out=raw[:, :, lo : lo + P // parts], in_=rows[:, :, lo : lo + P // parts])
+                planes = PACK // 2 if a < halved else PACK
+                for lo in range(0, PACK, planes):
+                    nc.sync.dma_start(out=raw[:, lo : lo + planes, :], in_=rows[:, lo : lo + planes, :])
                 tiles.append(raw)
             return tiles
 
@@ -168,9 +169,9 @@ def tile_list_session_slot_verdict_kernel(
         table_words.append(load_table(1))
         w1_raw = [load_w1(0, AT["z_natural"], 2)]
         nc.sync.dma_start(out=gain_rows[0:2, :], in_=gain[0 : 2 * P].rearrange("(c p) -> c p", p=P))
-        table_words.append(load_table(2))
         idx2 = lists.tile([P, S // LIST_ROWS], U16)
         nc.sync.dma_start(idx2[:], offs2)
+        table_words.append(load_table(2))
         wgs_tile = place("wgs_tile", [P, S], F32, AT["wgs"])
         for lo in range(0, S, BANK):
             nc.sync.dma_start(out=wgs_tile[:, lo : lo + BANK], in_=wgs[:, lo : lo + BANK])
@@ -272,7 +273,7 @@ def tile_list_session_slot_verdict_kernel(
         load_plane(7)
 
         cuts = (0, FIRST_CUT, BANK, S)
-        first_sums = [multiply_w1(0, u, cuts[u], cuts[u + 1]) for u in range(2)]
+        first_sums = [multiply_w1(0, b, lo, hi) for b, lo, hi in zip((0, 1, 6), cuts, cuts[1:])]
         weights = place("weights0", [P, S], F32, AT["weights0"])
         for lo in range(0, S, BANK):
             scale(weights[:, lo : lo + BANK], wgs_tile[:, lo : lo + BANK], gain_col[:, 0:1])
@@ -281,11 +282,10 @@ def tile_list_session_slot_verdict_kernel(
             lo, hi = cuts[u], cuts[u + 1]
             gelu(h_front[:, lo:hi], first_sums[u])
             scatter(0, h_front[:, lo:hi], weights, lo, hi)
-        last_sum = multiply_w1(0, 0, BANK, S)
-        group_w1(1, AT["grouped0"])
+        group_w1(1, AT["codes0"])
         quantize_w1(1, AT["codes1"])
         h_back = place("h0_back", [P, BANK], F32, AT["raw1"] + 4 * KIB)
-        gelu(h_back[:], last_sum)
+        gelu(h_back[:], first_sums[2])
         scatter(0, h_back[:], weights, BANK, S)
         group_w1(2, AT["grouped2"])
         quantize_w1(2, AT["codes2"])

@@ -46,11 +46,12 @@ SIZES = (
     ("raw1", 6 * KIB), ("grouped2", 3 * KIB), ("codes1", 3 * KIB),
     ("raw2", 6 * KIB), ("h_odd", 4 * KIB), ("codes2", 2 * KIB), ("raw3", 6 * KIB), ("pages", 24 * KIB),
     ("gain2", 6 * KIB), ("gain3", 6 * KIB), ("gain4", 6 * KIB), ("gain5", 6 * KIB), ("gain6", 4 * KIB),
-    ("gain7", 2 * KIB), ("z_codes", 2 * KIB), ("front", 4 * KIB), ("back", 6 * KIB), ("z_dealt", 8 * KIB),
+    ("z_codes", 2 * KIB), ("front", 4 * KIB), ("back", 6 * KIB), ("z_dealt", 8 * KIB),
     ("planes", 16 * KIB), ("sess", 16 * KIB), ("wa", 3 * KIB), ("wa_scales", 1536),
     ("wb_raw0", 12 * KIB), ("ident", 512), ("gain_rows", 512), ("gain_col", ALIGN), ("warm", ALIGN),
 )
 AT = {name: sum(size for other, size in SIZES[:i]) for i, (name, width) in enumerate(SIZES)}
+GAIN_AT = {c: AT[f"gain{c}"] if c < LAST else AT["back"] + 4 * KIB for c in range(2, R_TILES)}
 
 
 def interleave(nc, grouped, raw):
@@ -143,7 +144,7 @@ def tile_list_session_slot_verdict_kernel(
 
         def load_gain(c):
             width = PAIR if c == LAST else ALIGN // 4
-            gains[c] = place(f"gain{c}", [P, width], F32, AT[f"gain{c}"])[:, 0:1]
+            gains[c] = place(f"gain{c}", [P, width], F32, GAIN_AT[c])[:, 0:1]
             if c < NATURAL:
                 column = gain[c * P : (c + 1) * P].rearrange("(p o) -> p o", o=1)
             else:
@@ -152,7 +153,7 @@ def tile_list_session_slot_verdict_kernel(
                 nc.sync.dma_start(out=gains[c], in_=column)
 
         def load_plane(c):
-            wgs_rows[c] = place(f"wgs_dealt{c}", [P, S], F32, AT["planes"] + (c - NATURAL) * 4 * KIB)
+            wgs_rows[c] = place(f"wgs_dealt{c}", [P, S], F32, AT["planes"] + (c - NATURAL) * 4 * KIB if c < LAST else AT["back"])
             rows = wgs.rearrange("(p t) j -> p t j", t=PACK)[:, c - NATURAL, :]
             for q in (0, 2, 1, 3):
                 nc.sync.dma_start(out=wgs_rows[c][QUADRANT * q : QUADRANT * (q + 1), :], in_=rows)
@@ -257,20 +258,17 @@ def tile_list_session_slot_verdict_kernel(
             nc.vector.tensor_copy(v_words[2][:, lo:hi], table_words[2][:].indirect(entries(idx, lo, hi)))
 
         wb_raw = [load_wb(0, AT["wb_raw0"])]
-        load_sess(2, NATURAL)
         load_plane(4)
+        load_sess(2, NATURAL)
         wb_raw.append(load_wb(1, AT["table2"] + 4 * KIB))
-        load_sess(NATURAL, R_TILES)
         load_plane(5)
-        wa_codes = place("wa_codes", [P, R_PASSES, 2 * N], U8, AT["wa"])
-        nc.sync.dma_start(out=wa_codes[:].bitcast(I32), in_=wa_words.rearrange("a p n -> p a n").bitcast(I32))
+        load_plane(6)
+        load_sess(NATURAL, R_TILES)
         for q in range(P // QUADRANT):
             nc.sync.dma_start(
                 out=wa_scale_tile[QUADRANT * q : QUADRANT * q + SCALE_ROWS, :, :].bitcast(I32),
                 in_=wa_scales[:, SCALE_ROWS * q : SCALE_ROWS * (q + 1), :].rearrange("a r n -> r a n").bitcast(I32),
             )
-        load_plane(6)
-        load_plane(7)
 
         cuts = (0, FIRST_CUT, BANK, S)
         first_sums = [multiply_w1(0, b, lo, hi) for b, lo, hi in zip((0, 1, 6), cuts, cuts[1:])]
@@ -350,6 +348,11 @@ def tile_list_session_slot_verdict_kernel(
                 pick_natural(c - 1, back)
             else:
                 gather(back, c - 1, 0, M)
+            if c == NATURAL:
+                load_plane(LAST)
+            elif c == 5:
+                wa_codes = place("wa_codes", [P, R_PASSES, 2 * N], U8, AT["planes"] + 5 * KIB)
+                nc.sync.dma_start(out=wa_codes[:].bitcast(I32), in_=wa_words.rearrange("a p n -> p a n").bitcast(I32))
             if c in (2, 3):
                 deal_w1(2 * c, AT[f"gain{c}"])
             elif c in (4, 5):
@@ -358,7 +361,7 @@ def tile_list_session_slot_verdict_kernel(
                 z_first = place("z_first", [P, PACK * M], BF16, AT["gain6"])
                 interleave(nc, z_first[:], z_natural[:].rearrange("p (t m) -> p t m", t=PACK))
 
-        first_mx = quantize("z_first", z_first[:], AT["z_codes"], AT["gain7"])
+        first_mx = quantize("z_first", z_first[:], AT["z_codes"], GAIN_AT[LAST])
         spans = ((0, QUARTER), (QUARTER, HALF), (HALF, M))
         z_last = [place(f"z_last{u}", [P, PACK * (hi - lo)], BF16, AT["planes"] + 8 * KIB + 2 * PACK * lo)
                   for u, (lo, hi) in enumerate(spans)]
@@ -445,7 +448,7 @@ def tile_list_session_slot_verdict_kernel(
             finish(pair_sums[0, half], pair_sums[1, half], rows)
 
         wb_codes_at = AT["planes"]
-        quantize_wb(1, 0, PAIR, wb_codes_at, AT["gain7"] + 512)
+        quantize_wb(1, 0, PAIR, wb_codes_at, GAIN_AT[LAST] + 512)
         for u in range(3):
             last_quarter(u)
         quantize_z(0)

@@ -169,7 +169,7 @@ def tile_list_session_slot_verdict_kernel(
         nc.sync.dma_start(idx[:], offs)
         table_words.append(load_table(1))
         w1_raw = [load_w1(0, AT["z_natural"], 2)]
-        nc.sync.dma_start(out=gain_rows[0:2, :], in_=gain[0 : 2 * P].rearrange("(c p) -> c p", p=P))
+        nc.sync.dma_start(out=gain_rows[0:NATURAL, :], in_=gain[0:PASS].rearrange("(c p) -> c p", p=P))
         idx2 = lists.tile([P, S // LIST_ROWS], U16)
         nc.sync.dma_start(idx2[:], offs2)
         table_words.append(load_table(2))
@@ -184,15 +184,14 @@ def tile_list_session_slot_verdict_kernel(
         nc.sync.dma_start(idx3[:], offs3)
         load_sess(0, 1)
         w1_raw.append(load_w1(3, AT["raw3"]))
-        load_gain(2)
         w1_wide = [load_wide(a) for a in range(K_PASSES)]
-        load_sess(1, 2)
         load_gain(3)
+        load_sess(1, 2)
 
         gain_turned = bank(2, P)
         nc.tensor.transpose(gain_turned[:], gain_rows[:], ident[:])
-        gain_col = place("gain_col", [P, 2], F32, AT["gain_col"])
-        nc.scalar.copy(out=gain_col[:], in_=gain_turned[:, 0:2])
+        gain_col = place("gain_col", [P, NATURAL], F32, AT["gain_col"])
+        nc.scalar.copy(out=gain_col[:], in_=gain_turned[:, 0:NATURAL])
 
         v_words = [place(f"v_words{a}", [P, S], U32, AT["v01"] + a * 4 * KIB) for a in range(2)]
         nc.vector.tensor_copy(v_words[0][:], table_words[0][:].indirect(idx[:]))
@@ -336,8 +335,16 @@ def tile_list_session_slot_verdict_kernel(
             gelu(front[:], multiply_w1(c, 6, 0, BANK))
             gelu(back, multiply_w1(c, 7, BANK, S))
             h = place(f"h{c}", [P, S], F32, H_AT[c])
-            scale(h[:, 0:BANK], front[:], gains[c])
-            scale(h[:, BANK:S], back, gains[c])
+            if c == 2:
+                scale(h[:, 0:BANK], front[:], gain_col[:, c : c + 1])
+                scale(h[:, BANK:S], back, gain_col[:, c : c + 1])
+            elif c == 3:
+                scale(h[:, 0:BANK], front[:], gain_col[:, c : c + 1])
+                scale(h[:, BANK : S - P], back[:, 0 : BANK - P], gain_col[:, c : c + 1])
+                scale(h[:, S - P : S], back[:, BANK - P : BANK], gains[c])
+            else:
+                scale(h[:, 0:BANK], front[:], gains[c])
+                scale(h[:, BANK:S], back, gains[c])
             if c < LAST:
                 quantize_w1(c + 1, front_at)
                 scatter(c, h[:], wgs_rows[c], 0, S)

from contextlib import ExitStack

import concourse.mybir as mybir
from concourse.masks import make_identity

K, H, N, T, S, T2, M = 1536, 1024, 768, 4096, 1024, 2048, 512
FLOPS = 2 * K * H * S + 2 * 2 * H * N * M

F32 = mybir.dt.float32
BF16 = mybir.dt.bfloat16
I32 = mybir.dt.int32
U32 = mybir.dt.uint32
U16 = mybir.dt.uint16
U8 = mybir.dt.uint8
FP8X4 = mybir.dt.float8_e4m3fn_x4
FP4X4 = mybir.dt.float4_e2m1fn_x4
ACT = mybir.ActivationFunctionType
ALU = mybir.AluOpType

P = 128
PACK = 4
PASS = P * PACK
BANK = 512
QUADRANT = 32
SCALE_ROWS = 4
LIST_ROWS = 16
ALIGN = 64
K_PASSES = K // PASS
R_PASSES = H // PASS
R_TILES = H // P
NATURAL = PASS // P
LAST = R_TILES - 1
HALF = M // 2
QUARTER = M // 4
PAIR = 2 * P
FIRST_CUT = 256
LAST_CUT = 640
W1_CODES = K_PASSES * P
PAGES = 3

KIB = 1024
SIZES = (
    ("table0", 16 * KIB), ("table1", 16 * KIB), ("table2", 16 * KIB), ("z_natural", 8 * KIB),
    ("v01", 8 * KIB), ("table_scales", 4 * KIB),
    ("grouped0", 3 * KIB), ("codes0", 3 * KIB), ("wgs", 4 * KIB), ("weights0", 4 * KIB), ("h0", 2 * KIB),
    ("raw1", 6 * KIB), ("grouped2", 3 * KIB), ("codes1", 3 * KIB),
    ("raw2", 6 * KIB), ("h_odd", 4 * KIB), ("codes2", 2 * KIB), ("raw3", 6 * KIB), ("pages", 24 * KIB),
    ("gain2", 6 * KIB), ("gain3", 6 * KIB), ("gain4", 6 * KIB), ("gain5", 6 * KIB), ("gain6", 4 * KIB),
    ("z_codes", 2 * KIB), ("front", 4 * KIB), ("back", 6 * KIB), ("z_dealt", 8 * KIB),
    ("planes", 16 * KIB), ("sess", 16 * KIB), ("wa", 3 * KIB), ("wa_scales", 1536),
    ("wb_raw0", 12 * KIB), ("ident", 512), ("gain_rows", 512), ("gain_col", ALIGN), ("warm", ALIGN),
)
AT = {name: sum(size for other, size in SIZES[:i]) for i, (name, width) in enumerate(SIZES)}
GAIN_AT = {c: AT[f"gain{c}"] if c < LAST else AT["back"] + 4 * KIB for c in range(2, R_TILES)}


def interleave(nc, grouped, raw):
    nc.scalar.copy(
        out=grouped.rearrange("p (c j i) -> p c i j", j=4, i=PACK),
        in_=raw.rearrange("p i (c j) -> p c i j", j=4),
    )


def entries(offsets, lo, hi):
    return offsets[:, lo // LIST_ROWS : hi // LIST_ROWS]


def tile_list_session_slot_verdict_kernel(
    tc, tab_words, tab_scales, offs, w1, gain, wgs, offs2, offs3, sess, wa_words, wa_scales, wb, out
):
    nc = tc.nc
    with ExitStack() as ctx:
        lists = ctx.enter_context(tc.tile_pool(name="lists", bufs=1))
        placed = ctx.enter_context(tc.tile_pool(name="placed", bufs=1))
        psum = ctx.enter_context(tc.psum_pool(name="psum", bufs=1))

        def place(name, shape, dtype, offset):
            return placed.tile(shape, dtype, name=name, tag=name, align_bytes=ALIGN, offset=offset)

        def bank(b, width=BANK):
            return psum.tile([P, width], F32, name=f"bank{b}", tag=f"bank{b}")

        def quantize(name, grouped, codes_at, scales_at):
            width = grouped.shape[1] // PACK
            codes = place(f"{name}_codes", [P, width], U32, codes_at)
            scales = place(f"{name}_scales", [P, width], U8, scales_at)
            nc.vector.quantize_mx(out=codes[:].bitcast(FP8X4), scales=scales[:], in_=grouped)
            return codes, scales

        table_scales = place("table_scales", [P, T], U8, AT["table_scales"])
        nc.vector.memset(table_scales[:].bitcast(I32), 0)
        for q in range(P // QUADRANT):
            nc.gpsimd.dma_start(
                out=table_scales[QUADRANT * q : QUADRANT * q + SCALE_ROWS * K_PASSES, :].bitcast(I32),
                in_=tab_scales[:, SCALE_ROWS * q : SCALE_ROWS * (q + 1), :].bitcast(I32),
            )
        gain_rows = place("gain_rows", [P, P], F32, AT["gain_rows"])
        nc.vector.memset(gain_rows[:], 0.0)
        ident = place("ident", [P, P], F32, AT["ident"])
        make_identity(nc, ident[:])
        warm = place("warm", [P, 1], F32, AT["warm"])
        nc.scalar.activation(out=warm[:], in_=ident[:, 0:1], func=ACT.Gelu_apprx_tanh)
        wa_scale_tile = place("wa_scale_tile", [P, R_PASSES, N], U8, AT["wa_scales"])
        nc.vector.memset(wa_scale_tile[:].rearrange("p a n -> p (a n)").bitcast(I32), 0)

        def load_table(a):
            words = place(f"table_words{a}", [P, T], U32, AT[f"table{a}"])
            nc.sync.dma_start(out=words[:].bitcast(I32), in_=tab_words[a].rearrange("p t i -> p (t i)").bitcast(I32))
            return words

        def load_w1(c, offset, halved=0):
            tiles = []
            for a in range(K_PASSES):
                spare = ALIGN // 4 if c in (1, 2) and a == K_PASSES - 1 else 0
                raw = place(f"w1_raw{c}_{a}", [P, PASS + spare], F32, offset + a * 2 * KIB)[:, 0:PASS]
                raw = raw.rearrange("p (i c) -> p i c", i=PACK)
                rows = w1[a * PASS : (a + 1) * PASS, c * P : (c + 1) * P]
                rows = rows.rearrange("(p i) c -> p i c", i=PACK)
                planes = PACK // 2 if a < halved else PACK
                for lo in range(0, PACK, planes):
                    nc.sync.dma_start(out=raw[:, lo : lo + planes, :], in_=rows[:, lo : lo + planes, :])
                tiles.append(raw)
            return tiles

        def load_wide(a):
            wide = place(f"w1_wide{a}", [P, PACK, PASS], F32, AT["table0"] + a * 8 * KIB)
            rows = w1[a * PASS : (a + 1) * PASS, PASS:H]
            nc.sync.dma_start(out=wide[:], in_=rows.rearrange("(p i) c -> p i c", i=PACK))
            return wide

        sess_tiles = {}

        def load_sess(c0, c1):
            tiles = place(f"sess{c0}", [P, (c1 - c0) * M], F32, AT["sess"] + c0 * 2 * KIB)
            if c0 < NATURAL:
                rows = sess[c0 * P : c1 * P, :].rearrange("(c p) m -> p c m", p=P)
            else:
                rows = sess[PASS:H, :].rearrange("(p t) m -> p t m", t=PACK)
            nc.sync.dma_start(out=tiles[:].rearrange("p (c m) -> p c m", m=M), in_=rows)
            for c in range(c0, c1):
                sess_tiles[c] = tiles[:, (c - c0) * M : (c - c0 + 1) * M]

        gains, wgs_rows = {}, {}

        def load_gain(c):
            width = PAIR if c == LAST else ALIGN // 4
            gains[c] = place(f"gain{c}", [P, width], F32, GAIN_AT[c])[:, 0:1]
            if c < NATURAL:
                column = gain[c * P : (c + 1) * P].rearrange("(p o) -> p o", o=1)
            else:
                column = gain[PASS:H].rearrange("(p t) -> p t", t=PACK)[:, c - NATURAL : c - NATURAL + 1]
            with nc.allow_non_contiguous_dma(reason="one gain for each partition"):
                nc.sync.dma_start(out=gains[c], in_=column)

        def load_plane(c):
            wgs_rows[c] = place(f"wgs_dealt{c}", [P, S], F32, AT["planes"] + (c - NATURAL) * 4 * KIB if c < LAST else AT["back"])
            rows = wgs.rearrange("(p t) j -> p t j", t=PACK)[:, c - NATURAL, :]
            for q in (0, 2, 1, 3):
                nc.sync.dma_start(out=wgs_rows[c][QUADRANT * q : QUADRANT * (q + 1), :], in_=rows)
            load_gain(c)

        def load_wb(a, offset):
            raw = place(f"wb_raw{a}", [P, PACK, N], F32, offset)
            nc.sync.dma_start(out=raw[:], in_=wb[a * PASS : (a + 1) * PASS, :].rearrange("(p i) n -> p i n", i=PACK))
            return raw

        table_words = [load_table(0)]
        idx = lists.tile([P, S // LIST_ROWS], U16)
        nc.sync.dma_start(idx[:], offs)
        table_words.append(load_table(1))
        w1_raw = [load_w1(0, AT["z_natural"], 2)]
        nc.sync.dma_start(out=gain_rows[0:NATURAL, :], in_=gain[0:PASS].rearrange("(c p) -> c p", p=P))
        idx2 = lists.tile([P, S // LIST_ROWS], U16)
        nc.sync.dma_start(idx2[:], offs2)
        table_words.append(load_table(2))
        wgs_tile = place("wgs_tile", [P, S], F32, AT["wgs"])
        for lo in range(0, S, BANK):
            nc.sync.dma_start(out=wgs_tile[:, lo : lo + BANK], in_=wgs[:, lo : lo + BANK])
        for c in range(NATURAL):
            wgs_rows[c] = wgs_tile
        w1_raw.append(load_w1(1, AT["raw1"]))
        w1_raw.append(load_w1(2, AT["raw2"]))
        idx3 = lists.tile([P, M // LIST_ROWS], U16)
        nc.sync.dma_start(idx3[:], offs3)
        load_sess(0, 1)
        w1_raw.append(load_w1(3, AT["raw3"]))
        w1_wide = [load_wide(a) for a in range(K_PASSES)]
        load_gain(3)
        load_sess(1, 2)

        gain_turned = bank(2, P)
        nc.tensor.transpose(gain_turned[:], gain_rows[:], ident[:])
        gain_col = place("gain_col", [P, NATURAL], F32, AT["gain_col"])
        nc.scalar.copy(out=gain_col[:], in_=gain_turned[:, 0:NATURAL])

        v_words = [place(f"v_words{a}", [P, S], U32, AT["v01"] + a * 4 * KIB) for a in range(2)]
        nc.vector.tensor_copy(v_words[0][:], table_words[0][:].indirect(idx[:]))
        pages = [place(f"page{u}", [P, T2], F32, AT["pages"] + u * 8 * KIB) for u in range(PAGES)]
        for page in pages:
            nc.vector.memset(page[:].bitcast(I32), 0)
        nc.vector.tensor_copy(v_words[1][:], table_words[1][:].indirect(idx[:]))
        v_scales = place("v_scales", [P, S], U8, AT["table1"] + 12 * KIB)
        nc.vector.tensor_copy(v_scales[:], table_scales[:].indirect(idx[:]))

        w1_grouped, w1_mx = {}, {}

        def group_w1(c, offset):
            w1_grouped[c] = place(f"w1_grouped{c}", [P, K_PASSES * PASS], BF16, offset)[:]
            for a in range(K_PASSES):
                interleave(nc, w1_grouped[c][:, a * PASS : (a + 1) * PASS], w1_raw[c][a])

        def deal_w1(c, offset):
            dealt = place(f"w1_dealt{c}", [P, 2, K_PASSES * PASS], BF16, offset)
            t = c - NATURAL
            for a in range(K_PASSES):
                nc.scalar.copy(
                    out=dealt[:, :, a * PASS : (a + 1) * PASS].rearrange("p t (q e i) -> p q i e t", e=2, i=PACK),
                    in_=w1_wide[a][:].rearrange("p i (q e t) -> p q i e t", e=2, t=PACK)[:, :, :, :, t : t + 2],
                )
            for u in range(2):
                w1_grouped[c + u] = dealt[:, u, :]

        def quantize_w1(c, offset):
            w1_mx[c] = quantize(f"w1_{c}", w1_grouped[c], offset, offset + 4 * W1_CODES)

        def multiply_w1(c, b, lo, hi):
            codes, scales = w1_mx[c]
            acc = bank(b, hi - lo)
            for a in range(K_PASSES):
                nc.tensor.matmul_mx(
                    out=acc[:],
                    lhsT=codes[:, a * P : (a + 1) * P].bitcast(FP8X4),
                    lhsT_scale=scales[:, a * P : (a + 1) * P],
                    rhs=v_words[a][:, lo:hi].bitcast(FP8X4),
                    rhs_scale=v_scales[SCALE_ROWS * a : P, lo:hi],
                    start=(a == 0),
                    stop=(a == K_PASSES - 1),
                )
            return acc

        def gelu(dst, acc):
            nc.scalar.activation(out=dst, in_=acc[:], func=ACT.Gelu_apprx_tanh)

        def scale(dst, src, column):
            nc.scalar.activation(out=dst, in_=src, func=ACT.Copy, scale=column)

        def scatter(c, h, weights, lo, hi):
            nc.vector.tensor_tensor(pages[c % PAGES][:].indirect(entries(idx2, lo, hi)), h, weights[:, lo:hi], ALU.mult)

        def gather(x, c, lo, hi):
            nc.vector.tensor_tensor(x[:, lo:hi], pages[c % PAGES][:].indirect(entries(idx3, lo, hi)), sess_tiles[c][:, lo:hi], ALU.add)

        group_w1(0, AT["grouped0"])
        quantize_w1(0, AT["codes0"])
        v_words.append(place("v_words2", [P, S], U32, AT["table_scales"]))
        for lo, hi in ((0, FIRST_CUT), (FIRST_CUT, S)):
            nc.vector.tensor_copy(v_words[2][:, lo:hi], table_words[2][:].indirect(entries(idx, lo, hi)))

        wb_raw = [load_wb(0, AT["wb_raw0"])]
        load_plane(4)
        load_sess(2, NATURAL)
        wb_raw.append(load_wb(1, AT["table2"] + 4 * KIB))
        load_plane(5)
        load_plane(6)
        load_sess(NATURAL, R_TILES)
        for q in range(P // QUADRANT):
            nc.sync.dma_start(
                out=wa_scale_tile[QUADRANT * q : QUADRANT * q + SCALE_ROWS, :, :].bitcast(I32),
                in_=wa_scales[:, SCALE_ROWS * q : SCALE_ROWS * (q + 1), :].rearrange("a r n -> r a n").bitcast(I32),
            )

        cuts = (0, FIRST_CUT, BANK, S)
        first_sums = [multiply_w1(0, b, lo, hi) for b, lo, hi in zip((0, 1, 6), cuts, cuts[1:])]
        weights = place("weights0", [P, S], F32, AT["weights0"])
        for lo in range(0, S, BANK):
            scale(weights[:, lo : lo + BANK], wgs_tile[:, lo : lo + BANK], gain_col[:, 0:1])
        h_front = place("h0_front", [P, BANK], F32, AT["h0"])
        for u in range(2):
            lo, hi = cuts[u], cuts[u + 1]
            gelu(h_front[:, lo:hi], first_sums[u])
            scatter(0, h_front[:, lo:hi], weights, lo, hi)
        group_w1(1, AT["codes0"])
        quantize_w1(1, AT["codes1"])
        h_back = place("h0_back", [P, BANK], F32, AT["raw1"] + 4 * KIB)
        gelu(h_back[:], first_sums[2])
        scatter(0, h_back[:], weights, BANK, S)
        group_w1(2, AT["grouped2"])
        quantize_w1(2, AT["codes2"])

        z_natural = place("z_natural", [P, PACK * M], F32, AT["z_natural"])

        def pick_natural(c, x):
            gather(x, c, 0, M)
            for t in range(PACK):
                nc.sync.dma_start(
                    out=z_natural[QUADRANT * c : QUADRANT * (c + 1), t * M : (t + 1) * M], in_=x[t:P:PACK, :]
                )

        x0 = place("x0", [P, M], F32, AT["raw2"] + 4 * KIB)
        pick_natural(0, x0)
        weights = place("weights1", [P, S], F32, AT["raw2"])
        scale(weights[:], wgs_tile[:], gain_col[:, 1:2])
        h = place("h1", [P, S], F32, AT["h_odd"])
        for half in range(2):
            gelu(h[:, half * BANK : (half + 1) * BANK], multiply_w1(1, 6 + half, half * BANK, (half + 1) * BANK))
        scatter(1, h[:], weights, 0, S)
        group_w1(3, AT["codes1"])

        z_dealt = place("z_dealt", [P, (PACK - 1) * M], F32, AT["z_dealt"])
        H_AT = {2: AT["raw3"] + 2 * KIB, 3: AT["h_odd"], 4: AT["raw3"] + 2 * KIB, 5: AT["table0"],
                6: AT["wb_raw0"], 7: AT["z_natural"] - 2 * KIB}
        wb_grouped, wb_mx = {}, {}

        def group_wb(a, offset):
            wb_grouped[a] = place(f"wb_grouped{a}", [P, PACK * N], BF16, offset)
            for lo in range(0, N, PAIR):
                interleave(nc, wb_grouped[a][:, PACK * lo : PACK * (lo + PAIR)], wb_raw[a][:, :, lo : lo + PAIR])

        def quantize_wb(a, lo, hi, codes_at, scales_at):
            codes, scales = quantize(f"wb{a}_{lo}", wb_grouped[a][:, PACK * lo : PACK * hi], codes_at, scales_at)
            for n in range(lo // P, hi // P):
                first = n * P - lo
                wb_mx[a, n] = (codes[:, first : first + P], scales[:, first : first + P])

        def z_plane(c):
            return z_dealt[:, (c - NATURAL) * M : (c - NATURAL + 1) * M]

        for c in range(2, R_TILES):
            front_at = AT["front"] + c % 2 * 2 * KIB
            front = place(f"front{c}", [P, BANK], F32, front_at)
            if c <= NATURAL:
                back = place(f"back{c}", [P, BANK], F32, AT["back"] + (c - 2) * 2 * KIB)[:]
            else:
                back = z_plane(c - 1)
            gelu(front[:], multiply_w1(c, 6, 0, BANK))
            gelu(back, multiply_w1(c, 7, BANK, S))
            h = place(f"h{c}", [P, S], F32, H_AT[c])
            if c == 2:
                scale(h[:, 0:BANK], front[:], gain_col[:, c : c + 1])
                scale(h[:, BANK:S], back, gain_col[:, c : c + 1])
            elif c == 3:
                scale(h[:, 0:BANK], front[:], gain_col[:, c : c + 1])
                scale(h[:, BANK : S - P], back[:, 0 : BANK - P], gain_col[:, c : c + 1])
                scale(h[:, S - P : S], back[:, BANK - P : BANK], gains[c])
            else:
                scale(h[:, 0:BANK], front[:], gains[c])
                scale(h[:, BANK:S], back, gains[c])
            if c < LAST:
                quantize_w1(c + 1, front_at)
                scatter(c, h[:], wgs_rows[c], 0, S)
            else:
                quantize_wb(0, 0, PAIR, front_at, front_at + 4 * PAIR)
                scatter(c, h[:, 0:LAST_CUT], wgs_rows[c], 0, LAST_CUT)
            if c <= NATURAL:
                pick_natural(c - 1, back)
            else:
                gather(back, c - 1, 0, M)
            if c == NATURAL:
                load_plane(LAST)
            elif c == 5:
                wa_codes = place("wa_codes", [P, R_PASSES, 2 * N], U8, AT["planes"] + 5 * KIB)
                nc.sync.dma_start(out=wa_codes[:].bitcast(I32), in_=wa_words.rearrange("a p n -> p a n").bitcast(I32))
            if c in (2, 3):
                deal_w1(2 * c, AT[f"gain{c}"])
            elif c in (4, 5):
                group_wb(c - 4, AT[f"gain{c}"])
            elif c == 6:
                z_first = place("z_first", [P, PACK * M], BF16, AT["gain6"])
                interleave(nc, z_first[:], z_natural[:].rearrange("p (t m) -> p t m", t=PACK))

        first_mx = quantize("z_first", z_first[:], AT["z_codes"], GAIN_AT[LAST])
        spans = ((0, QUARTER), (QUARTER, HALF), (HALF, M))
        z_last = [place(f"z_last{u}", [P, PACK * (hi - lo)], BF16, AT["planes"] + 8 * KIB + 2 * PACK * lo)
                  for u, (lo, hi) in enumerate(spans)]

        def z_columns(lo, hi):
            u = min(lo // QUARTER, 2)
            first = lo - spans[u][0]
            return z_last[u][:].rearrange("p (m t) -> p m t", t=PACK)[:, first : first + hi - lo, :]

        for lo, hi in spans:
            nc.scalar.copy(
                out=z_columns(lo, hi)[:, :, 0 : PACK - 1],
                in_=z_dealt[:].rearrange("p (t m) -> p m t", t=PACK - 1)[:, lo:hi, :],
            )
        scatter(LAST, h[:, LAST_CUT:S], wgs_rows[LAST], LAST_CUT, S)

        z_half = [(place(f"z_codes{half}", [P, HALF], U32, AT["gain2"] + half * 2 * KIB),
                   place(f"z_scales{half}", [P, HALF], U8, AT["gain2"] + half * 2 * KIB + KIB)) for half in range(2)]

        def multiply(acc, which, n, a, lo, hi, start, stop):
            if which == 0:
                codes = wa_codes[:, a, 2 * n * P : 2 * (n + 1) * P].bitcast(FP4X4)
                scales = wa_scale_tile[:, a, n * P : (n + 1) * P]
            else:
                codes, scales = wb_mx[a, n]
                codes = codes.bitcast(FP8X4)
            if a == 0:
                moving, moving_scales = first_mx[0][:, lo:hi], first_mx[1][:, lo:hi]
            else:
                half, first = divmod(lo, HALF)
                moving = z_half[half][0][:, first : first + hi - lo]
                moving_scales = z_half[half][1][:, first : first + hi - lo]
            nc.tensor.matmul_mx(
                out=acc, lhsT=codes, lhsT_scale=scales, rhs=moving.bitcast(FP8X4), rhs_scale=moving_scales,
                start=start, stop=stop,
            )

        def pair_pass(acc, which, pair, a, lo, hi, start, stop):
            first = lo % HALF
            for u in range(2):
                multiply(acc[:, u * HALF + first : u * HALF + first + hi - lo], which, 2 * pair + u, a, lo, hi,
                         start and u == 0, stop and u == 1)

        pair_sums, row_sums = {}, {}
        for half in range(2):
            for which in range(2):
                acc = bank(6 * half + which)
                pair_sums[which, half] = acc
                pair_pass(acc, which, 0, 0, half * HALF, (half + 1) * HALF, True, False)
            if half == 0:
                for n in range(2, N // P):
                    row_sums[n] = bank(n)
                    multiply(row_sums[n][:], 0, n, 0, 0, M, True, False)

        def quantize_z(u):
            lo, hi = spans[u]
            half, first = divmod(lo, HALF)
            codes, scales = z_half[half]
            nc.vector.quantize_mx(out=codes[:, first : first + hi - lo].bitcast(FP8X4),
                                  scales=scales[:, first : first + hi - lo], in_=z_last[u][:])

        x_last_at = AT["z_dealt"] + 6 * KIB
        x_last = {}

        def last_quarter(u):
            lo, hi = u * QUARTER, (u + 1) * QUARTER
            x = place(f"x_last{u}", [P, QUARTER], F32, x_last_at + 4 * lo)
            x_last[u] = x
            nc.vector.tensor_tensor(x[:], pages[LAST % PAGES][:].indirect(entries(idx3, lo, hi)), sess_tiles[LAST][:, lo:hi], ALU.add)
            nc.scalar.copy(out=z_columns(lo, hi)[:, :, PACK - 1], in_=x[:])

        copied = []

        def finish(sum_a, sum_b, rows):
            ya = place(f"ya{len(copied)}", [P, BANK], F32, AT["v01"] + len(copied) * 2 * KIB)
            best = place(f"best{len(copied)}", [P, BANK], F32, AT["table0"] + len(copied) * 2 * KIB)
            copied.append(ya)
            nc.scalar.copy(out=ya[:], in_=sum_a[:])
            nc.vector.tensor_tensor(best[:], sum_b[:], ya[:], ALU.max)
            nc.sync.dma_start(out=rows, in_=best[:].rearrange("p (n m) -> p n m", m=rows.shape[2]))

        def finish_pair(half):
            rows = out[0:PAIR, half * HALF : (half + 1) * HALF].rearrange("(n p) m -> p n m", p=P)
            finish(pair_sums[0, half], pair_sums[1, half], rows)

        wb_codes_at = AT["planes"]
        quantize_wb(1, 0, PAIR, wb_codes_at, GAIN_AT[LAST] + 512)
        for u in range(3):
            last_quarter(u)
        quantize_z(0)
        for which in range(2):
            pair_pass(pair_sums[which, 0], which, 0, 1, 0, QUARTER, False, False)
        last_quarter(3)
        quantize_z(1)
        for which in range(2):
            pair_pass(pair_sums[which, 0], which, 0, 1, QUARTER, HALF, False, True)
        for n in row_sums:
            multiply(row_sums[n][:, 0:HALF], 0, n, 1, 0, HALF, False, False)
        quantize_wb(0, PAIR, N, wb_codes_at + KIB, x_last_at + 4 * QUARTER)
        quantize_z(2)
        for which in range(2):
            pair_pass(pair_sums[which, 1], which, 0, 1, HALF, M, False, True)
        for n in row_sums:
            multiply(row_sums[n][:, HALF:M], 0, n, 1, HALF, M, False, True)
        quantize_wb(1, PAIR, 2 * PAIR, wb_codes_at + 3 * KIB, x_last_at + 12 * QUARTER)
        finish_pair(0)
        quantize_wb(1, 2 * PAIR, N, wb_codes_at + 4 * KIB, x_last_at + 12 * QUARTER + PAIR)
        finish_pair(1)
        for b, n in zip((0, 1, 6, 2), row_sums):
            late = bank(b)
            multiply(late[:], 1, n, 0, 0, M, True, False)
            for half in range(2):
                lo, hi = half * HALF, (half + 1) * HALF
                multiply(late[:, lo:hi], 1, n, 1, lo, hi, False, half == 1)
            finish(row_sums[n], late, out[n * P : (n + 1) * P, :].rearrange("(o p) m -> p o m", o=1))
